import numpy as np, ml_dtypes
CORES = [23,119,17,113]
N = 4
import mx_ref
BF = ml_dtypes.bfloat16
def tile(rs):
    return np.stack(rs, axis=2).reshape(128, -1).astype(BF)
def pick(q, e):
    c = np.concatenate([q[0].reshape(128, -1, 4), np.zeros((128, 1, 4), np.uint8)], axis=1); s = np.concatenate([q[1], np.ones((16, 1), np.uint8)], axis=1)
    return (np.ascontiguousarray(c[:, e].reshape(128, -1)), np.ascontiguousarray(s[:, e]))
def join(*qs):
    return (np.concatenate([q[0] for q in qs], axis=1), np.concatenate([q[1] for q in qs], axis=1))
def put(q, e, v):
    c, s = q[0].reshape(128, -1, 4).copy(), q[1].copy(); c[:, e] = v[0].reshape(128, -1, 4); s[:, e] = v[1]
    return (c.reshape(128, -1), s)
def pk(c, s):
    return (np.ascontiguousarray(c), mx_ref.live(s))
def emit(q):
    return q[0], q[1]
def packed(v, rng):
    q = [mx_ref.quantize(np.ascontiguousarray(v[r])) for r in range(N)]
    return np.stack([a for a, b in q]), np.stack([mx_ref.plane(b, rng) for a, b in q])
def values_of_codes():
    e, c = np.zeros((128, 128, 4), np.float32), np.zeros((128, 2, 4), np.uint8)
    e[np.arange(128), np.arange(128), 0] = 1
    c[:127, :, 0] = np.arange(256).reshape(2, 128).T[:127]
    return mx_ref.matmul(mx_ref.quantize(e.reshape(128, 512).astype(BF)), (c.reshape(128, 8), np.full((16, 2), 127, np.uint8))).T.reshape(-1).astype(np.float64)
CODE_VALUE, SCALE_VALUE = values_of_codes(), 2.0 ** (np.arange(256) - 127.0)
def decode(q):
    return (CODE_VALUE[q[0]].reshape(16, 8, -1, 4) * SCALE_VALUE[q[1]][:, None, :, None] + 0.0).reshape(128, -1).astype(np.float32)
def f(rng, *shape):
    return mx_ref.flush((rng.standard_normal(shape, dtype=np.float32) * np.exp2(rng.integers(-2, 3, shape[:-1] + (1,)))).astype(BF))
def wide(rng, *shape, cols=0):
    v = rng.standard_normal(shape, dtype=np.float32) * np.exp2(rng.integers(-12, 13, shape)).astype(np.float32)
    if cols: v *= np.repeat(np.exp2(rng.integers(-cols, cols + 1, shape[:-2] + (1, shape[-1] // 4))) * (rng.random(shape[:-2] + (1, shape[-1] // 4)) > 0.0625), 4, axis=-1).astype(np.float32)
    return mx_ref.flush(v.astype(BF))
C, H, E = 320, 96, 416
STEP = [1, 2, 3]
def parts(t, h, n):
    return np.ascontiguousarray(t.reshape(8, 16, -1, 4)[h, :, n].transpose(0, 2, 1, 3)).reshape(128, -1)
def big(v):
    v = v.astype(np.float32)
    v[np.abs(v) < np.float32(2.0 ** -16)] = 0
    return v.astype(BF)
def numbers_of(rng):
    return {"x": big(f(rng, N, 128, 4 * C)), "u": np.array(f(rng, N, 128, 512)), "v": np.array(f(rng, N, 128, 512))}
def edges(rng):
    return {"nb": rng.integers(0, E, (N, 4, C)).astype(np.int32), "e": rng.integers(0, 8, (N, 4, C)).astype(np.int32)}
def layers(rng):
    return big(f(rng, N, 128, 2048)).reshape(N, 8, 16, 4, 8, 16, 4)
def weights(rng, w):
    c, p = packed(np.ascontiguousarray(w).reshape(N, 128, 2048), rng)
    return {"wc": c, "ws": p}
def bare(u):
    u = u.reshape(N, 128, 128, 4)
    u[:, :, ::16] = 0
    u[:, :, 1::16] = 0
    u[:, :, 2] = 0
    return u
def setup_inputs(rng):
    return {**numbers_of(rng), **edges(rng), **weights(rng, layers(rng))}
def setup_inputs_ties(rng):
    d = numbers_of(rng)
    x = d["x"].reshape(N, 8, 16, C, 4)
    x[:, :, :3] = 0
    x[:, :, :3, :, 0] = rng.integers(1, 4, (N, 8, 3, C)).astype(np.float32).astype(BF)
    u = bare(d["u"])
    o = rng.permutation(N)
    for r in range(N):
        k = 0.0 if r == o[0] else -1.0 if r == o[1] else 1.0
        u[r, 2, 2, 0] = k
        for h in range(0, 128, 16):
            u[r, h, h, 0] = k
            u[r, h + 1, h + 1, 0] = k
    w = layers(rng)
    w[:, :, :, :, :, :3] = 0
    return {"x": x.reshape(N, 128, 4 * C), "u": u.reshape(N, 128, 512), "v": d["v"], **edges(rng), **weights(rng, w)}
def setup_inputs_near(rng):
    d = numbers_of(rng)
    x = d["x"].astype(np.float32).reshape(N, 8, 16, C, 4)
    u = bare(d["u"])
    o = rng.permutation(N) % 4
    x[:, :, 0] = 0
    x[:, :, 8:] = 0
    s = rng.integers(0, 16, (N, 8, 3, C))
    x[:, :, 8:11] = ((s[..., None] >> np.arange(4)) & 1) * np.exp2(np.arange(4) - 23.0)
    x[:, :, 11, :, 0] = 2.0 ** -10
    for r in range(N):
        x[r, :, 0, :, 0] = -1.0 if o[r] == 1 else 1.0
        if o[r] == 3:
            x[r, :, 8:] = 0
            x[r, :, 8:11, :, 0] = rng.choice([0.0, 1.0, 1.125], (8, 3, C)) * 2.0 ** -29
            x[r, :, 12, :, 0] = 2.0 ** -29
            for g in np.append(0, 1 + rng.permutation(7)[:3]): x[r, int(g), 8:11, int(rng.integers(C)), 0] = 2.0 ** 29
        k = 1.0 if o[r] == 0 else 2.0 ** -30
        for h, i, j in [(h, 8 + i, h + i) for h in range(0, 128, 16) for i in (0, 1)] + [(0, 10, 2)]:
            u[r, h + i, j] = k if o[r] < 3 or j == 2 else k * 1.25 if h < 64 else k * 1.125
            if o[r] < 2:
                u[r, h, j, 0] = k
                u[r, h + 11, j, 0] = k
        if o[r] == 2:
            a, b = [16 * int(h) for h in rng.permutation(8)[:2]]
            u[r, a, a, 0] = 1.0
            u[r, b, b, 0] = -1.0
            u[r, b, b + 1, 0] = -1.0
            m, n = [int(h) for h in rng.permutation(C)[:2]]
            x[r, :, 0, m, 1] = 1.0
            x[r, :, 0, n, 1] = -1.0
            u[r, 0, 2, 1] = 1.0
        if o[r] == 3: u[r, 12, 2, 0] = -k
    w = layers(rng)
    for i in [0] + [8 + k for k in range(8)]:
        w[:, :, i] = 0
        w[:, :, :, :, :, i] = 0
    return {"x": x.reshape(N, 128, 4 * C).astype(BF), "u": u.reshape(N, 128, 512), "v": d["v"], **edges(rng), **weights(rng, w)}
def setup_inputs_huge(rng):
    d = numbers_of(rng)
    o = rng.permutation(N)
    c = rng.integers(0, 2, (N, C)) * 2.0 - 1.0
    a = 2.0 ** 29 * (1.0 - 0.1 * rng.random((N, 8, 16, 17, 4)))
    for g in range(8):
        a[:, g, :, g] *= 2.0
        a[:, g, :, 8 + g] *= 2.0
    for r in range(N):
        if o[r] < 2: c[r] = -1.0
        if o[r] == 0:
            c[r, rng.permutation(C)[:H // 2]] = 1.0
            a[r] = 2.0 ** 30
            for g in range(8):
                a[r, 0, :7 - g, g] *= 0.5
                a[r, 0, :7 - g, 8 + g] *= 0.5
        if o[r] >= N // 2: a[r, :, :, 8:16] *= (rng.permutation(8) % 2 * 2.0 - 1.0)[:, None]
    x = (0.6 + 0.09 * rng.random((N, 8, 16, C, 4))) * c[:, None, None, :, None]
    x[o == 0] = 0.875 * np.sign(x[o == 0])
    u = bare(d["u"])
    u[:, :, [16 * h for h in range(8)] + [16 * h + 1 for h in range(8)] + [2]] = a.reshape(N, 128, 17, 4).astype(np.float32).astype(BF)
    w = np.zeros((N, 128, 4, 128, 4), np.float32)
    i = np.arange(128)
    for b in range(4): w[:, i, b, i, b] = 1
    return {"x": (2.0 ** 30 * x).astype(np.float32).reshape(N, 128, 4 * C).astype(BF), "u": u.reshape(N, 128, 512), "v": d["v"], **edges(rng), **weights(rng, w.astype(BF))}
def setup_inputs_few(rng):
    d = numbers_of(rng)
    x = (129 + 2 * rng.integers(0, 64, (N, 8, 16, C, 4))) * np.exp2(rng.integers(-14, -7, (N, 8, 16, C, 4)) - 7.0) * (rng.integers(0, 2, (N, 8, 16, C, 4)) * 2.0 - 1.0)
    x[:, :, ::8, :, 0] = 1.96875
    u = d["u"].reshape(N, 8, 16, 128, 4)
    u[:, :, ::8] = 0
    t = edges(rng)
    o = rng.permutation(N)
    t["nb"][o[0]] = E - 1
    t["nb"][o[1]] = np.arange(C)
    t["e"][o[1]] = 7
    t["nb"][o[2]] = C + rng.integers(0, H, (4, C))
    t["nb"][o[3]] = 0
    t["e"][o[3]] = 0
    w = layers(rng)
    w[:, :, :, :, :, 8:] = 0
    return {"x": (16.0 * x).astype(np.float32).reshape(N, 128, 4 * C).astype(BF), "u": u.reshape(N, 128, 512), "v": d["v"], **t, **weights(rng, w)}
def setup_inputs_spread(rng):
    d = setup_inputs(rng)
    d["x"] = big(wide(rng, N, 128, 4 * C, cols=6))
    return d
def check_inputs(d):
    b = []
    for k in ("x", "u", "v"):
        a = np.abs(d[k].astype(np.float32))
        if not (np.isfinite(a).all() and ((a == 0) | (a >= 2.0 ** -30) & (a <= 2.0 ** 30)).all()): b.append("a value of " + k)
    if not ((d["nb"] >= 0) & (d["nb"] < E)).all(): b.append("an entry of nb")
    if not ((d["e"] >= 0) & (d["e"] < 8)).all(): b.append("an entry of e")
    none, least, most = [emit(mx_ref.quantize(np.full((128, 16), k, np.float32).astype(BF)))[1][0, 0] for k in (0.0, 2.0 ** -30, 2.0 ** 30)]
    for r in range(N):
        if ((d["wc"][r] == 0x7F) | (d["wc"][r] == 0xFF)).any(): b.append("wc: a code that is no number")
        s = mx_ref.live(d["ws"][r])
        if ((s != none) & ((s < least) | (s > most))).any(): b.append("ws: a scale out of range")
    return b
def reference(x, u, v, nb, e, wc, ws):
    qu = [mx_ref.quantize(u[r]) for r in range(N)]
    lay = [pk(wc[r], ws[r]) for r in range(N)]
    now = [x[r] for r in range(N)]
    shift = e.astype(np.int64)
    g, i = np.arange(8), np.arange(C)
    for d in STEP:
        q = [mx_ref.quantize(now[r]) for r in range(N)]
        own = [mx_ref.matmul(qu[r], q[r]) + np.float32(0.0) for r in range(N)]
        border = [pick(q[r], np.argsort(-own[r][2], kind="stable")[:H]) for r in range(N)]
        made = []
        for r in range(N):
            came = border[(r + d) % N]
            p = np.concatenate([own[r], mx_ref.matmul(qu[r], came) + np.float32(0.0)], axis=1)
            val = decode(join(q[r], came))
            k = np.argmax(p[1::16], axis=0)
            shift[r] = (shift[r] + k[nb[r]] - k[:C]) % 8
            src = (g[:, None, None] + shift[r]) % 8
            c = np.argmax(p[::16][src, nb[r]], axis=1)
            a = parts(val, (g[:, None] + k[:C]) % 8, i)
            b = parts(val, np.take_along_axis(src, c[:, None], axis=1)[:, 0], nb[r][c, i])
            z = mx_ref.quantize(((a + b) * np.float32(0.5)).astype(BF))
            made.append(tile([np.maximum(mx_ref.matmul(pick(lay[r], np.arange(128 * t, 128 * t + 128)), z), np.float32(0.0)) * np.float32(0.03125) + a[:, t::4] for t in range(4)]))
        now = made
    y, oe = np.zeros((N, 128, C), np.float32), np.zeros((N, 4, C), np.float32)
    oc, osc = np.zeros((N, 128, 4 * C), np.uint8), np.zeros((N, 16, C), np.uint8)
    for r in range(N):
        q = mx_ref.quantize(now[r])
        y[r] = mx_ref.matmul(mx_ref.quantize(v[r]), q)
        oe[r] = shift[r]
        oc[r], osc[r] = emit(q)
    return {"y": y, "oe": oe, "oc": oc, "osc": osc}

@@ -1,0 +1,590 @@
+from concourse.mybir import dt, AluOpType, ActivationFunctionType
+
+C, H, E = 320, 96, 416
+STEP = [1, 2, 3]
+BF, F32, I32, U16, CD, PL = "bfloat16", "float32", "int32", "uint16", "float8_e4m3fn_x4", "uint8"
+SB = {
+    "X0": (1280, BF), "X1": (1280, BF), "U": (512, BF), "VV": (512, BF),
+    "QU": (128, CD), "SU": (128, PL), "QV": (128, CD), "SV": (128, PL),
+    "QU2": (128, CD), "SU2": (128, PL), "QUP": (416, CD), "SUP": (416, PL),
+    "WC": (512, CD), "WS": (512, PL),
+    "EB": (512, BF), "ET": (4096, BF), "QE": (1024, CD), "SE": (1024, PL),
+    "CT": (1536, BF), "QC": (384, CD), "SC": (384, PL), "ZT": (512, BF),
+    "F1": (1280, BF), "QF1": (320, CD), "SF1": (320, PL), "F2": (768, BF), "QF2": (192, CD), "SF2": (192, PL),
+    "MK0": (256, BF), "MK": (320, BF), "DD": (320, BF), "SC3": (4, F32), "INN": (192, BF), "OT": (192, F32),
+    "FT": (160, F32), "PM": (160, F32), "FL": (160, BF), "KS": (160, BF), "RS": (160, F32), "KP": (160, BF),
+    "KT": (416, BF), "KG": (384, BF), "KX": (736, BF), "KO": (480, BF), "KOT": (480, BF), "KF": (48, F32),
+    "KA": (80, F32), "KR": (40, F32),
+    "NI": (64, I32), "NE": (32, F32), "NF": (32, F32), "ND": (64, F32), "NT": (64, F32), "NY": (80, F32),
+    "YF": (40, F32), "PF": (64, F32), "PH": (64, F32), "T2": (40, I32), "T3": (40, I32),
+    "T4": (80, I32), "T5": (80, I32), "T6": (40, I32), "T7": (40, I32),
+    "CB": (160, F32), "CD0": (20, F32), "CF": (160, F32), "CM": (80, F32), "CTP": (80, F32), "C1": (160, F32),
+    "C2": (80, F32), "C5": (80, I32), "C6": (80, I32),
+    "MT": (4096, F32), "MG": (640, F32), "MX": (640, F32),
+    "VW": (4096, BF), "AP": (1280, BF), "AS": (1280, BF), "ZP": (1280, BF), "Z": (1280, BF),
+    "QZ": (320, CD), "SZ": (320, PL), "RL": (1280, F32), "YO": (320, F32),
+    "IT": (288, F32), "PT": (288, F32), "CI": (64, F32), "PC": (1, F32), "GI": (8, I32), "GJ": (8, I32), "GF": (8, F32),
+    "HB": (4, F32), "AB": (80, F32), "PD": (6, F32),
+    "L2": (8, U16), "LU": (26, U16), "LA": (4, U16), "LB": (6, U16), "LD": (30, U16), "LE": (4, U16), "LF": (2, U16),
+    "OK": (20, U16), "OM": (40, U16), "OA": (80, U16), "OB": (80, U16),
+    "SF": (64, F32), "SH": (32, F32), "ST": (32, F32),
+}
+for _r in range(4):
+    SB["QX%d" % _r] = (320, CD)
+    SB["SX%d" % _r] = (320, PL)
+for _r in range(3):
+    SB["QB%d" % _r] = (96, CD)
+    SB["SB%d" % _r] = (96, PL)
+    SB["QL%d" % _r] = (224, CD)
+    SB["SL%d" % _r] = (224, PL)
+    SB["OL%d" % _r] = (6, U16)
+PART = {}
+for _pool, _names in (("TI", "T2 T3 T4 T5 T6 T7 C5 C6"), ("TF", "CF CM CTP C1 C2 CD0 CB KA KR")):
+    _at = 0
+    for _k in _names.split():
+        PART[_k] = (_pool, _at, SB[_k][0])
+        _at += SB[_k][0]
+        SB[_pool] = (_at, SB.pop(_k)[1])
+SCRATCH = {k: ("sbuf", [128, n], d) for k, (n, d) in SB.items()}
+SCRATCH["PL"] = ("psum", [128, 512 * 5], F32)
+SCRATCH["PV"] = ("psum", [128, 512 * 3], F32)
+SEMAPHORES = ["eV", "eS", "eP", "eG", "dx0", "dx1", "du", "dv", "dw", "dn", "da", "do0", "do2", "dc0", "dc1", "dy0", "dy1",
+              "arr0", "arr1", "arr2", "loc"]
+WIDE = {BF: 2, F32: 4, I32: 4, U16: 2, CD: 4, PL: 1}
+SYNC, OVER, GATHER, PE = 90.0, 55.0, 1.55, 0.75
+TRIES, EARLY = 2000, 7000.0
+CUT = ((0, 192), (192, 320))
+Op, Fn = AluOpType, ActivationFunctionType
+
+
+def rank_program(g, core, T, topo):
+    rank = T.rank_of(core)
+    if rank is None:
+        return
+    N = len(T.cores)
+    ops = []
+    boost = [0.0]
+    Q = {"V": g.vector, "S": g.scalar, "P": g.tensor, "G": g, "Y": g.sync}
+
+    def A(name, c0=0, c1=None, step=1, p0=0, p1=128):
+        if name in PART:
+            pool, at, width = PART[name]
+            return A(pool, at + c0, at + (width if c1 is None else c1), step, p0, p1)
+        if name in ("PL", "PV"):
+            cm = 0
+            for b in range(c0 // 512, (c1 - 1) // 512 + 1):
+                cm |= 1 << b
+            reg = (name, (1 << 128) - 1, cm)
+            kind = F32
+        else:
+            if c1 is None:
+                c1 = SB[name][0]
+            if step == 1:
+                cm = ((1 << (c1 - c0)) - 1) << c0
+            else:
+                cm = 0
+                for c in range(c0, c1, step):
+                    cm |= 1 << c
+            reg = (name, ((1 << (p1 - p0)) - 1) << p0, cm)
+            kind = SB[name][1]
+        view = T[name][p0:p1, c0:c1] if step == 1 else T[name][p0:p1, c0:c1:step]
+        return {"ap": view, "regs": [reg], "n": len(range(c0, c1, step)), "w": WIDE[kind], "kind": kind, "ind": False,
+                "ps": name in ("PL", "PV")}
+
+    def bank(name, b, c0, c1, step=1):
+        return A(name, 512 * b + c0, 512 * b + c1, step)
+
+    def by(win, off):
+        return {"ap": win["ap"].indirect(off["ap"]), "regs": win["regs"] + off["regs"], "n": 16 * off["n"], "w": 4, "ind": True, "ps": False}
+
+    def ap(v):
+        return v["ap"] if isinstance(v, dict) else v
+
+    def add(alts, reads, writes, **kw):
+        o = {"alts": alts, "r": [x for v in reads if isinstance(v, dict) for x in v["regs"]],
+             "w": [x for v in writes for x in v["regs"]], "lat": 0.0, "sem": None, "inc": 1, "after": [], "boost": boost[0]}
+        o.update(kw)
+        ops.append(o)
+        return len(ops) - 1
+
+    def cv(out, *ins):
+        vs = [v for v in (out,) + ins if isinstance(v, dict) and (v["n"] > 1 or v is out)]
+        n = out["n"]
+        if any(v["ind"] for v in vs):
+            return 60 + GATHER * n
+        return max(64.0, OVER + n * (0.5 if all(v["w"] == 2 for v in vs) else 1.0))
+
+    def cs(out, in_):
+        return (80 + GATHER * out["n"]) if in_["ind"] else OVER + 20 + out["n"]
+
+    def ts(out, in0, s1, op0, s2=None, op1=None):
+        if op1 is None:
+            f = lambda: g.vector.tensor_scalar(ap(out), ap(in0), ap(s1), None, op0)
+        else:
+            f = lambda: g.vector.tensor_scalar(ap(out), ap(in0), ap(s1), ap(s2), op0, op1)
+        return add([("V", cv(out, in0), f)], [in0, s1, s2], [out])
+
+    def tt(out, in0, in1, op):
+        c = cv(out, in0) if in0["ind"] else OVER + out["n"] * (1 if in0["ps"] or in1["ps"] else 2)
+        return add([("V", c, lambda: g.vector.tensor_tensor(ap(out), ap(in0), ap(in1), op))], [in0, in1], [out])
+
+    def cp(out, in_, on="V", scale=None):
+        alts = []
+        if "S" in on:
+            if scale is None:
+                alts.append(("S", cs(out, in_), lambda: g.scalar.activation(ap(out), ap(in_), Fn.Copy)))
+            else:
+                alts.append(("S", cs(out, in_), lambda: g.scalar.activation(ap(out), ap(in_), Fn.Copy, scale=ap(scale))))
+        if "V" in on:
+            if scale is None:
+                alts.append(("V", cv(out, in_), lambda: g.vector.tensor_copy(ap(out), ap(in_))))
+            else:
+                alts.append(("V", cv(out, in_), lambda: g.vector.tensor_scalar(ap(out), ap(in_), ap(scale), None, Op.mult)))
+        return add(alts, [in_, scale], [out])
+
+    def act(out, in_, fn, bias=0.0, scale=1.0):
+        return add([("S", cs(out, in_), lambda: g.scalar.activation(ap(out), ap(in_), fn, bias=ap(bias), scale=ap(scale)))],
+                   [in_, bias, scale], [out])
+
+    def plus(out, in_, k):
+        return add([("S", cs(out, in_), lambda: g.scalar.activation(ap(out), ap(in_), Fn.Identity, bias=ap(k))),
+                    ("V", cv(out, in_), lambda: g.vector.tensor_scalar(ap(out), ap(in_), ap(k), None, Op.add))], [in_, k], [out])
+
+    def iota(out, pattern, base=0, cm=0):
+        if out["kind"] == I32:
+            f = lambda: g.iota(ap(out), pattern, base, cm)
+        else:
+            f = lambda: g.iota(ap(out), pattern, base, cm, allow_small_or_imprecise_dtypes=True)
+        return add([("G", 160 + 2 * out["n"], f)], [], [out])
+
+    def fill(out, k, on="V"):
+        if on == "G":
+            return iota(out, [[0, out["n"]]], int(k))
+        return add([("V", cv(out), lambda: g.vector.memset(ap(out), k))], [], [out])
+
+    def tr(out, in_):
+        return add([("V", cv(out, in_), lambda: g.vector.transpose(ap(out), ap(in_)))], [in_], [out])
+
+    def scan(out, d0, d1, init, op0, op1):
+        return add([("V", cv(out, d0, d1), lambda: g.vector.tensor_tensor_scan(ap(out), ap(d0), ap(d1), init, op0, op1))], [d0, d1], [out])
+
+    def pair(q, s, c0, c1):
+        return (A(q, c0, c1), A(s, c0, c1))
+
+    def quant(dst, in_):
+        return add([("V", 30 + 0.265 * in_["n"], lambda: g.vector.quantize_mx(ap(dst[0]), ap(dst[1]), ap(in_)))], [in_], [dst[0], dst[1]])
+
+    def mm(out, *terms):
+        def f():
+            last = None
+            for k, (w, x) in enumerate(terms):
+                last = g.tensor.matmul_mx(ap(out), ap(w[0]), ap(w[1]), ap(x[0]), ap(x[1]), k == 0, k == len(terms) - 1)
+            return last
+        return add([("P", len(terms) * PE * (out["n"] + 16), f)], [v for w, x in terms for v in w + x], [out])
+
+    def pick(dst, src, off):
+        f = lambda: g.vector.tensor_copy(ap(dst[0]).bitcast(dt.uint32), ap(src[0]).bitcast(dt.uint32).indirect(ap(off)))
+        add([("V", 60 + GATHER * dst[0]["n"], f)], [src[0], off], [dst[0]])
+        cp(dst[1], by(src[1], off), "S")
+
+    def dma(q, sem, moves, reads, writes, lat):
+        def f():
+            for o, i in moves:
+                Q[q].dma_start(o, i).then_inc(T.sem[sem], 16)
+        return add([(q, 60.0 * len(moves), f)], reads, writes, sem=sem, inc=16 * len(moves), lat=lat)
+
+    u8 = lambda v: ap(v).bitcast(dt.uint8)
+
+    dma("Y", "dx0", [(T.X0[:, 0:640], T.x[:, 0:640])], [], [A("X0", 0, 640)], 3000.0)
+    dma("S", "du", [(T.U[:], T.u[:])], [], [A("U")], 2800.0)
+    dma("S", "dx1", [(T.X0[:, 640:1280], T.x[:, 640:1280])], [], [A("X0", 640, 1280)], 3000.0)
+    fill(A("NI"), 0)
+    dma("Y", "dn", [(T.NI[64 * u + 10 * k:64 * u + 10 * k + 10, 32 * j:32 * j + 32], src[k::2, 160 * u:160 * u + 160])
+                    for u in range(2) for k in range(2) for j, src in enumerate((T.nb, T.e))], [], [A("NI")], 2400.0)
+    dma("Y", "dw", [(u8(A("WC")), T.wc[:]), (T.WS[:], T.ws[:])], [], [A("WC"), A("WS")], 3500.0)
+    dma("Y", "dv", [(T.VV[:], T.v[:])], [], [A("VV")], 2400.0)
+
+    tabs = [([[0, 2], [1, 16]], 0),
+            ([[0, 2], [1, 8], [32, 2]], 0),
+            ([[1, 2], [2, 8], [32, 2]], 0),
+            ([[0, 4], [16, 8]], 1),
+            ([[0, 2], [32, 4], [0, 4]], 0),
+            ([[1, 32]], 0),
+            ([[1, 2], [2, 16]], 0),
+            ([[512, 2], [0, 16]], 0)]
+    col = lambda k: A("PT", 32 * k, 32 * k + 1)
+    fill(A("MK0"), 2.0 ** -120)
+    add([("G", 200 + 512, lambda: g.affine_select(T.MK[:, 0:256], T.MK0[:], [[0, 2], [-1, 128]], Op.is_ge, 0.0, 0, 1))],
+        [A("MK0")], [A("MK", 0, 256)])
+    add([("G", 200 + 128, lambda: g.affine_select(T.MK[:, 256:320], T.MK0[:, 0:64], [[-1, 64]], Op.is_ge, 0.0, -64, 1))],
+        [A("MK0")], [A("MK", 256, 320)])
+    fill(A("MK", 256, 320, p1=64), 1e29)
+    for k, (pat, base) in enumerate(tabs):
+        boost[0] = EARLY if k in (3, 4) else 0.0
+        iota(A("IT", 32 * k, 32 * k + 32), pat, base)
+    iota(A("IT", 256, 272), [[16, 8], [352, 2]], 7)
+    iota(A("IT", 272, 288), [[16, 8], [-320, 2]], 327)
+    iota(A("PC"), [[0, 1]], 0, 1)
+    iota(A("INN"), [[16, 6], [0, 2], [1, 16]])
+    iota(A("CI", 0, 4), [[16, 2], [0, 2]])
+    iota(A("CI", 8, 16), [[1, 8]])
+    iota(A("CI", 16, 36), [[32, 10], [0, 2]])
+    iota(A("CI", 36, 40), [[1024, 4]])
+    iota(A("CI", 40, 44), [[64, 4]], -160)
+    iota(A("AB"), [[1024, 4], [16, 20]])
+    tr(A("PT", 0, 32), A("IT", 0, 32))
+    tr(A("PT", 32, 96), A("IT", 32, 96))
+    tr(A("PT", 160, 288), A("IT", 160, 288))
+    fill(A("L2"), 2)
+    ts(A("LA"), A("CI", 0, 4), col(0), Op.add)
+    ts(A("LB", 0, 3), A("CI", 8, 11), 8.0, Op.mult, col(1), Op.add)
+    ts(A("LB", 3, 5), A("CI", 8, 10), 16.0, Op.mult, col(2), Op.add)
+    ts(A("LD", 0, 20), A("CI", 16, 36), col(5), Op.add)
+    ts(A("PD", 4, 5), A("PC"), 64.0, Op.is_ge, 160.0, Op.mult)
+    ts(A("LD", 20, 30), A("CI", 16, 26), col(5), Op.add, A("PD", 4, 5), Op.add)
+    ts(A("LE", 0, 3), A("CI", 8, 11), 128.0, Op.mult, col(8), Op.add)
+    ts(A("LF"), A("CI", 8, 10), 32.0, Op.mult, col(6), Op.add)
+    plus(A("HB"), A("CI", 36, 40), col(7))
+    ts(A("AB"), A("AB"), col(0), Op.add, col(7), Op.add)
+    fill(A("ZT"), 0.0)
+    fill(A("CT", 0, 512), 1.0)
+    fill(A("CT", 2, 512, 4, p1=64), 0.0)
+    fill(A("CT", 512, 1536), 0.0)
+    ts(A("PD", 0, 4), A("CI", 40, 44), A("PC"), Op.add, col(0), Op.subtract)
+    for t, k, p0 in ((0, 0, 0), (1, 2, 0), (2, 3, 64)):
+        plus(A("CT", 512 + t, 1024, 4, p0=p0), A("ZT", 0, 128, p0=p0), A("PD", k, k + 1, p0=p0))
+        plus(A("CT", 1024 + t, 1536, 4, p0=p0), A("ZT", 0, 128, p0=p0), A("PT", 0, 1, p0=p0))
+    quant(pair("QC", "SC", 0, 128), A("CT", 0, 512))
+    quant(pair("QC", "SC", 128, 384), A("CT", 512, 1536))
+    boost[0] = EARLY
+    iota(A("GI"), [[-16, 8]], 0, 1)
+    fill(A("EB"), 0.0)
+    for t in range(4):
+        ts(A("EB", 129 * t, 128 * t + 128, 4), A("IT", 0, 32), col(0), Op.is_equal)
+    ts(A("GJ"), A("GI"), 4, Op.arith_shift_right)
+    ts(A("GF"), A("GJ"), 0.0, Op.is_equal)
+    for f in range(8):
+        cp(A("ET", 512 * f, 512 * f + 512), A("EB"), "SV", scale=A("GF", f, f + 1))
+    for k in range(4):
+        quant(pair("QE", "SE", 256 * k, 256 * k + 256), A("ET", 1024 * k, 1024 * k + 1024))
+    tr(A("PT", 96, 160), A("IT", 96, 160))
+    cp(A("LU", 0, 8), A("PT", 96, 104))
+    cp(A("LU", 8, 17), A("PT", 128, 137))
+    ts(A("LU", 17, 26), A("PT", 128, 137), 16.0, Op.add)
+    boost[0] = 0.0
+    for r in range(3):
+        quant(pair("QL%d" % r, "SL%d" % r, 96, 224), A("ZT"))
+    fill(A("RS"), 0.0, "G")
+    fill(A("RS", 0, 160, 32), -1e29)
+    fill(A("KP"), 1.0, "G")
+    fill(A("KP", 0, 160, 32), 0.0)
+    fill(A("FL", 88, 160), 0.0, "G")
+    fill(A("KG", 16, 32), 0.0, "G")
+    fill(A("KG", 352, 368), 0.0, "G")
+    fill(A("KX", 672, 736), 0.0, "G")
+    fill(A("F1", 0, 512, 4), 0.0)
+    fill(A("F1", 513, 1024, 4), 0.0)
+    fill(A("F1", 1026, 1280, 4), 0.0)
+    fill(A("F2", 3, 768, 4), 0.0)
+    fill(A("CF", 0, 160, 2), 0.0)
+    fill(A("CTP", 0, 80, 2), 0.0)
+    fill(A("PF", 40, 64), 0.0, "G")
+    fill(A("SF", 40, 64), 0.0, "G")
+    quant(pair("QU", "SU", 0, 128), A("U"))
+    pick(pair("QU2", "SU2", 0, 128), pair("QU", "SU", 0, 128), A("L2"))
+    boost[0] = EARLY
+    pick(pair("QUP", "SUP", 0, 128), pair("QU", "SU", 0, 128), A("LU", 0, 8))
+    pick(pair("QUP", "SUP", 128, 416), pair("QU", "SU", 0, 128), A("LU", 8, 26))
+    boost[0] = 0.0
+    quant(pair("QV", "SV", 0, 128), A("VV"))
+    U2, UF = pair("QU2", "SU2", 0, 128), pair("QUP", "SUP", 0, 128)
+    UM = [pair("QUP", "SUP", 128 + 144 * (h % 2) + 4 * (h // 2), 256 + 144 * (h % 2) + 4 * (h // 2)) for h in range(8)]
+    EF = [pair("QE", "SE", 128 * f, 128 * f + 128) for f in range(8)]
+    ts(A("NE"), A("NI", 32, 64), 512.0, Op.mult)
+    for q in range(4):
+        s0 = 64 * (q // 2)
+        tt(A("NF", p0=32 * q, p1=32 * q + 32), A("NE", p0=s0, p1=s0 + 32), A("NI", 0, 32, p0=s0, p1=s0 + 32), Op.add)
+    cp(A("ND"), by(A("NF"), A("LA")), "S")
+    tr(A("NT"), A("ND"))
+    cp(A("NY"), by(A("NT"), A("LB", 0, 5)), "S")
+    cp(A("YF"), A("NY", 0, 40), "S")
+    cp(A("T6", 0, 20), A("NY", 48, 68))
+    ts(A("T7", 0, 20), A("T6", 0, 20), 511, Op.bitwise_and)
+    cp(A("OK"), A("T7", 0, 20))
+
+    quant(pair("QX0", "SX0", 0, C), A("X0"))
+    turn = {"l": 0, "v": 0}
+
+    def frames(src, n, c0, b):
+        mm(bank("PL", b, 0, max(n, 128)), (UF, src))
+        split = n == C
+        if split:
+            n = C // 2
+            for u in range(2):
+                tr(A("FT", p0=64 * u, p1=64 * u + 64), A("PL", 512 * b + n * u, 512 * b + n * u + n, p0=64 * u, p1=64 * u + 64))
+        else:
+            tr(A("FT", 0, n), bank("PL", b, 0, n))
+        scan(A("PM", 0, n), A("RS", 0, n), A("FT", 0, n), 0.0, Op.add, Op.max)
+        tt(A("FL", 0, n - 8), A("PM", 0, n - 8), A("PM", 8, n), Op.is_lt)
+        scan(A("KS", 0, n), A("KP", 0, n), A("FL", 0, n), 0.0, Op.mult, Op.add)
+        if split:
+            for u in range(2):
+                for w in range(2):
+                    tr(A("KT", n * u, n * u + n, p0=64 * w, p1=64 * w + 64), A("KS", p0=64 * u, p1=64 * u + 64))
+        else:
+            tr(A("KT", c0, c0 + n), A("KS", 0, n))
+
+    def tables(src, n, c0, marks, values):
+        for h in range(8):
+            if values:
+                b = turn["v"] % 3
+                turn["v"] += 1
+                mm(bank("PV", b, 0, max(n, 128)), (EF[h], src))
+                cp(A("VW", 512 * h + c0, 512 * h + c0 + n), bank("PV", b, 0, n), values)
+            if marks:
+                b = 1 + turn["l"] % 4
+                turn["l"] += 1
+                mm(bank("PL", b, 0, max(n, 128)), (UM[h], src))
+                cp(A("MT", 512 * h + c0, 512 * h + c0 + n), bank("PL", b, 0, n), marks)
+
+    for r, d in enumerate(STEP):
+        qx, sx = "QX%d" % r, "SX%d" % r
+        X = pair(qx, sx, 0, C)
+        chunk = (0, 128, 192)
+        mm(bank("PL", 0, 0, C), (U2, X))
+        for t in (2, 0, 1):
+            mm(bank("PL", 2 + t, 0, 128), (pair(qx, sx, chunk[t], chunk[t] + 128), U2))
+        mm(bank("PL", 1, 0, C), (U2, X))
+        cp(A("SC3", 0, 3), A("PL", 1024, 2049, 512))
+        for t, (j0, j1) in enumerate(((0, 128), (128, 256), (256, 320))):
+            act(A("DD", j0, j1), bank("PL", 1, j0, j1), Fn.Identity, bias=A("SC3", t, t + 1), scale=-1.0)
+        for t, j0, j1, op in ((2, 0, 256, Op.is_lt), (0, 128, 320, Op.is_le), (1, 0, 128, Op.is_lt), (1, 256, 320, Op.is_le)):
+            ts(A("F1", 4 * j0 + t, 4 * j1, 4), bank("PL", 0, j0, j1), bank("PL", 2 + t, 0, 1), op)
+        tt(A("F1", 3, 1280, 4), A("DD"), A("MK"), Op.is_ge)
+        quant(pair("QF1", "SF1", 0, C), A("F1"))
+        for t in range(3):
+            mm(bank("PL", 2 + t, 0, 128), (pair("QF1", "SF1", chunk[t], chunk[t] + 128), pair("QC", "SC", 0, 128)))
+            ts(A("F2", t, 768, 4), A("INN"), bank("PL", 2 + t, 0, 1), Op.is_equal)
+        quant(pair("QF2", "SF2", 0, 192), A("F2"))
+        f2 = pair("QF2", "SF2", 0, 192)
+        mm(bank("PL", 0, 0, 192), (pair("QC", "SC", 128, 256), f2), (pair("QC", "SC", 256, 384), f2))
+        tr(A("OT"), bank("PL", 0, 0, 192))
+        ol = A("OL%d" % r)
+        ts(ol, A("OT", 0, 192, 32), 160.0, Op.add)
+        B = pair("QB%d" % r, "SB%d" % r, 0, H)
+        pick(B, X, ol)
+        dst = T.cores[(rank - d) % N]
+        src = T.cores[(rank + d) % N]
+        L = pair("QL%d" % r, "SL%d" % r, 0, H)
+
+        def send(B=B, L=L, dst=dst, r=r):
+            rid, pid = topo.addr(dst)[:2]
+            m = topo.mask(core, dst)
+            g.remote_dma(u8(L[0]), u8(B[0]), T.sem["arr%d" % r], T.sem.loc, pid, rid, m)
+            g.remote_dma(ap(L[1]), ap(B[1]), T.sem["arr%d" % r], T.sem.loc, pid, rid, m)
+        sent = add([("G", 400.0, send)], [B[0], B[1]], [], sem="loc", inc=2 * len(topo.engines(core, dst)), lat=2000.0)
+        add([("R", 0.0, None)], [], [L[0], L[1]], sem="arr%d" % r, inc=2 * len(topo.engines(src, core)),
+            lat=2600.0 if r == 0 else 900.0, after=[sent])
+        frames(X, C, 0, 1)
+        for j0, j1 in (CUT if r else ((0, C),)):
+            tables(pair(qx, sx, j0, j1), j1 - j0, j0, None, "SV")
+        tables(X, C, 0, "SV", None)
+        cp(A("KO"), by(A("KT", 0, C), A("LD")), "S", scale=512.0)
+        tr(A("KOT"), A("KO"))
+        for q in range(4):
+            cp(A("KA", 20 * q, 20 * q + 20), A("KOT", 7, 320, 16), "SV")
+            cp(A("KR", 10 * q, 10 * q + 10), A("KOT", 327, 480, 16), "SV")
+        tt(A("T4"), A("AB"), A("KA"), Op.add)
+        ts(A("T5"), A("T4"), 4095, Op.bitwise_and)
+        cp(A("OA"), A("T5"))
+        for q in range(4):
+            cp(A("AP", C * q, C * q + C), by(A("VW"), A("OA", 20 * q, 20 * q + 20)), "SV")
+        dma("Y", "da", [(T.AS[32 * q:32 * q + 32, C * t:C * t + C], T.AP[32 * t:32 * t + 32, C * q:C * q + C])
+                        for q in range(4) for t in range(4)], [A("AP")], [A("AS")], 2600.0)
+        tt(A("PF", 0, 40), A("YF"), A("KR"), Op.subtract)
+        cp(A("PH", 0, 32), by(A("PF"), A("LF")), "SV")
+        plus(A("PH", 32, 64), A("PH", 0, 32), 512.0)
+        LL = pair("QL%d" % r, "SL%d" % r, 0, 128)
+        frames(LL, H, C, 0)
+        tables(LL, H, C, "SV", None)
+        tables(LL, H, C, None, "SV")
+        cp(A("KG", 32, 224), by(A("KT"), A("OK", 0, 12)), "V", scale=512.0)
+        cp(A("KG", 224, 352), by(A("KT"), A("OK", 12, 20)), "SV", scale=512.0)
+        tr(A("KX", 0, 320), A("KG", 32, 352))
+        for h in range(2):
+            tt(A("T2", h, 40, 2), A("PH", 32 * h, 32 * h + 20), A("KX", 7, 320, 16), Op.add)
+        ts(A("T3"), A("T2"), 4095, Op.bitwise_and)
+        cp(A("OM"), A("T3"))
+        tr(A("KX", 320, 672), A("KG", 16, 368))
+        cp(A("KF"), by(A("KX"), A("LE", 0, 3)), "SV")
+        tt(A("YF"), A("PF", 0, 40), A("KF", 0, 40), Op.add)
+        tt(A("CD0"), A("YF", 20, 40), A("YF", 0, 20), Op.subtract)
+        for q in range(4):
+            plus(A("CB", 2 * q + 1, 160, 8), A("YF", 0, 20), A("HB", q, q + 1))
+            cp(A("CB", 2 * q, 160, 8), A("CD0"), "SV")
+        for q in range(2):
+            cp(A("MG", C * q, C * q + C), by(A("MT"), A("OM", 20 * q, 20 * q + 20)), "SV")
+            tr(A("MX", C * q, C * q + C), A("MG", C * q, C * q + C))
+        tt(A("CF", 1, 160, 2), A("MX", 320, 640, 4), A("MX", 0, 320, 4), Op.is_gt)
+        tt(A("CM"), A("MX", 320, 640, 4), A("MX", 0, 320, 4), Op.max)
+        scan(A("C1"), A("CF"), A("CB"), 0.0, Op.mult, Op.add)
+        tt(A("CTP", 1, 80, 2), A("CM", 40, 80), A("CM", 0, 40), Op.is_gt)
+        tt(A("C1", 0, 80, 2), A("C1", 81, 160, 2), A("C1", 1, 80, 2), Op.subtract)
+        scan(A("C2"), A("CTP"), A("C1", 0, 80), 0.0, Op.mult, Op.add)
+        for u in range(2):
+            for w in range(2):
+                cp(A("C5", 40 * u, 40 * u + 40, p0=64 * w, p1=64 * w + 64), A("C2", 1, 80, 2, p0=64 * u, p1=64 * u + 64))
+        ts(A("C6"), A("C5"), 4095, Op.bitwise_and)
+        for q in range(4):
+            cp(A("OB", 20 * q, 20 * q + 20), A("C6", q, 80, 4))
+        for q in range(4):
+            tt(A("ZP", C * q, C * q + C), by(A("VW"), A("OB", 20 * q, 20 * q + 20)), A("AP", C * q, C * q + C), Op.add)
+            for t in range(4):
+                cp(A("Z", t, 1280, 4, p0=32 * q, p1=32 * q + 32), A("ZP", C * q, C * q + C, p0=32 * t, p1=32 * t + 32), "SV", scale=0.5)
+        for j0, j1 in CUT:
+            QZ = pair("QZ", "SZ", j0, j1)
+            quant(QZ, A("Z", 4 * j0, 4 * j1))
+            for t in range(4):
+                b = turn["v"] % 3
+                turn["v"] += 1
+                mm(bank("PV", b, 0, j1 - j0), (pair("WC", "WS", 128 * t, 128 * t + 128), QZ))
+                act(A("RL", C * t + j0, C * t + j1), bank("PV", b, 0, j1 - j0), Fn.Relu, scale=0.03125)
+                tt(A("X1", 4 * j0 + t, 4 * j1, 4), A("RL", C * t + j0, C * t + j1), A("AS", C * t + j0, C * t + j1), Op.add)
+            quant(pair("QX%d" % (r + 1), "SX%d" % (r + 1), j0, j1), A("X1", 4 * j0, 4 * j1))
+
+    cp(A("T6"), A("YF"))
+    ts(A("T7"), A("T6"), 9, Op.arith_shift_right, 7, Op.bitwise_and)
+    cp(A("SF", 0, 40), A("T7"))
+    cp(A("SH"), by(A("SF"), A("LF")), "S")
+    tr(A("ST"), A("SH"))
+    dma("Y", "do0", [(T.oe[k::2, 160 * u:160 * u + 160], T.ST[64 * u + 10 * k:64 * u + 10 * k + 10, :]) for u in range(2) for k in range(2)],
+        [A("ST")], [], 2000.0)
+    for k, (j0, j1) in enumerate(CUT):
+        b = turn["v"] % 3
+        turn["v"] += 1
+        mm(bank("PV", b, 0, j1 - j0), (pair("QV", "SV", 0, 128), pair("QX3", "SX3", j0, j1)))
+        cp(A("YO", j0, j1), bank("PV", b, 0, j1 - j0), "SV")
+        dma("Y", "dc%d" % k, [(T.oc[:, 4 * j0:4 * j1], u8(A("QX3", j0, j1)))], [A("QX3", j0, j1)], [], 2200.0 + 2 * (j1 - j0))
+        dma("SY"[k], "dy%d" % k, [(T.y[:, j0:j1], T.YO[:, j0:j1])], [A("YO", j0, j1)], [], 2200.0 + 2 * (j1 - j0))
+    dma("S", "do2", [(T.osc[4 * k:4 * k + 4, :], T.SX3[32 * k:32 * k + 4, :]) for k in range(4)], [A("SX3")], [], 2000.0)
+
+    emit(g, T, Q, ops)
+
+
+PLAN = {}
+
+
+def plan(ops, deps, soft):
+    n = len(ops)
+    level = [0.0] * n
+    users = [[] for _ in range(n)]
+    for i in range(n - 1, -1, -1):
+        level[i] += min(a[1] for a in ops[i]["alts"]) + ops[i]["lat"] + SYNC
+        for j in deps[i]:
+            level[j] = max(level[j], level[i])
+            users[j].append(i)
+    best, seed = None, 12345
+    base, tilt = [level[i] + ops[i]["boost"] for i in range(n)], [400.0] * n
+    for trial in range(TRIES):
+        prio, lean = list(base), list(tilt)
+        if trial:
+            run, push = 0, 0.0
+            for i in range(n):
+                seed = (seed * 1103515245 + 12345) % 2147483648
+                k = seed >> 8
+                if k % 40 == 0:
+                    prio[i] += (k >> 6) % 2001 - 1000
+                if k % 40 == 1:
+                    lean[i] = (k >> 6) % 2001 - 600.0
+                if k % 400 == 2:
+                    run, push = (k >> 9) % 24, ((k >> 14) % 41 - 20) * 250.0
+                if run > 0:
+                    run -= 1
+                    prio[i] += push
+        busy = {q: [] for q in "VSPGYR"}
+        start, end, eng = [0.0] * n, [0.0] * n, [0] * n
+        left = [len(d) for d in deps]
+        ready = [i for i in range(n) if not left[i]]
+        while ready:
+            i = max(ready, key=lambda k: (prio[k], -k))
+            ready.remove(i)
+            got = None
+            for k, a in enumerate(ops[i]["alts"]):
+                s = 0.0
+                for j in deps[i]:
+                    s = max(s, end[j] + (0.0 if j in soft[i] and ops[j]["alts"][eng[j]][0] == a[0] else SYNC))
+                for b0, b1 in busy[a[0]]:
+                    if s + a[1] <= b0:
+                        break
+                    s = max(s, b1)
+                if got is None or s + a[1] + lean[i] < got[0] + got[2]:
+                    got = (s, k, a[1], a[0])
+            start[i], eng[i] = got[0], got[1]
+            end[i] = got[0] + got[2] + ops[i]["lat"]
+            busy[got[3]].append((got[0], got[0] + got[2]))
+            busy[got[3]].sort()
+            for u in users[i]:
+                left[u] -= 1
+                if not left[u]:
+                    ready.append(u)
+        if best is None or max(end) <= best[0]:
+            best = (max(end), start, end, eng)
+            base, tilt = prio, lean
+    return best
+
+
+def emit(g, T, Q, ops):
+    n = len(ops)
+    deps = [set(o["after"]) for o in ops]
+    hard = [set(o["after"]) for o in ops]
+    seen = {}
+    for i, o in enumerate(ops):
+        for regs, w in ((o["r"], False), (o["w"], True)):
+            for name, pm, cm in regs:
+                ps = name in ("PL", "PV")
+                for j, pj, cj, wj in seen.get(name, ()):
+                    if j != i and (w or wj or ps) and pm & pj and cm & cj:
+                        deps[i].add(j)
+                        if w or wj:
+                            hard[i].add(j)
+        for regs, w in ((o["r"], False), (o["w"], True)):
+            for name, pm, cm in regs:
+                old = seen.get(name, [])
+                if w:
+                    old = [e for e in old if (e[1] & ~pm) or (e[2] & ~cm)]
+                seen[name] = old + [(i, pm, cm, w)]
+    lastsem = {}
+    for i, o in enumerate(ops):
+        if o["sem"] is not None:
+            if o["sem"] in lastsem:
+                deps[i].add(lastsem[o["sem"]])
+                hard[i].add(lastsem[o["sem"]])
+            lastsem[o["sem"]] = i
+    soft = [deps[i] - hard[i] for i in range(n)]
+    if n not in PLAN:
+        PLAN[n] = plan(ops, [sorted(d) for d in deps], soft)
+    span, start, end, eng = PLAN[n]
+    count, known, mark = {}, {q: {} for q in Q}, [None] * n
+    for i in sorted(range(n), key=lambda k: (start[k], k)):
+        o = ops[i]
+        q = o["alts"][eng[i]][0]
+        sem = o["sem"] or "e" + q
+        count[sem] = count.get(sem, 0) + o["inc"]
+        if q == "R":
+            mark[i] = (sem, count[sem], {})
+            continue
+        for j in sorted(deps[i], key=lambda k: (-end[k], k)):
+            if j in soft[i] and ops[j]["alts"][eng[j]][0] == q:
+                continue
+            s, v, clock = mark[j]
+            if known[q].get(s, 0) < v:
+                Q[q].wait_ge(T.sem[s], v)
+                known[q][s] = v
+                for s2, v2 in clock.items():
+                    known[q][s2] = max(known[q].get(s2, 0), v2)
+        ins = o["alts"][eng[i]][2]()
+        if o["sem"] is None:
+            ins.then_inc(T.sem[sem], 1)
+        mark[i] = (sem, count[sem], dict(known[q]))
+    for s, v in count.items():
+        g.wait_ge(T.sem[s], v)

@@ -14,18 +14,18 @@ SB = {
     "MK0": (256, BF), "MK": (320, BF), "DD": (320, BF), "SC3": (4, F32), "INN": (192, BF), "OT": (192, F32),
     "FT": (160, F32), "PM": (160, F32), "FL": (160, BF), "KS": (160, BF), "RS": (160, F32), "KP": (160, BF),
     "KT": (416, BF), "KG": (384, BF), "KX": (736, BF), "KO": (480, BF), "KOT": (480, BF), "KF": (48, F32),
-    "KA": (80, F32), "KR": (40, F32),
+    "KA": (128, F32), "SQ": (128, F32), "SD": (256, F32), "SW": (256, F32), "HT": (160, F32), "LK": (8, U16), "LC": (10, U16),
     "NI": (64, I32), "NE": (32, F32), "NF": (32, F32), "ND": (64, F32), "NT": (64, F32), "NY": (80, F32),
-    "YF": (40, F32), "PF": (64, F32), "PH": (64, F32), "T2": (40, I32), "T3": (40, I32),
+    "YF": (64, F32), "PF": (64, F32), "PH": (64, F32), "T2": (40, I32), "T3": (40, I32),
     "T4": (80, I32), "T5": (80, I32), "T6": (40, I32), "T7": (40, I32),
-    "CB": (160, F32), "CD0": (20, F32), "CF": (160, F32), "CM": (80, F32), "CTP": (80, F32), "C1": (160, F32),
+    "CB": (160, F32), "CF": (160, F32), "CM": (80, F32), "CTP": (80, F32), "C1": (160, F32),
     "C2": (80, F32), "C5": (80, I32), "C6": (80, I32),
     "MT": (4096, F32), "MG": (640, F32), "MX": (640, F32),
     "VW": (4096, BF), "AP": (1280, BF), "AS": (1280, BF), "ZP": (1280, BF), "Z": (1280, BF),
     "QZ": (320, CD), "SZ": (320, PL), "RL": (1280, F32), "YO": (320, F32),
-    "IT": (288, F32), "PT": (288, F32), "CI": (64, F32), "PC": (1, F32), "GI": (8, I32), "GJ": (8, I32), "GF": (8, F32),
-    "HB": (4, F32), "AB": (80, F32), "PD": (6, F32),
-    "L2": (8, U16), "LU": (26, U16), "LA": (4, U16), "LB": (6, U16), "LD": (30, U16), "LE": (4, U16), "LF": (2, U16),
+    "IT": (320, F32), "PT": (320, F32), "CI": (80, F32), "PC": (1, F32), "GI": (8, I32), "GJ": (8, I32), "GF": (8, F32),
+    "AB": (80, F32), "PD": (6, F32),
+    "L2": (8, U16), "LU": (26, U16), "LA": (16, U16), "LB": (6, U16), "LD": (30, U16), "LE": (4, U16), "LF": (2, U16),
     "OK": (20, U16), "OM": (40, U16), "OA": (80, U16), "OB": (80, U16),
     "SF": (64, F32), "SH": (32, F32), "ST": (32, F32),
 }
@@ -39,7 +39,7 @@ for _r in range(3):
     SB["SL%d" % _r] = (224, PL)
     SB["OL%d" % _r] = (6, U16)
 PART = {}
-for _pool, _names in (("TI", "T2 T3 T4 T5 T6 T7 C5 C6"), ("TF", "CF CM CTP C1 C2 CD0 CB KA KR")):
+for _pool, _names in (("TI", "T2 T3 T4 T5 T6 T7 C5 C6"), ("TF", "CF CM CTP C1 C2 CB KA")):
     _at = 0
     for _k in _names.split():
         PART[_k] = (_pool, _at, SB[_k][0])
@@ -51,8 +51,8 @@ SCRATCH["PV"] = ("psum", [128, 512 * 3], F32)
 SEMAPHORES = ["eV", "eS", "eP", "eG", "dx0", "dx1", "du", "dv", "dw", "dn", "da", "do0", "do2", "dc0", "dc1", "dy0", "dy1",
               "arr0", "arr1", "arr2", "loc"]
 WIDE = {BF: 2, F32: 4, I32: 4, U16: 2, CD: 4, PL: 1}
-SYNC, OVER, GATHER, PE = 90.0, 55.0, 1.55, 0.75
-TRIES, EARLY = 2000, 7000.0
+SYNC, OVER, GATHER, PE = 170.0, 60.0, 1.55, 1.3
+TRIES, EARLY = 2500, 5000.0
 CUT = ((0, 192), (192, 320))
 Op, Fn = AluOpType, ActivationFunctionType
 
@@ -65,6 +65,12 @@ def rank_program(g, core, T, topo):
     ops = []
     boost = [0.0]
     Q = {"V": g.vector, "S": g.scalar, "P": g.tensor, "G": g, "Y": g.sync}
+
+    def lanes(k):
+        m = -1
+        for d in STEP:
+            m &= topo.mask(T.cores[k], T.cores[(k - d) % N])
+        return m, bin(m).count("1")
 
     def A(name, c0=0, c1=None, step=1, p0=0, p1=128):
         if name in PART:
@@ -224,19 +230,31 @@ def rank_program(g, core, T, topo):
         iota(A("IT", 32 * k, 32 * k + 32), pat, base)
     iota(A("IT", 256, 272), [[16, 8], [352, 2]], 7)
     iota(A("IT", 272, 288), [[16, 8], [-320, 2]], 327)
+    for h in range(2):
+        iota(A("IT", 288 + 16 * h, 304 + 16 * h), [[1, 2], [0, 4], [-40, 2]], 40)
     iota(A("PC"), [[0, 1]], 0, 1)
     iota(A("INN"), [[16, 6], [0, 2], [1, 16]])
-    iota(A("CI", 0, 4), [[16, 2], [0, 2]])
     iota(A("CI", 8, 16), [[1, 8]])
     iota(A("CI", 16, 36), [[32, 10], [0, 2]])
-    iota(A("CI", 36, 40), [[1024, 4]])
     iota(A("CI", 40, 44), [[64, 4]], -160)
+    iota(A("CI", 48, 64), [[16, 8], [0, 2]])
+    iota(A("CI", 64, 74), [[2, 10]])
+    iota(A("SQ", 0, 80), [[0, 4], [16, 20]], 7)
+    iota(A("SQ", 80, 120), [[0, 4], [16, 10]], 327)
+    fill(A("SQ", 120, 128), 0.0, "G")
+    iota(A("HT", 1, 160, 2), [[0, 20], [1024, 4]])
     iota(A("AB"), [[1024, 4], [16, 20]])
     tr(A("PT", 0, 32), A("IT", 0, 32))
     tr(A("PT", 32, 96), A("IT", 32, 96))
-    tr(A("PT", 160, 288), A("IT", 160, 288))
+    tr(A("PT", 160, 320), A("IT", 160, 320))
     fill(A("L2"), 2)
-    ts(A("LA"), A("CI", 0, 4), col(0), Op.add)
+    ts(A("LA"), A("CI", 48, 64), col(0), Op.add)
+    cp(A("SD"), by(A("SQ"), A("LA")), "S")
+    tr(A("SW"), A("SD"))
+    cp(A("LK"), A("SW", 0, 256, 32))
+    ts(A("LC"), A("CI", 64, 74), col(9), Op.add)
+    fill(A("HT", 0, 160, 2), 0.0)
+    plus(A("HT", 1, 160, 2), A("HT", 1, 160, 2), col(7))
     ts(A("LB", 0, 3), A("CI", 8, 11), 8.0, Op.mult, col(1), Op.add)
     ts(A("LB", 3, 5), A("CI", 8, 10), 16.0, Op.mult, col(2), Op.add)
     ts(A("LD", 0, 20), A("CI", 16, 36), col(5), Op.add)
@@ -244,7 +262,6 @@ def rank_program(g, core, T, topo):
     ts(A("LD", 20, 30), A("CI", 16, 26), col(5), Op.add, A("PD", 4, 5), Op.add)
     ts(A("LE", 0, 3), A("CI", 8, 11), 128.0, Op.mult, col(8), Op.add)
     ts(A("LF"), A("CI", 8, 10), 32.0, Op.mult, col(6), Op.add)
-    plus(A("HB"), A("CI", 36, 40), col(7))
     ts(A("AB"), A("AB"), col(0), Op.add, col(7), Op.add)
     fill(A("ZT"), 0.0)
     fill(A("CT", 0, 512), 1.0)
@@ -304,10 +321,10 @@ def rank_program(g, core, T, topo):
     for q in range(4):
         s0 = 64 * (q // 2)
         tt(A("NF", p0=32 * q, p1=32 * q + 32), A("NE", p0=s0, p1=s0 + 32), A("NI", 0, 32, p0=s0, p1=s0 + 32), Op.add)
-    cp(A("ND"), by(A("NF"), A("LA")), "S")
+    cp(A("ND"), by(A("NF"), A("LA", 0, 4)), "S")
     tr(A("NT"), A("ND"))
     cp(A("NY"), by(A("NT"), A("LB", 0, 5)), "S")
-    cp(A("YF"), A("NY", 0, 40), "S")
+    cp(A("YF", 0, 40), A("NY", 0, 40), "S")
     cp(A("T6", 0, 20), A("NY", 48, 68))
     ts(A("T7", 0, 20), A("T6", 0, 20), 511, Op.bitwise_and)
     cp(A("OK"), A("T7", 0, 20))
@@ -374,34 +391,30 @@ def rank_program(g, core, T, topo):
         B = pair("QB%d" % r, "SB%d" % r, 0, H)
         pick(B, X, ol)
         dst = T.cores[(rank - d) % N]
-        src = T.cores[(rank + d) % N]
         L = pair("QL%d" % r, "SL%d" % r, 0, H)
 
         def send(B=B, L=L, dst=dst, r=r):
             rid, pid = topo.addr(dst)[:2]
-            m = topo.mask(core, dst)
+            m = lanes(rank)[0]
             g.remote_dma(u8(L[0]), u8(B[0]), T.sem["arr%d" % r], T.sem.loc, pid, rid, m)
             g.remote_dma(ap(L[1]), ap(B[1]), T.sem["arr%d" % r], T.sem.loc, pid, rid, m)
-        sent = add([("G", 400.0, send)], [B[0], B[1]], [], sem="loc", inc=2 * len(topo.engines(core, dst)), lat=2000.0)
-        add([("R", 0.0, None)], [], [L[0], L[1]], sem="arr%d" % r, inc=2 * len(topo.engines(src, core)),
+        sent = add([("G", 400.0, send)], [B[0], B[1]], [], sem="loc", inc=2 * lanes(rank)[1], lat=2000.0)
+        add([("R", 0.0, None)], [], [L[0], L[1]], sem="arr%d" % r, inc=2 * lanes((rank + d) % N)[1],
             lat=2600.0 if r == 0 else 900.0, after=[sent])
         frames(X, C, 0, 1)
-        for j0, j1 in (CUT if r else ((0, C),)):
-            tables(pair(qx, sx, j0, j1), j1 - j0, j0, None, "SV")
+        tables(X, C, 0, None, "SV")
         tables(X, C, 0, "SV", None)
         cp(A("KO"), by(A("KT", 0, C), A("LD")), "S", scale=512.0)
         tr(A("KOT"), A("KO"))
-        for q in range(4):
-            cp(A("KA", 20 * q, 20 * q + 20), A("KOT", 7, 320, 16), "SV")
-            cp(A("KR", 10 * q, 10 * q + 10), A("KOT", 327, 480, 16), "SV")
-        tt(A("T4"), A("AB"), A("KA"), Op.add)
+        cp(A("KA"), by(A("KOT"), A("LK")), "SV")
+        tt(A("T4"), A("AB"), A("KA", 0, 80), Op.add)
         ts(A("T5"), A("T4"), 4095, Op.bitwise_and)
         cp(A("OA"), A("T5"))
         for q in range(4):
             cp(A("AP", C * q, C * q + C), by(A("VW"), A("OA", 20 * q, 20 * q + 20)), "SV")
         dma("Y", "da", [(T.AS[32 * q:32 * q + 32, C * t:C * t + C], T.AP[32 * t:32 * t + 32, C * q:C * q + C])
-                        for q in range(4) for t in range(4)], [A("AP")], [A("AS")], 2600.0)
-        tt(A("PF", 0, 40), A("YF"), A("KR"), Op.subtract)
+                        for q in range(4) for t in range(4)], [A("AP")], [A("AS")], 3200.0)
+        tt(A("PF", 0, 40), A("YF", 0, 40), A("KA", 80, 120), Op.subtract)
         cp(A("PH", 0, 32), by(A("PF"), A("LF")), "SV")
         plus(A("PH", 32, 64), A("PH", 0, 32), 512.0)
         LL = pair("QL%d" % r, "SL%d" % r, 0, 128)
@@ -417,11 +430,9 @@ def rank_program(g, core, T, topo):
         cp(A("OM"), A("T3"))
         tr(A("KX", 320, 672), A("KG", 16, 368))
         cp(A("KF"), by(A("KX"), A("LE", 0, 3)), "SV")
-        tt(A("YF"), A("PF", 0, 40), A("KF", 0, 40), Op.add)
-        tt(A("CD0"), A("YF", 20, 40), A("YF", 0, 20), Op.subtract)
-        for q in range(4):
-            plus(A("CB", 2 * q + 1, 160, 8), A("YF", 0, 20), A("HB", q, q + 1))
-            cp(A("CB", 2 * q, 160, 8), A("CD0"), "SV")
+        tt(A("YF", 0, 40), A("PF", 0, 40), A("KF", 0, 40), Op.add)
+        tt(A("YF", 40, 60), A("YF", 20, 40), A("YF", 0, 20), Op.subtract)
+        tt(A("CB"), by(A("YF", 0, 60), A("LC")), A("HT"), Op.add)
         for q in range(2):
             cp(A("MG", C * q, C * q + C), by(A("MT"), A("OM", 20 * q, 20 * q + 20)), "SV")
             tr(A("MX", C * q, C * q + C), A("MG", C * q, C * q + C))
@@ -452,7 +463,7 @@ def rank_program(g, core, T, topo):
                 tt(A("X1", 4 * j0 + t, 4 * j1, 4), A("RL", C * t + j0, C * t + j1), A("AS", C * t + j0, C * t + j1), Op.add)
             quant(pair("QX%d" % (r + 1), "SX%d" % (r + 1), j0, j1), A("X1", 4 * j0, 4 * j1))
 
-    cp(A("T6"), A("YF"))
+    cp(A("T6"), A("YF", 0, 40))
     ts(A("T7"), A("T6"), 9, Op.arith_shift_right, 7, Op.bitwise_and)
     cp(A("SF", 0, 40), A("T7"))
     cp(A("SH"), by(A("SF"), A("LF")), "S")

@@ -11,7 +11,7 @@ SB = {
     "EB": (512, BF), "ET": (4096, BF), "QE": (1024, CD), "SE": (1024, PL),
     "CT": (1536, BF), "QC": (384, CD), "SC": (384, PL), "ZT": (512, BF),
     "F1": (1280, BF), "QF1": (320, CD), "SF1": (320, PL), "F2": (768, BF), "QF2": (192, CD), "SF2": (192, PL),
-    "MK0": (256, BF), "MK": (320, BF), "DD": (320, BF), "SC3": (4, F32), "INN": (192, BF), "OT": (192, F32),
+    "MK0": (128, BF), "MK": (320, BF), "DD": (320, BF), "SC3": (4, F32), "INN": (192, BF), "OT": (192, F32),
     "FT": (160, F32), "PM": (160, F32), "FL": (160, BF), "KS": (160, BF), "RS": (160, F32), "KP": (160, BF),
     "KT": (416, BF), "KG": (384, BF), "KX": (736, BF), "KO": (480, BF), "KOT": (480, BF), "KF": (48, F32),
     "KA": (128, F32), "SQ": (128, F32), "SD": (256, F32), "SW": (256, F32), "HT": (160, F32), "LK": (8, U16), "LC": (10, U16),
@@ -48,11 +48,11 @@ for _pool, _names in (("TI", "T2 T3 T4 T5 T6 T7 C5 C6"), ("TF", "CF CM CTP C1 C2
 SCRATCH = {k: ("sbuf", [128, n], d) for k, (n, d) in SB.items()}
 SCRATCH["PL"] = ("psum", [128, 512 * 5], F32)
 SCRATCH["PV"] = ("psum", [128, 512 * 3], F32)
-SEMAPHORES = ["eV", "eS", "eP", "eG", "dx0", "dx1", "du", "dv", "dw", "dn", "da", "do0", "do2", "dc0", "dc1", "dy0", "dy1",
-              "arr0", "arr1", "arr2", "loc"]
+SEMAPHORES = ["eV", "eS", "eP", "eG", "dx0", "dx1", "du", "dv", "dw", "dn", "da0", "da1", "da2", "da3",
+              "do0", "do2", "dc0", "dc1", "dy0", "dy1", "arr0", "arr1", "arr2", "loc0", "loc1"]
 WIDE = {BF: 2, F32: 4, I32: 4, U16: 2, CD: 4, PL: 1}
-SYNC, OVER, GATHER, PE = 170.0, 60.0, 1.55, 1.3
-TRIES, EARLY = 2500, 5000.0
+SYNC, OVER, GATHER, PE = 165.0, 66.0, 1.55, 1.3
+TRIES, EARLY = 18000, 5000.0
 CUT = ((0, 192), (192, 320))
 Op, Fn = AluOpType, ActivationFunctionType
 
@@ -197,13 +197,13 @@ def rank_program(g, core, T, topo):
         def f():
             for o, i in moves:
                 Q[q].dma_start(o, i).then_inc(T.sem[sem], 16)
-        return add([(q, 60.0 * len(moves), f)], reads, writes, sem=sem, inc=16 * len(moves), lat=lat)
+        return add([(q, 150.0 * len(moves), f)], reads, writes, sem=sem, inc=16 * len(moves), lat=lat)
 
     u8 = lambda v: ap(v).bitcast(dt.uint8)
 
-    dma("Y", "dx0", [(T.X0[:, 0:640], T.x[:, 0:640])], [], [A("X0", 0, 640)], 3000.0)
+    dma("Y", "dx0", [(T.X0[:, 0:768], T.x[:, 0:768])], [], [A("X0", 0, 768)], 3000.0)
     dma("S", "du", [(T.U[:], T.u[:])], [], [A("U")], 2800.0)
-    dma("S", "dx1", [(T.X0[:, 640:1280], T.x[:, 640:1280])], [], [A("X0", 640, 1280)], 3000.0)
+    dma("S", "dx1", [(T.X0[:, 768:1280], T.x[:, 768:1280])], [], [A("X0", 768, 1280)], 3000.0)
     fill(A("NI"), 0)
     dma("Y", "dn", [(T.NI[64 * u + 10 * k:64 * u + 10 * k + 10, 32 * j:32 * j + 32], src[k::2, 160 * u:160 * u + 160])
                     for u in range(2) for k in range(2) for j, src in enumerate((T.nb, T.e))], [], [A("NI")], 2400.0)
@@ -220,11 +220,12 @@ def rank_program(g, core, T, topo):
             ([[512, 2], [0, 16]], 0)]
     col = lambda k: A("PT", 32 * k, 32 * k + 1)
     fill(A("MK0"), 2.0 ** -120)
-    add([("G", 200 + 512, lambda: g.affine_select(T.MK[:, 0:256], T.MK0[:], [[0, 2], [-1, 128]], Op.is_ge, 0.0, 0, 1))],
-        [A("MK0")], [A("MK", 0, 256)])
-    add([("G", 200 + 128, lambda: g.affine_select(T.MK[:, 256:320], T.MK0[:, 0:64], [[-1, 64]], Op.is_ge, 0.0, -64, 1))],
-        [A("MK0")], [A("MK", 256, 320)])
-    fill(A("MK", 256, 320, p1=64), 1e29)
+    add([("G", 200 + 256, lambda: g.affine_select(T.MK[:, 0:128], T.MK0[:], [[-1, 128]], Op.is_ge, 0.0, 0, 1))],
+        [A("MK0")], [A("MK", 0, 128)])
+    add([("G", 200 + 128, lambda: g.affine_select(T.MK[:, 128:192], T.MK0[:, 0:64], [[-1, 64]], Op.is_ge, 0.0, -64, 1))],
+        [A("MK0")], [A("MK", 128, 192)])
+    fill(A("MK", 128, 192, p1=64), 1e29)
+    cp(A("MK", 192, 320), A("MK", 0, 128), "SV")
     for k, (pat, base) in enumerate(tabs):
         boost[0] = EARLY if k in (3, 4) else 0.0
         iota(A("IT", 32 * k, 32 * k + 32), pat, base)
@@ -265,10 +266,10 @@ def rank_program(g, core, T, topo):
     ts(A("AB"), A("AB"), col(0), Op.add, col(7), Op.add)
     fill(A("ZT"), 0.0)
     fill(A("CT", 0, 512), 1.0)
-    fill(A("CT", 2, 512, 4, p1=64), 0.0)
+    fill(A("CT", 1, 512, 4, p1=64), 0.0)
     fill(A("CT", 512, 1536), 0.0)
     ts(A("PD", 0, 4), A("CI", 40, 44), A("PC"), Op.add, col(0), Op.subtract)
-    for t, k, p0 in ((0, 0, 0), (1, 2, 0), (2, 3, 64)):
+    for t, k, p0 in ((0, 0, 0), (1, 1, 64), (2, 3, 0)):
         plus(A("CT", 512 + t, 1024, 4, p0=p0), A("ZT", 0, 128, p0=p0), A("PD", k, k + 1, p0=p0))
         plus(A("CT", 1024 + t, 1536, 4, p0=p0), A("ZT", 0, 128, p0=p0), A("PT", 0, 1, p0=p0))
     quant(pair("QC", "SC", 0, 128), A("CT", 0, 512))
@@ -300,8 +301,8 @@ def rank_program(g, core, T, topo):
     fill(A("KG", 352, 368), 0.0, "G")
     fill(A("KX", 672, 736), 0.0, "G")
     fill(A("F1", 0, 512, 4), 0.0)
-    fill(A("F1", 513, 1024, 4), 0.0)
-    fill(A("F1", 1026, 1280, 4), 0.0)
+    fill(A("F1", 513, 768, 4), 0.0)
+    fill(A("F1", 770, 1280, 4), 0.0)
     fill(A("F2", 3, 768, 4), 0.0)
     fill(A("CF", 0, 160, 2), 0.0)
     fill(A("CTP", 0, 80, 2), 0.0)
@@ -329,7 +330,8 @@ def rank_program(g, core, T, topo):
     ts(A("T7", 0, 20), A("T6", 0, 20), 511, Op.bitwise_and)
     cp(A("OK"), A("T7", 0, 20))
 
-    quant(pair("QX0", "SX0", 0, C), A("X0"))
+    for j0, j1 in CUT:
+        quant(pair("QX0", "SX0", j0, j1), A("X0", 4 * j0, 4 * j1))
     turn = {"l": 0, "v": 0}
 
     def frames(src, n, c0, b):
@@ -367,18 +369,28 @@ def rank_program(g, core, T, topo):
     for r, d in enumerate(STEP):
         qx, sx = "QX%d" % r, "SX%d" % r
         X = pair(qx, sx, 0, C)
-        chunk = (0, 128, 192)
-        mm(bank("PL", 0, 0, C), (U2, X))
-        for t in (2, 0, 1):
+        chunk = (0, 64, 192)
+        XA, XB = pair(qx, sx, 0, 192), pair(qx, sx, 192, C)
+        sc = lambda t: A("SC3", t, t + 1)
+        for t in (0, 1):
             mm(bank("PL", 2 + t, 0, 128), (pair(qx, sx, chunk[t], chunk[t] + 128), U2))
-        mm(bank("PL", 1, 0, C), (U2, X))
-        cp(A("SC3", 0, 3), A("PL", 1024, 2049, 512))
-        for t, (j0, j1) in enumerate(((0, 128), (128, 256), (256, 320))):
-            act(A("DD", j0, j1), bank("PL", 1, j0, j1), Fn.Identity, bias=A("SC3", t, t + 1), scale=-1.0)
-        for t, j0, j1, op in ((2, 0, 256, Op.is_lt), (0, 128, 320, Op.is_le), (1, 0, 128, Op.is_lt), (1, 256, 320, Op.is_le)):
-            ts(A("F1", 4 * j0 + t, 4 * j1, 4), bank("PL", 0, j0, j1), bank("PL", 2 + t, 0, 1), op)
-        tt(A("F1", 3, 1280, 4), A("DD"), A("MK"), Op.is_ge)
-        quant(pair("QF1", "SF1", 0, C), A("F1"))
+        mm(bank("PL", 1, 0, 192), (U2, XA))
+        mm(bank("PL", 0, 0, 192), (U2, XA))
+        cp(A("SC3", 0, 2), A("PL", 1024, 1537, 512), "SV")
+        act(A("DD", 0, 128), bank("PL", 1, 0, 128), Fn.Identity, bias=sc(0), scale=-1.0)
+        act(A("DD", 128, 192), bank("PL", 1, 128, 192), Fn.Identity, bias=sc(1), scale=-1.0)
+        ts(A("F1", 512, 768, 4), bank("PL", 0, 128, 192), sc(0), Op.is_le)
+        ts(A("F1", 1, 512, 4), bank("PL", 0, 0, 128), sc(1), Op.is_lt)
+        tt(A("F1", 3, 768, 4), A("DD", 0, 192), A("MK", 0, 192), Op.is_ge)
+        mm(bank("PL", 4, 0, 128), (XB, U2))
+        mm(bank("PL", 2, 0, 128), (U2, XB))
+        ts(A("DD", 192, C), bank("PL", 2, 0, 128), bank("PL", 4, 0, 1), Op.subtract, -1.0, Op.mult)
+        ts(A("F1", 2, 768, 4), bank("PL", 0, 0, 192), bank("PL", 4, 0, 1), Op.is_lt)
+        for t in (0, 1):
+            ts(A("F1", 768 + t, 1280, 4), bank("PL", 2, 0, 128), sc(t), Op.is_le)
+        tt(A("F1", 771, 1280, 4), A("DD", 192, C), A("MK", 192, C), Op.is_ge)
+        for j0, j1 in CUT:
+            quant(pair("QF1", "SF1", j0, j1), A("F1", 4 * j0, 4 * j1))
         for t in range(3):
             mm(bank("PL", 2 + t, 0, 128), (pair("QF1", "SF1", chunk[t], chunk[t] + 128), pair("QC", "SC", 0, 128)))
             ts(A("F2", t, 768, 4), A("INN"), bank("PL", 2 + t, 0, 1), Op.is_equal)
@@ -393,16 +405,18 @@ def rank_program(g, core, T, topo):
         dst = T.cores[(rank - d) % N]
         L = pair("QL%d" % r, "SL%d" % r, 0, H)
 
-        def send(B=B, L=L, dst=dst, r=r):
+        def send(out, in_, sem, dst=dst, r=r):
             rid, pid = topo.addr(dst)[:2]
-            m = lanes(rank)[0]
-            g.remote_dma(u8(L[0]), u8(B[0]), T.sem["arr%d" % r], T.sem.loc, pid, rid, m)
-            g.remote_dma(ap(L[1]), ap(B[1]), T.sem["arr%d" % r], T.sem.loc, pid, rid, m)
-        sent = add([("G", 400.0, send)], [B[0], B[1]], [], sem="loc", inc=2 * lanes(rank)[1], lat=2000.0)
+            return lambda: g.remote_dma(out, in_, T.sem["arr%d" % r], T.sem[sem], pid, rid, lanes(rank)[0])
+        sent = [add([("G", 200.0, send(ap(L[1]), ap(B[1]), "loc0"))], [B[1]], [], sem="loc0", inc=lanes(rank)[1], lat=2000.0),
+                add([("G", 200.0, send(u8(L[0]), u8(B[0]), "loc1"))], [B[0]], [], sem="loc1", inc=lanes(rank)[1], lat=2200.0)]
         add([("R", 0.0, None)], [], [L[0], L[1]], sem="arr%d" % r, inc=2 * lanes((rank + d) % N)[1],
-            lat=2600.0 if r == 0 else 900.0, after=[sent])
+            lat=2600.0 if r == 0 else 900.0, after=sent)
         frames(X, C, 0, 1)
-        tables(X, C, 0, None, "SV")
+        boost[0] = 3000.0 if r else 0.0
+        tables(XA, 192, 0, None, "S")
+        boost[0] = 0.0
+        tables(XB, 128, 192, None, "SV")
         tables(X, C, 0, "SV", None)
         cp(A("KO"), by(A("KT", 0, C), A("LD")), "S", scale=512.0)
         tr(A("KOT"), A("KO"))
@@ -412,8 +426,8 @@ def rank_program(g, core, T, topo):
         cp(A("OA"), A("T5"))
         for q in range(4):
             cp(A("AP", C * q, C * q + C), by(A("VW"), A("OA", 20 * q, 20 * q + 20)), "SV")
-        dma("Y", "da", [(T.AS[32 * q:32 * q + 32, C * t:C * t + C], T.AP[32 * t:32 * t + 32, C * q:C * q + C])
-                        for q in range(4) for t in range(4)], [A("AP")], [A("AS")], 3200.0)
+            dma("Y", "da%d" % q, [(T.AS[32 * q:32 * q + 32, C * t:C * t + C], T.AP[32 * t:32 * t + 32, C * q:C * q + C])
+                                  for t in range(4)], [A("AP", C * q, C * q + C)], [A("AS", p0=32 * q, p1=32 * q + 32)], 3200.0)
         tt(A("PF", 0, 40), A("YF", 0, 40), A("KA", 80, 120), Op.subtract)
         cp(A("PH", 0, 32), by(A("PF"), A("LF")), "SV")
         plus(A("PH", 32, 64), A("PH", 0, 32), 512.0)
@@ -449,9 +463,12 @@ def rank_program(g, core, T, topo):
         for q in range(4):
             cp(A("OB", 20 * q, 20 * q + 20), A("C6", q, 80, 4))
         for q in range(4):
-            tt(A("ZP", C * q, C * q + C), by(A("VW"), A("OB", 20 * q, 20 * q + 20)), A("AP", C * q, C * q + C), Op.add)
-            for t in range(4):
-                cp(A("Z", t, 1280, 4, p0=32 * q, p1=32 * q + 32), A("ZP", C * q, C * q + C, p0=32 * t, p1=32 * t + 32), "SV", scale=0.5)
+            for j0, j1 in (CUT if q >= 2 else ((0, C),)):
+                tt(A("ZP", C * q + j0, C * q + j1), by(A("VW"), A("OB", 20 * q + j0 // 16, 20 * q + j1 // 16)),
+                   A("AP", C * q + j0, C * q + j1), Op.add)
+                for t in range(4):
+                    cp(A("Z", 4 * j0 + t, 4 * j1, 4, p0=32 * q, p1=32 * q + 32),
+                       A("ZP", C * q + j0, C * q + j1, p0=32 * t, p1=32 * t + 32), "SV", scale=0.5)
         for j0, j1 in CUT:
             QZ = pair("QZ", "SZ", j0, j1)
             quant(QZ, A("Z", 4 * j0, 4 * j1))
@@ -503,11 +520,11 @@ def plan(ops, deps, soft):
             for i in range(n):
                 seed = (seed * 1103515245 + 12345) % 2147483648
                 k = seed >> 8
-                if k % 40 == 0:
+                if k % 80 == 0:
                     prio[i] += (k >> 6) % 2001 - 1000
-                if k % 40 == 1:
+                if k % 80 == 1:
                     lean[i] = (k >> 6) % 2001 - 600.0
-                if k % 400 == 2:
+                if k % 800 == 2:
                     run, push = (k >> 9) % 24, ((k >> 14) % 41 - 20) * 250.0
                 if run > 0:
                     run -= 1
@@ -517,23 +534,25 @@ def plan(ops, deps, soft):
         left = [len(d) for d in deps]
         ready = [i for i in range(n) if not left[i]]
         while ready:
-            i = max(ready, key=lambda k: (prio[k], -k))
+            i = max(ready, key=lambda k: prio[k])
             ready.remove(i)
             got = None
             for k, a in enumerate(ops[i]["alts"]):
                 s = 0.0
                 for j in deps[i]:
                     s = max(s, end[j] + (0.0 if j in soft[i] and ops[j]["alts"][eng[j]][0] == a[0] else SYNC))
-                for b0, b1 in busy[a[0]]:
-                    if s + a[1] <= b0:
-                        break
-                    s = max(s, b1)
+                row = busy[a[0]]
+                at = len(row)
+                while at and row[at - 1][1] > s:
+                    at -= 1
+                while at < len(row) and s + a[1] > row[at][0]:
+                    s = max(s, row[at][1])
+                    at += 1
                 if got is None or s + a[1] + lean[i] < got[0] + got[2]:
-                    got = (s, k, a[1], a[0])
+                    got = (s, k, a[1], a[0], at)
             start[i], eng[i] = got[0], got[1]
             end[i] = got[0] + got[2] + ops[i]["lat"]
-            busy[got[3]].append((got[0], got[0] + got[2]))
-            busy[got[3]].sort()
+            busy[got[3]].insert(got[4], (got[0], got[0] + got[2]))
             for u in users[i]:
                 left[u] -= 1
                 if not left[u]:

@@ -6,54 +6,58 @@ BF, F32, I32, U16, CD, PL = "bfloat16", "float32", "int32", "uint16", "float8_e4
 SB = {
     "X0": (1280, BF), "X1": (1280, BF), "U": (512, BF), "VV": (512, BF),
     "QU": (128, CD), "SU": (128, PL), "QV": (128, CD), "SV": (128, PL),
-    "QU2": (128, CD), "SU2": (128, PL), "QUP": (416, CD), "SUP": (416, PL),
-    "WC": (512, CD), "WS": (512, PL),
-    "EB": (512, BF), "ET": (4096, BF), "QE": (1024, CD), "SE": (1024, PL),
-    "CT": (1536, BF), "QC": (384, CD), "SC": (384, PL), "ZT": (512, BF),
+    "QU2": (160, CD), "SU2": (160, PL), "QUP": (416, CD), "SUP": (416, PL),
+    "WC": (512, CD), "WS": (512, PL), "QB": (416, CD), "SB": (416, PL),
+    "EB": (512, BF), "ET": (2048, BF), "QE": (512, CD), "SE": (512, PL), "QE2": (512, CD), "SE2": (512, PL),
+    "HI": (1, F32), "I32": (32, F32), "CT": (528, BF), "QC": (132, CD), "SC": (132, PL), "ZT": (512, BF),
     "F1": (1280, BF), "QF1": (320, CD), "SF1": (320, PL), "F2": (768, BF), "QF2": (192, CD), "SF2": (192, PL),
-    "MK0": (128, BF), "MK": (320, BF), "DD": (320, BF), "SC3": (4, F32), "INN": (192, BF), "OT": (192, F32),
-    "FT": (160, F32), "PM": (160, F32), "FL": (160, BF), "KS": (160, BF), "RS": (160, F32), "KP": (160, BF),
-    "KT": (416, BF), "KG": (384, BF), "KX": (736, BF), "KO": (480, BF), "KOT": (480, BF), "KF": (48, F32),
-    "KA": (128, F32), "SQ": (128, F32), "SD": (256, F32), "SW": (256, F32), "HT": (160, F32), "LK": (8, U16), "LC": (10, U16),
-    "NI": (64, I32), "NE": (32, F32), "NF": (32, F32), "ND": (64, F32), "NT": (64, F32), "NY": (80, F32),
-    "YF": (64, F32), "PF": (64, F32), "PH": (64, F32), "T2": (40, I32), "T3": (40, I32),
-    "T4": (80, I32), "T5": (80, I32), "T6": (40, I32), "T7": (40, I32),
-    "CB": (160, F32), "CF": (160, F32), "CM": (80, F32), "CTP": (80, F32), "C1": (160, F32),
-    "C2": (80, F32), "C5": (80, I32), "C6": (80, I32),
-    "MT": (4096, F32), "MG": (640, F32), "MX": (640, F32),
-    "VW": (4096, BF), "AP": (1280, BF), "AS": (1280, BF), "ZP": (1280, BF), "Z": (1280, BF),
+    "MK0": (128, BF), "MK": (320, BF), "DD": (320, BF), "INN": (192, BF), "OT": (192, F32),
+    "FT": (96, F32), "PM": (192, F32), "FL": (192, BF), "KS": (192, BF), "KQ": (768, BF), "RS": (96, F32), "KP": (96, BF),
+    "KT": (432, BF), "KG": (192, BF), "KX": (352, BF), "KXA": (672, BF), "KF": (32, F32),
+    "KA": (112, F32), "SQ": (416, BF), "SD": (608, BF), "SW": (608, BF), "HT": (80, F32),
+    "NI": (128, I32), "NE": (64, F32), "NF": (64, F32), "ND": (32, F32),
+    "YF": (32, F32), "PF": (32, F32), "PH": (32, F32), "T2": (20, I32), "T3": (20, I32),
+    "T4": (80, I32), "T5": (80, I32), "T6": (32, I32), "T7": (32, I32), "G1": (80, I32), "G2": (80, I32),
+    "CB": (80, F32), "CF": (80, F32), "CM": (40, F32), "CTP": (72, F32), "C1": (80, F32), "CZ": (288, F32),
+    "MS": (320, F32), "MT": (4096, F32), "MG": (320, F32), "MX": (320, F32),
+    "VW": (4096, BF), "AP": (1280, BF), "AS": (1280, BF), "A2": (1280, BF), "ZP": (1280, BF), "Z": (1280, BF),
     "QZ": (320, CD), "SZ": (320, PL), "RL": (1280, F32), "YO": (320, F32),
-    "IT": (320, F32), "PT": (320, F32), "CI": (80, F32), "PC": (1, F32), "GI": (8, I32), "GJ": (8, I32), "GF": (8, F32),
-    "AB": (80, F32), "PD": (6, F32),
-    "L2": (8, U16), "LU": (26, U16), "LA": (16, U16), "LB": (6, U16), "LD": (30, U16), "LE": (4, U16), "LF": (2, U16),
-    "OK": (20, U16), "OM": (40, U16), "OA": (80, U16), "OB": (80, U16),
-    "SF": (64, F32), "SH": (32, F32), "ST": (32, F32),
+    "IT": (256, F32), "PT": (256, F32), "CI": (86, F32), "CX": (12, F32), "PC": (1, F32), "GI": (4, I32), "GJ": (4, I32),
+    "GF": (4, F32), "GK": (8, I32), "GL": (8, I32), "AB": (80, F32), "PD": (11, F32),
+    "L2": (10, U16), "LU": (26, U16), "LS": (32, U16), "LA": (38, U16), "LK": (8, U16), "LC": (6, U16), "LZ": (6, U16),
+    "LE": (2, U16), "LF": (2, U16), "LO": (2, U16), "LN": (2, U16), "LQ": (20, U16),
+    "OK": (16, U16), "OM": (20, U16), "OA": (80, U16), "OB": (80, U16),
+    "SF": (32, F32), "ST": (32, F32), "SG": (64, F32),
 }
 for _r in range(4):
     SB["QX%d" % _r] = (320, CD)
     SB["SX%d" % _r] = (320, PL)
 for _r in range(3):
-    SB["QB%d" % _r] = (96, CD)
-    SB["SB%d" % _r] = (96, PL)
-    SB["QL%d" % _r] = (224, CD)
-    SB["SL%d" % _r] = (224, PL)
-    SB["OL%d" % _r] = (6, U16)
+    SB["QL%d" % _r] = (320, CD)
+    SB["SL%d" % _r] = (320, PL)
+    SB["OL%d" % _r] = (12, U16)
+    SB["LL%d" % _r] = (12, U16)
 PART = {}
-for _pool, _names in (("TI", "T2 T3 T4 T5 T6 T7 C5 C6"), ("TF", "CF CM CTP C1 C2 CB KA")):
+for _pool, _names in (("TI", "T2 T3 T4 T5 T6 T7 G1 G2"), ("TF", "CF CM CTP C1 CB KA KF PH YF PF NE NF ND SF ST"),
+                      ("TU", "LA LK LC LZ LE LF LO LN LQ"), ("TO", "OK OM OA OB"), ("TG", "GI GJ GK GL")):
     _at = 0
     for _k in _names.split():
         PART[_k] = (_pool, _at, SB[_k][0])
-        _at += SB[_k][0]
+        _at += (SB[_k][0] + 7) // 8 * 8
         SB[_pool] = (_at, SB.pop(_k)[1])
 SCRATCH = {k: ("sbuf", [128, n], d) for k, (n, d) in SB.items()}
 SCRATCH["PL"] = ("psum", [128, 512 * 5], F32)
 SCRATCH["PV"] = ("psum", [128, 512 * 3], F32)
-SEMAPHORES = ["eV", "eS", "eP", "eG", "dx0", "dx1", "du", "dv", "dw", "dn", "da0", "da1", "da2", "da3",
-              "do0", "do2", "dc0", "dc1", "dy0", "dy1", "arr0", "arr1", "arr2", "loc0", "loc1"]
+SEMAPHORES = ["eV", "eS", "eP", "eG", "dx0", "dx1", "du", "dv", "dw", "dn", "dm", "dt", "da0", "da1", "da2", "da3",
+              "do0", "do2", "dc0", "dc1", "dy0", "dy1", "arr0", "arr1", "arr2", "col0", "col1", "col2", "loc"]
 WIDE = {BF: 2, F32: 4, I32: 4, U16: 2, CD: 4, PL: 1}
-SYNC, OVER, GATHER, PE = 165.0, 66.0, 1.55, 1.3
-TRIES, EARLY = 18000, 5000.0
+SYNC, OVER, GATHER, PE = 165.0, 66.0, 1.55, 1.1
+USE_DM, USE_DT, USE_G = False, False, False
+FIXED, PER_ROW, PER_BYTE = 1400.0, 60.0, 0.048
+TRIES, WEIGHT, HEAT = 170000, 0.2, 40.0
 CUT = ((0, 192), (192, 320))
+CHUNK = (0, 64, 192)
+ROW = 6
 Op, Fn = AluOpType, ActivationFunctionType
 
 
@@ -63,7 +67,6 @@ def rank_program(g, core, T, topo):
         return
     N = len(T.cores)
     ops = []
-    boost = [0.0]
     Q = {"V": g.vector, "S": g.scalar, "P": g.tensor, "G": g, "Y": g.sync}
 
     def lanes(k):
@@ -95,7 +98,7 @@ def rank_program(g, core, T, topo):
             kind = SB[name][1]
         view = T[name][p0:p1, c0:c1] if step == 1 else T[name][p0:p1, c0:c1:step]
         return {"ap": view, "regs": [reg], "n": len(range(c0, c1, step)), "w": WIDE[kind], "kind": kind, "ind": False,
-                "ps": name in ("PL", "PV")}
+                "ps": name in ("PL", "PV"), "p": (p0, p1)}
 
     def bank(name, b, c0, c1, step=1):
         return A(name, 512 * b + c0, 512 * b + c1, step)
@@ -103,13 +106,19 @@ def rank_program(g, core, T, topo):
     def by(win, off):
         return {"ap": win["ap"].indirect(off["ap"]), "regs": win["regs"] + off["regs"], "n": 16 * off["n"], "w": 4, "ind": True, "ps": False}
 
+    def blk(b, n=32):
+        return {"p0": n * b, "p1": n * b + n}
+
     def ap(v):
         return v["ap"] if isinstance(v, dict) else v
 
     def add(alts, reads, writes, **kw):
         o = {"alts": alts, "r": [x for v in reads if isinstance(v, dict) for x in v["regs"]],
-             "w": [x for v in writes for x in v["regs"]], "lat": 0.0, "sem": None, "inc": 1, "after": [], "boost": boost[0]}
+             "w": [x for v in writes for x in v["regs"]], "lat": 0.0, "sem": None, "inc": 1, "after": [], "free": False, "work": 0.0}
         o.update(kw)
+        o["alone"] = any(v["p"][0] for v in list(reads) + list(writes) if isinstance(v, dict) and "p" in v)
+        if o["alone"]:
+            o["alts"] = [(a[0], a[1] + SYNC * (a[0] == "G"), a[2]) for a in alts]
         ops.append(o)
         return len(ops) - 1
 
@@ -146,6 +155,8 @@ def rank_program(g, core, T, topo):
                 alts.append(("V", cv(out, in_), lambda: g.vector.tensor_copy(ap(out), ap(in_))))
             else:
                 alts.append(("V", cv(out, in_), lambda: g.vector.tensor_scalar(ap(out), ap(in_), ap(scale), None, Op.mult)))
+        if "G" in on:
+            alts.append(("G", 260 + 2.2 * out["n"], lambda: g.affine_select(ap(out), ap(in_), [[0, out["n"]]], Op.is_ge, 0.0, 0, 0)))
         return add(alts, [in_, scale], [out])
 
     def act(out, in_, fn, bias=0.0, scale=1.0):
@@ -156,17 +167,24 @@ def rank_program(g, core, T, topo):
         return add([("S", cs(out, in_), lambda: g.scalar.activation(ap(out), ap(in_), Fn.Identity, bias=ap(k))),
                     ("V", cv(out, in_), lambda: g.vector.tensor_scalar(ap(out), ap(in_), ap(k), None, Op.add))], [in_, k], [out])
 
-    def iota(out, pattern, base=0, cm=0):
+    def count(out, pattern, base=0, cm=0):
         if out["kind"] == I32:
-            f = lambda: g.iota(ap(out), pattern, base, cm)
-        else:
-            f = lambda: g.iota(ap(out), pattern, base, cm, allow_small_or_imprecise_dtypes=True)
-        return add([("G", 160 + 2 * out["n"], f)], [], [out])
+            return ("G", 200 + 2.2 * out["n"], lambda: g.iota(ap(out), pattern, base, cm))
+        return ("G", 200 + 2.2 * out["n"], lambda: g.iota(ap(out), pattern, base, cm, allow_small_or_imprecise_dtypes=True))
+
+    def iota(out, pattern, base=0, cm=0):
+        return add([count(out, pattern, base, cm)], [], [out])
 
     def fill(out, k, on="V"):
-        if on == "G":
-            return iota(out, [[0, out["n"]]], int(k))
-        return add([("V", cv(out), lambda: g.vector.memset(ap(out), k))], [], [out])
+        alts, zero = [], None
+        if "S" in on:
+            zero = A("ZT", 0, out["n"], 1, *out["p"])
+            alts.append(("S", cs(out, zero), lambda: g.scalar.activation(ap(out), ap(zero), Fn.Identity, bias=k)))
+        if "V" in on:
+            alts.append(("V", cv(out), lambda: g.vector.memset(ap(out), k)))
+        if "G" in on:
+            alts.append(count(out, [[0, out["n"]]], int(k)))
+        return add(alts, [zero], [out])
 
     def tr(out, in_):
         return add([("V", cv(out, in_), lambda: g.vector.transpose(ap(out), ap(in_)))], [in_], [out])
@@ -193,173 +211,187 @@ def rank_program(g, core, T, topo):
         add([("V", 60 + GATHER * dst[0]["n"], f)], [src[0], off], [dst[0]])
         cp(dst[1], by(src[1], off), "S")
 
-    def dma(q, sem, moves, reads, writes, lat):
+    def dma(q, sem, moves, reads, writes, rows, width):
         def f():
             for o, i in moves:
                 Q[q].dma_start(o, i).then_inc(T.sem[sem], 16)
-        return add([(q, 150.0 * len(moves), f)], reads, writes, sem=sem, inc=16 * len(moves), lat=lat)
+        return add([(q, 100.0 * len(moves), f)], reads, writes, sem=sem, inc=16 * len(moves), lat=FIXED,
+                   work=rows / 16 * (PER_ROW + PER_BYTE * width))
 
     u8 = lambda v: ap(v).bitcast(dt.uint8)
 
-    dma("Y", "dx0", [(T.X0[:, 0:768], T.x[:, 0:768])], [], [A("X0", 0, 768)], 3000.0)
-    dma("S", "du", [(T.U[:], T.u[:])], [], [A("U")], 2800.0)
-    dma("S", "dx1", [(T.X0[:, 768:1280], T.x[:, 768:1280])], [], [A("X0", 768, 1280)], 3000.0)
-    fill(A("NI"), 0)
-    dma("Y", "dn", [(T.NI[64 * u + 10 * k:64 * u + 10 * k + 10, 32 * j:32 * j + 32], src[k::2, 160 * u:160 * u + 160])
-                    for u in range(2) for k in range(2) for j, src in enumerate((T.nb, T.e))], [], [A("NI")], 2400.0)
-    dma("Y", "dw", [(u8(A("WC")), T.wc[:]), (T.WS[:], T.ws[:])], [], [A("WC"), A("WS")], 3500.0)
-    dma("Y", "dv", [(T.VV[:], T.v[:])], [], [A("VV")], 2400.0)
+    dma("Y", "dx0", [(T.X0[:, 0:768], T.x[:, 0:768])], [], [A("X0", 0, 768)], 128, 1536)
+    dma("S", "du", [(T.U[:], T.u[:])], [], [A("U")], 128, 1024)
+    dma("S", "dx1", [(T.X0[:, 768:1280], T.x[:, 768:1280])], [], [A("X0", 768, 1280)], 128, 1024)
+    fill(A("ZT"), 0.0)
+    fill(A("NI", p1=32), 0)
+    dma("Y", "dn", [(T.NI[0:20, 0:64], T.nb[:]), (T.NI[0:20, 64:128], T.e[:])], [], [A("NI", p1=32)], 40, 256)
+    dma("Y", "dw", [(u8(A("WC")), T.wc[:]), (T.WS[:], T.ws[:])], [], [A("WC"), A("WS")], 256, 1280)
+    dma("Y", "dv", [(T.VV[:], T.v[:])], [], [A("VV")], 128, 1024)
 
+    FAR = C // 16 + 1
     tabs = [([[0, 2], [1, 16]], 0),
-            ([[0, 2], [1, 8], [32, 2]], 0),
-            ([[1, 2], [2, 8], [32, 2]], 0),
             ([[0, 4], [16, 8]], 1),
             ([[0, 2], [32, 4], [0, 4]], 0),
-            ([[1, 32]], 0),
-            ([[1, 2], [2, 16]], 0),
-            ([[512, 2], [0, 16]], 0)]
+            ([[0, 8], [2, 4]], 0),
+            ([[16, 2], [0, 16]], 0),
+            ([[10, 2], [1, 16]], 0),
+            ([[1, 2], [2, 8], [10, 2]], 0)]
     col = lambda k: A("PT", 32 * k, 32 * k + 1)
+    pd = lambda k: A("PD", k, k + 1)
     fill(A("MK0"), 2.0 ** -120)
     add([("G", 200 + 256, lambda: g.affine_select(T.MK[:, 0:128], T.MK0[:], [[-1, 128]], Op.is_ge, 0.0, 0, 1))],
         [A("MK0")], [A("MK", 0, 128)])
     add([("G", 200 + 128, lambda: g.affine_select(T.MK[:, 128:192], T.MK0[:, 0:64], [[-1, 64]], Op.is_ge, 0.0, -64, 1))],
         [A("MK0")], [A("MK", 128, 192)])
-    fill(A("MK", 128, 192, p1=64), 1e29)
+    fill(A("MK", 128, 192, p1=64), 1e29, "SV")
     cp(A("MK", 192, 320), A("MK", 0, 128), "SV")
     for k, (pat, base) in enumerate(tabs):
-        boost[0] = EARLY if k in (3, 4) else 0.0
-        iota(A("IT", 32 * k, 32 * k + 32), pat, base)
-    iota(A("IT", 256, 272), [[16, 8], [352, 2]], 7)
-    iota(A("IT", 272, 288), [[16, 8], [-320, 2]], 327)
-    for h in range(2):
-        iota(A("IT", 288 + 16 * h, 304 + 16 * h), [[1, 2], [0, 4], [-40, 2]], 40)
+        if k != 3 or USE_DM:
+            iota(A("IT", 32 * k, 32 * k + 32), pat, base)
+    fill(A("IT", 47, 64, 16), 2.0, "SVG")
+    for b in range(4):
+        iota(A("IT", 224, 256, **blk(b)), [[0, 8], [2 - 4 * (b // 2), 2], [1 - 2 * (b % 2), 2]], b)
+    for t in range(3):
+        act(A("CX", 4 * t, 4 * t + 4), A("IT", 224, 228), Fn.Identity, bias=32.0 * t, scale=96.0)
     iota(A("PC"), [[0, 1]], 0, 1)
     iota(A("INN"), [[16, 6], [0, 2], [1, 16]])
-    iota(A("CI", 8, 16), [[1, 8]])
-    iota(A("CI", 16, 36), [[32, 10], [0, 2]])
-    iota(A("CI", 40, 44), [[64, 4]], -160)
-    iota(A("CI", 48, 64), [[16, 8], [0, 2]])
-    iota(A("CI", 64, 74), [[2, 10]])
-    iota(A("SQ", 0, 80), [[0, 4], [16, 20]], 7)
-    iota(A("SQ", 80, 120), [[0, 4], [16, 10]], 327)
-    fill(A("SQ", 120, 128), 0.0, "G")
-    iota(A("HT", 1, 160, 2), [[0, 20], [1024, 4]])
+    if USE_DM:
+        iota(A("CI", 0, 8), [[1, 8]])
+    iota(A("CI", 8, 12), [[192, 2], [64, 2]], -160)
+    iota(A("CI", 16, 30), [[16, 7], [112, 2]])
+    iota(A("CI", 30, 54), [[16, 12], [0, 2]], 224)
+    for a in range(2):
+        iota(A("SQ", 112 * a, 112 * a + 80), [[0, 4], [2, 10], [1 + FAR * (1 - 2 * a), 2]], FAR * a)
+        iota(A("SQ", 112 * a + 80, 112 * a + 100), [[12 - 22 * a, 2], [1, 10]], 10 * a)
+        fill(A("SQ", 112 * a + 100, 112 * a + 112), 0.0, "SVG")
+    iota(A("SQ", 224, 244), [[0, 4], [4, 5]])
+    fill(A("SQ", 244, 256), 0.0, "SVG")
+    for k in range(2):
+        iota(A("SQ", 256 + k, 336, 2), [[1, 5], [10, 2], [0, 4]], 5 - 5 * k)
+    iota(A("SQ", 336, 416), [[2, 4], [16, 5], [0, 4]], 1)
+    iota(A("HT"), [[0, 10], [1024, 4], [0, 2]])
     iota(A("AB"), [[1024, 4], [16, 20]])
-    tr(A("PT", 0, 32), A("IT", 0, 32))
-    tr(A("PT", 32, 96), A("IT", 32, 96))
-    tr(A("PT", 160, 320), A("IT", 160, 320))
-    fill(A("L2"), 2)
-    ts(A("LA"), A("CI", 48, 64), col(0), Op.add)
-    cp(A("SD"), by(A("SQ"), A("LA")), "S")
-    tr(A("SW"), A("SD"))
-    cp(A("LK"), A("SW", 0, 256, 32))
-    ts(A("LC"), A("CI", 64, 74), col(9), Op.add)
-    fill(A("HT", 0, 160, 2), 0.0)
-    plus(A("HT", 1, 160, 2), A("HT", 1, 160, 2), col(7))
-    ts(A("LB", 0, 3), A("CI", 8, 11), 8.0, Op.mult, col(1), Op.add)
-    ts(A("LB", 3, 5), A("CI", 8, 10), 16.0, Op.mult, col(2), Op.add)
-    ts(A("LD", 0, 20), A("CI", 16, 36), col(5), Op.add)
-    ts(A("PD", 4, 5), A("PC"), 64.0, Op.is_ge, 160.0, Op.mult)
-    ts(A("LD", 20, 30), A("CI", 16, 26), col(5), Op.add, A("PD", 4, 5), Op.add)
-    ts(A("LE", 0, 3), A("CI", 8, 11), 128.0, Op.mult, col(8), Op.add)
-    ts(A("LF"), A("CI", 8, 10), 32.0, Op.mult, col(6), Op.add)
-    ts(A("AB"), A("AB"), col(0), Op.add, col(7), Op.add)
-    fill(A("ZT"), 0.0)
-    fill(A("CT", 0, 512), 1.0)
-    fill(A("CT", 1, 512, 4, p1=64), 0.0)
-    fill(A("CT", 512, 1536), 0.0)
-    ts(A("PD", 0, 4), A("CI", 40, 44), A("PC"), Op.add, col(0), Op.subtract)
-    for t, k, p0 in ((0, 0, 0), (1, 1, 64), (2, 3, 0)):
-        plus(A("CT", 512 + t, 1024, 4, p0=p0), A("ZT", 0, 128, p0=p0), A("PD", k, k + 1, p0=p0))
-        plus(A("CT", 1024 + t, 1536, 4, p0=p0), A("ZT", 0, 128, p0=p0), A("PT", 0, 1, p0=p0))
-    quant(pair("QC", "SC", 0, 128), A("CT", 0, 512))
-    quant(pair("QC", "SC", 128, 384), A("CT", 512, 1536))
-    boost[0] = EARLY
-    iota(A("GI"), [[-16, 8]], 0, 1)
-    fill(A("EB"), 0.0)
+    for k0, k1 in ((0, 2), (2, 3 + USE_DM), (4, 8)):
+        tr(A("PT", 32 * k0, 32 * k1), A("IT", 32 * k0, 32 * k1))
+    fill(A("L2", 2, 10), 2)
+    ts(A("LA"), A("CI", 16, 54), col(0), Op.add)
+    for k0, k1 in ((0, 9), (9, 19)):
+        cp(A("SD", 32 * k0, 32 * k1), by(A("SQ"), A("LA", 2 * k0, 2 * k1)), "S")
+        tr(A("SW", 32 * k0, 32 * k1), A("SD", 32 * k0, 32 * k1))
+    turned = lambda k0, k1: A("SW", 32 * k0, 32 * k1, 32)
+    tt(pd(0), A("IT", 225, 226), A("IT", 224, 225), Op.subtract)
+    act(pd(1), col(4), Fn.Identity, bias=-8.0 * FAR, scale=float(FAR))
+    act(pd(2), A("IT", 224, 225), Fn.Identity, bias=8.0 * FAR + ROW, scale=16.0)
+    act(pd(3), pd(0), Fn.Identity, bias=pd(2), scale=pd(1))
+    act(pd(4), col(7), Fn.Copy, scale=72.0)
+    act(pd(6), col(4), Fn.Copy, scale=160.0)
+    ts(A("LK", 0, 5), turned(0, 5), 16.0, Op.mult, float(ROW), Op.add)
+    ts(A("LE"), turned(5, 7), 16.0, Op.mult, float(ROW), Op.add)
+    ts(A("LK", 5, 7), turned(7, 9), 16.0, Op.mult, pd(3), Op.add)
+    cp(A("LC", 0, 5), turned(9, 14))
+    ts(A("LZ", 0, 5), turned(14, 19), pd(4), Op.add)
+    for a in range(2):
+        ts(A("LQ", a, 8, 2), A("CX", 0, 4), col(0), Op.add, 16.0 * a, Op.add)
+        ts(A("LQ", 8 + a, 20, 2), A("CX", 6, 12), col(0), Op.add, 16.0 * a, Op.add)
+    plus(A("HT"), A("HT"), pd(6))
+    ts(A("AB"), A("AB"), col(0), Op.add, pd(6), Op.add)
+    cp(A("LF"), A("PT", 160, 162))
+    cp(A("LO"), A("PT", 192, 194))
+    ts(A("LN"), A("IT", 224, 229, 4), 16.0, Op.mult, col(0), Op.add)
+    fill(A("CT"), 0.0)
+    plus(pd(5), col(4), -192.0)
+    ts(A("PD", 8, 11), A("CI", 8, 11), A("PC"), Op.add, col(0), Op.subtract)
+    for t in range(3):
+        plus(A("CT", t, 512, 128), A("ZT", 0, 4), pd(8 + t))
+        plus(A("CT", 4 + t, 512, 128), A("CX", 4 * t, 4 * t + 4), pd(5))
+        for k in (8, 12):
+            plus(A("CT", k + t, 512, 128), A("ZT", 0, 4), col(0))
+    fill(A("CT", 16, 20), 1.0, "SV")
+    fill(A("CT", 1, 512, 4, p1=64), 0.0, "SV")
+    quant(pair("QC", "SC", 0, 132), A("CT"))
+    for u in range(2):
+        iota(A("GI", **blk(u, 64)), [[-16, 4]], 0, 1)
+        fill(A("HI", **blk(u, 64)), 16.0 * u)
+    iota(A("I32"), [[1, 32]])
+    iota(A("CI", 54, 86), [[32, 16], [-16, 2]], 16)
+    plus(A("HI"), A("HI"), col(0))
+    fill(A("EB"), 0.0, "SV")
     for t in range(4):
-        ts(A("EB", 129 * t, 128 * t + 128, 4), A("IT", 0, 32), col(0), Op.is_equal)
+        ts(A("EB", 129 * t, 128 * t + 128, 4), A("I32"), A("HI"), Op.is_equal)
     ts(A("GJ"), A("GI"), 4, Op.arith_shift_right)
     ts(A("GF"), A("GJ"), 0.0, Op.is_equal)
-    for f in range(8):
+    for f in range(4):
         cp(A("ET", 512 * f, 512 * f + 512), A("EB"), "SV", scale=A("GF", f, f + 1))
-    for k in range(4):
+    for k in range(2):
         quant(pair("QE", "SE", 256 * k, 256 * k + 256), A("ET", 1024 * k, 1024 * k + 1024))
-    tr(A("PT", 96, 160), A("IT", 96, 160))
-    cp(A("LU", 0, 8), A("PT", 96, 104))
-    cp(A("LU", 8, 17), A("PT", 128, 137))
-    ts(A("LU", 17, 26), A("PT", 128, 137), 16.0, Op.add)
-    boost[0] = 0.0
-    for r in range(3):
-        quant(pair("QL%d" % r, "SL%d" % r, 96, 224), A("ZT"))
-    fill(A("RS"), 0.0, "G")
-    fill(A("RS", 0, 160, 32), -1e29)
-    fill(A("KP"), 1.0, "G")
-    fill(A("KP", 0, 160, 32), 0.0)
-    fill(A("FL", 88, 160), 0.0, "G")
-    fill(A("KG", 16, 32), 0.0, "G")
-    fill(A("KG", 352, 368), 0.0, "G")
-    fill(A("KX", 672, 736), 0.0, "G")
-    fill(A("F1", 0, 512, 4), 0.0)
-    fill(A("F1", 513, 768, 4), 0.0)
-    fill(A("F1", 770, 1280, 4), 0.0)
-    fill(A("F2", 3, 768, 4), 0.0)
-    fill(A("CF", 0, 160, 2), 0.0)
-    fill(A("CTP", 0, 80, 2), 0.0)
-    fill(A("PF", 40, 64), 0.0, "G")
-    fill(A("SF", 40, 64), 0.0, "G")
+    ts(A("LS"), A("CI", 54, 86), col(0), Op.add)
+    pick(pair("QE2", "SE2", 0, 512), pair("QE", "SE", 0, 512), A("LS"))
+    cp(A("L2", 0, 2), A("PT", 32, 34))
+    cp(A("LU", 0, 9), A("PT", 64, 73))
+    ts(A("LU", 9, 18), A("PT", 64, 73), 16.0, Op.add)
+    if USE_DM:
+        ts(A("GK"), A("CI", 0, 8), col(3), Op.add)
+        ts(A("GL"), A("GK"), 7, Op.bitwise_and)
+        ts(A("LU", 18, 26), A("GL"), 16.0, Op.mult)
+    quant(pair("QB", "SB", 288, 416), A("ZT"))
+    fill(A("RS"), 0.0, "SVG")
+    fill(A("RS", 0, 96, 16), -1e29, "SV")
+    fill(A("KP"), 1.0, "SVG")
+    fill(A("KP", 0, 96, 16), 0.0, "SVG")
+    for name, c0, c1, step in (("FL", 88, 96, 1), ("FL", 184, 192, 1), ("KT", 0, 16, 1), ("KT", 336, 352, 1), ("KG", 0, 16, 1),
+                               ("KG", 176, 192, 1), ("F1", 0, 512, 4), ("F1", 513, 768, 4), ("F1", 770, 1280, 4), ("F2", 3, 768, 4),
+                               ("CF", 0, 80, 2), ("CTP", 0, 72, 2)):
+        fill(A(name, c0, c1, step), 0.0, "SVG")
+    for h in range(3 * USE_DT):
+        fill(A("VW", 512 * h + C, 512 * h + 512), 0.0, "SVG")
     quant(pair("QU", "SU", 0, 128), A("U"))
-    pick(pair("QU2", "SU2", 0, 128), pair("QU", "SU", 0, 128), A("L2"))
-    boost[0] = EARLY
-    pick(pair("QUP", "SUP", 0, 128), pair("QU", "SU", 0, 128), A("LU", 0, 8))
-    pick(pair("QUP", "SUP", 128, 416), pair("QU", "SU", 0, 128), A("LU", 8, 26))
-    boost[0] = 0.0
+    pick(pair("QU2", "SU2", 0, 160), pair("QU", "SU", 0, 128), A("L2"))
+    pick(pair("QUP", "SUP", 0, 288), pair("QU", "SU", 0, 128), A("LU", 0, 18))
+    if USE_DM:
+        pick(pair("QUP", "SUP", 288, 416), pair("QU", "SU", 0, 128), A("LU", 18, 26))
     quant(pair("QV", "SV", 0, 128), A("VV"))
-    U2, UF = pair("QU2", "SU2", 0, 128), pair("QUP", "SUP", 0, 128)
-    UM = [pair("QUP", "SUP", 128 + 144 * (h % 2) + 4 * (h // 2), 256 + 144 * (h % 2) + 4 * (h // 2)) for h in range(8)]
-    EF = [pair("QE", "SE", 128 * f, 128 * f + 128) for f in range(8)]
-    ts(A("NE"), A("NI", 32, 64), 512.0, Op.mult)
-    for q in range(4):
-        s0 = 64 * (q // 2)
-        tt(A("NF", p0=32 * q, p1=32 * q + 32), A("NE", p0=s0, p1=s0 + 32), A("NI", 0, 32, p0=s0, p1=s0 + 32), Op.add)
-    cp(A("ND"), by(A("NF"), A("LA", 0, 4)), "S")
-    tr(A("NT"), A("ND"))
-    cp(A("NY"), by(A("NT"), A("LB", 0, 5)), "S")
-    cp(A("YF", 0, 40), A("NY", 0, 40), "S")
-    cp(A("T6", 0, 20), A("NY", 48, 68))
-    ts(A("T7", 0, 20), A("T6", 0, 20), 511, Op.bitwise_and)
-    cp(A("OK"), A("T7", 0, 20))
+    U2, UF, UA = pair("QU2", "SU2", 32, 160), pair("QU2", "SU2", 0, 128), pair("QUP", "SUP", 288, 416)
+    UM = [pair("QUP", "SUP", 144 * (h % 2) + 4 * (h // 2), 128 + 144 * (h % 2) + 4 * (h // 2)) for h in range(8)]
+    EF = [pair("QE" + k, "SE" + k, 128 * f, 128 * f + 128) for k in ("", "2") for f in range(4)]
+    ts(A("NE", p1=32), A("NI", 64, 128, p1=32), 512.0, Op.mult)
+    tt(A("NF", p1=32), A("NE", p1=32), A("NI", 0, 64, p1=32), Op.add)
+    cp(A("NF", p0=32, p1=64), A("NF", p1=32), "SV")
+    cp(A("NF", p0=64), A("NF", p1=64), "SV")
+    cp(A("ND"), by(A("NF"), A("LN")), "SV")
+    tr(A("YF"), A("ND"))
+    cp(A("T6", 0, 16), by(A("YF"), A("LO", 0, 1)))
+    ts(A("T7", 0, 16), A("T6", 0, 16), 511, Op.bitwise_and)
+    cp(A("OK"), A("T7", 0, 16))
 
     for j0, j1 in CUT:
         quant(pair("QX0", "SX0", j0, j1), A("X0", 4 * j0, 4 * j1))
     turn = {"l": 0, "v": 0}
 
-    def frames(src, n, c0, b):
-        mm(bank("PL", b, 0, max(n, 128)), (UF, src))
-        split = n == C
-        if split:
-            n = C // 2
-            for u in range(2):
-                tr(A("FT", p0=64 * u, p1=64 * u + 64), A("PL", 512 * b + n * u, 512 * b + n * u + n, p0=64 * u, p1=64 * u + 64))
+    def scores(q, s, t, k, b):
+        mm(bank("PL", b, 0, 128), (pair(q, s, CHUNK[t], CHUNK[t] + 128), UF))
+        if k:
+            scan(A("PM", 96 + 32 * t, 128 + 32 * t), A("RS", 0, 32), bank("PL", b, 0, 32), 0.0, Op.add, Op.max)
         else:
-            tr(A("FT", 0, n), bank("PL", b, 0, n))
-        scan(A("PM", 0, n), A("RS", 0, n), A("FT", 0, n), 0.0, Op.add, Op.max)
-        tt(A("FL", 0, n - 8), A("PM", 0, n - 8), A("PM", 8, n), Op.is_lt)
-        scan(A("KS", 0, n), A("KP", 0, n), A("FL", 0, n), 0.0, Op.mult, Op.add)
-        if split:
-            for u in range(2):
-                for w in range(2):
-                    tr(A("KT", n * u, n * u + n, p0=64 * w, p1=64 * w + 64), A("KS", p0=64 * u, p1=64 * u + 64))
-        else:
-            tr(A("KT", c0, c0 + n), A("KS", 0, n))
+            cp(A("FT", 32 * t, 32 * t + 32), bank("PL", b, 0, 32), "SV")
 
-    def tables(src, n, c0, marks, values):
-        for h in range(8):
+    def frames(k):
+        a, z = 96 * k, 384 * k
+        tt(A("FL", a, a + 88), A("PM", a, a + 88), A("PM", a + 8, a + 96), Op.is_lt)
+        scan(A("KS", a, a + 96), A("KP"), A("FL", a, a + 96), 0.0, Op.mult, Op.add)
+        tr(A("KQ", z, z + 96), A("KS", a, a + 96))
+        for b in range(4):
+            cp(A("KQ", z + 96, z + 192, **blk(b ^ 1)), A("KQ", z, z + 96, **blk(b)), "SV")
+        for u in range(2):
+            cp(A("KQ", z + 192, z + 384, **blk(1 - u, 64)), A("KQ", z, z + 192, **blk(u, 64)), "SV")
+
+    def tables(src, n, c0, marks, values, slots=8, first=0):
+        for h in range(first, slots):
             if values:
                 b = turn["v"] % 3
                 turn["v"] += 1
                 mm(bank("PV", b, 0, max(n, 128)), (EF[h], src))
-                cp(A("VW", 512 * h + c0, 512 * h + c0 + n), bank("PV", b, 0, n), values)
+                cp(A("VW", 512 * h + c0, 512 * h + c0 + n), bank("PV", b, 0, n), values, scale=0.5 if USE_G else None)
             if marks:
                 b = 1 + turn["l"] % 4
                 turn["l"] += 1
@@ -367,108 +399,128 @@ def rank_program(g, core, T, topo):
                 cp(A("MT", 512 * h + c0, 512 * h + c0 + n), bank("PL", b, 0, n), marks)
 
     for r, d in enumerate(STEP):
-        qx, sx = "QX%d" % r, "SX%d" % r
+        qx, sx, ql, sl = "QX%d" % r, "SX%d" % r, "QL%d" % r, "SL%d" % r
         X = pair(qx, sx, 0, C)
-        chunk = (0, 64, 192)
+        dst = T.cores[(rank - d) % N]
+
+        def send(out, in_, sem, view=ap, dst=dst):
+            rid, pid = topo.addr(dst)[:2]
+            f = lambda: g.remote_dma(view(out), view(in_), T.sem[sem], T.sem["loc"], pid, rid, lanes(rank)[0])
+            return add([("G", 350.0, f)], [in_], [], sem="loc", inc=lanes(rank)[1], lat=FIXED + 300, free=True,
+                       work=16 * (PER_ROW + 1.3 * PER_BYTE * in_["n"] * in_["w"]))
+
+        def landed(sem, writes, sent):
+            add([("R", 0.0, None)], [], writes, sem=sem, inc=len(sent) * lanes((rank + d) % N)[1], lat=2000.0 if sem == "col0" else 300.0, after=sent)
+        sent = [send(A(ql, j0, j1), A(qx, j0, j1), "col%d" % r, u8) for j0, j1 in (CUT if r else ((0, C),))]
+        landed("col%d" % r, [A(ql), A(sl)], sent + [send(A(sl), A(sx), "col%d" % r)])
         XA, XB = pair(qx, sx, 0, 192), pair(qx, sx, 192, C)
-        sc = lambda t: A("SC3", t, t + 1)
+        sc = lambda t: A("FT", 32 * t + 15, 32 * t + 16)
         for t in (0, 1):
-            mm(bank("PL", 2 + t, 0, 128), (pair(qx, sx, chunk[t], chunk[t] + 128), U2))
+            scores(qx, sx, t, 0, 2 + t)
         mm(bank("PL", 1, 0, 192), (U2, XA))
         mm(bank("PL", 0, 0, 192), (U2, XA))
-        cp(A("SC3", 0, 2), A("PL", 1024, 1537, 512), "SV")
         act(A("DD", 0, 128), bank("PL", 1, 0, 128), Fn.Identity, bias=sc(0), scale=-1.0)
         act(A("DD", 128, 192), bank("PL", 1, 128, 192), Fn.Identity, bias=sc(1), scale=-1.0)
         ts(A("F1", 512, 768, 4), bank("PL", 0, 128, 192), sc(0), Op.is_le)
         ts(A("F1", 1, 512, 4), bank("PL", 0, 0, 128), sc(1), Op.is_lt)
         tt(A("F1", 3, 768, 4), A("DD", 0, 192), A("MK", 0, 192), Op.is_ge)
-        mm(bank("PL", 4, 0, 128), (XB, U2))
+        scores(qx, sx, 2, 0, 4)
         mm(bank("PL", 2, 0, 128), (U2, XB))
-        ts(A("DD", 192, C), bank("PL", 2, 0, 128), bank("PL", 4, 0, 1), Op.subtract, -1.0, Op.mult)
-        ts(A("F1", 2, 768, 4), bank("PL", 0, 0, 192), bank("PL", 4, 0, 1), Op.is_lt)
+        mm(bank("PL", 3, 0, 128), (U2, XB))
+        act(A("DD", 192, C), bank("PL", 3, 0, 128), Fn.Identity, bias=sc(2), scale=-1.0)
         for t in (0, 1):
             ts(A("F1", 768 + t, 1280, 4), bank("PL", 2, 0, 128), sc(t), Op.is_le)
+        ts(A("F1", 2, 768, 4), bank("PL", 0, 0, 192), sc(2), Op.is_lt)
         tt(A("F1", 771, 1280, 4), A("DD", 192, C), A("MK", 192, C), Op.is_ge)
         for j0, j1 in CUT:
             quant(pair("QF1", "SF1", j0, j1), A("F1", 4 * j0, 4 * j1))
         for t in range(3):
-            mm(bank("PL", 2 + t, 0, 128), (pair("QF1", "SF1", chunk[t], chunk[t] + 128), pair("QC", "SC", 0, 128)))
+            mm(bank("PL", 2 + t, 0, 128), (pair("QF1", "SF1", CHUNK[t], CHUNK[t] + 128), pair("QC", "SC", 4, 132)))
             ts(A("F2", t, 768, 4), A("INN"), bank("PL", 2 + t, 0, 1), Op.is_equal)
         quant(pair("QF2", "SF2", 0, 192), A("F2"))
         f2 = pair("QF2", "SF2", 0, 192)
-        mm(bank("PL", 0, 0, 192), (pair("QC", "SC", 128, 256), f2), (pair("QC", "SC", 256, 384), f2))
+        mm(bank("PL", 0, 0, 192), (pair("QC", "SC", 0, 128), f2), (pair("QC", "SC", 2, 130), f2))
         tr(A("OT"), bank("PL", 0, 0, 192))
-        ol = A("OL%d" % r)
-        ts(ol, A("OT", 0, 192, 32), 160.0, Op.add)
-        B = pair("QB%d" % r, "SB%d" % r, 0, H)
-        pick(B, X, ol)
-        dst = T.cores[(rank - d) % N]
-        L = pair("QL%d" % r, "SL%d" % r, 0, H)
-
-        def send(out, in_, sem, dst=dst, r=r):
-            rid, pid = topo.addr(dst)[:2]
-            return lambda: g.remote_dma(out, in_, T.sem["arr%d" % r], T.sem[sem], pid, rid, lanes(rank)[0])
-        sent = [add([("G", 200.0, send(ap(L[1]), ap(B[1]), "loc0"))], [B[1]], [], sem="loc0", inc=lanes(rank)[1], lat=2000.0),
-                add([("G", 200.0, send(u8(L[0]), u8(B[0]), "loc1"))], [B[0]], [], sem="loc1", inc=lanes(rank)[1], lat=2200.0)]
-        add([("R", 0.0, None)], [], [L[0], L[1]], sem="arr%d" % r, inc=2 * lanes((rank + d) % N)[1],
-            lat=2600.0 if r == 0 else 900.0, after=sent)
-        frames(X, C, 0, 1)
-        boost[0] = 3000.0 if r else 0.0
-        tables(XA, 192, 0, None, "S")
-        boost[0] = 0.0
-        tables(XB, 128, 192, None, "SV")
-        tables(X, C, 0, "SV", None)
-        cp(A("KO"), by(A("KT", 0, C), A("LD")), "S", scale=512.0)
-        tr(A("KOT"), A("KO"))
-        cp(A("KA"), by(A("KOT"), A("LK")), "SV")
+        ol, ll = "OL%d" % r, "LL%d" % r
+        ts(A(ol, 0, 6), A("OT", 0, 192, 32), 160.0, Op.add)
+        ts(A(ol, 6, 12), A("OT", 1, 192, 32), 192.0, Op.add)
+        landed("arr%d" % r, [A(ll)], [send(A(ll), A(ol), "arr%d" % r)])
+        if r and USE_DM:
+            mm(bank("PL", 1, 0, C), (UA, X))
+            cp(A("MS"), bank("PL", 1, 0, C), "SV")
+            dma("Y", "dm", [(T.MT[64 * k:64 * k + 64:4, 512 * h:512 * h + C], T.MS[16 * h:16 * h + 16, :]) for h in range(8) for k in range(2)],
+                [A("MS")], [A("MT", 512 * h, 512 * h + C) for h in range(8)], 256, 1280)
+        else:
+            tables(X, C, 0, "SV", None)
+        scan(A("PM", 0, 96), A("RS"), A("FT"), 0.0, Op.add, Op.max)
+        frames(0)
+        cp(A("KT", 16, 16 + C), by(A("KQ", 0, 384), A("LQ")), "SV")
+        tables(XA, 192, 0, None, "SV", 4)
+        tables(XB, 128, 192, None, "SV", 4)
+        if USE_DT:
+            dma("Y", "dt", [(T.VW[16 * k:16 * k + 16, 2048:3904], T.VW[16 * (k ^ 1):16 * (k ^ 1) + 16, 0:1856]) for k in range(8)],
+                [A("VW", 0, 1856)], [A("VW", 2048, 3904)], 128, 3712)
+        else:
+            tables(X, C, 0, None, "SV", 8, 4)
+        tr(A("KXA", 0, C), A("KT", 16, 16 + C))
+        tr(A("KXA", C, C + 352), A("KT", 0, 352))
+        cp(A("KA"), by(A("KXA"), A("LK", 0, 7)), "SV", scale=512.0)
         tt(A("T4"), A("AB"), A("KA", 0, 80), Op.add)
         ts(A("T5"), A("T4"), 4095, Op.bitwise_and)
         cp(A("OA"), A("T5"))
         for q in range(4):
             cp(A("AP", C * q, C * q + C), by(A("VW"), A("OA", 20 * q, 20 * q + 20)), "SV")
-            dma("Y", "da%d" % q, [(T.AS[32 * q:32 * q + 32, C * t:C * t + C], T.AP[32 * t:32 * t + 32, C * q:C * q + C])
-                                  for t in range(4)], [A("AP", C * q, C * q + C)], [A("AS", p0=32 * q, p1=32 * q + 32)], 3200.0)
-        tt(A("PF", 0, 40), A("YF", 0, 40), A("KA", 80, 120), Op.subtract)
-        cp(A("PH", 0, 32), by(A("PF"), A("LF")), "SV")
-        plus(A("PH", 32, 64), A("PH", 0, 32), 512.0)
-        LL = pair("QL%d" % r, "SL%d" % r, 0, 128)
-        frames(LL, H, C, 0)
-        tables(LL, H, C, "SV", None)
-        tables(LL, H, C, None, "SV")
-        cp(A("KG", 32, 224), by(A("KT"), A("OK", 0, 12)), "V", scale=512.0)
-        cp(A("KG", 224, 352), by(A("KT"), A("OK", 12, 20)), "SV", scale=512.0)
-        tr(A("KX", 0, 320), A("KG", 32, 352))
+            a2 = "A2" if USE_G else "AP"
+            if USE_G:
+                cp(A("A2", C * q, C * q + C), A("AP", C * q, C * q + C), "SV", scale=2.0)
+            dma("Y", "da%d" % q, [(T.AS[32 * q:32 * q + 32, C * t:C * t + C], T[a2][32 * t:32 * t + 32, C * q:C * q + C])
+                                  for t in range(4)], [A(a2, C * q, C * q + C)], [A("AS", **blk(q))], 128, 640)
+        tt(A("PF"), A("YF"), A("KA", 80, 112), Op.subtract)
+        cp(A("PH", 0, 16), by(A("PF"), A("LF", 0, 1)), "SV")
+        plus(A("PH", 16, 32), A("PH", 0, 16), 512.0)
+        for t in range(3):
+            scores(ql, sl, t, 1, 2 + t)
+        frames(1)
+        cp(A("KT", 16 + C, 16 + E), by(A("KQ", 384, 768), A(ll, 6, 12)), "SV")
+        at = H * (2 - r)
+        pick(pair("QB", "SB", at, at + H), pair(ql, sl, 0, C), A(ll, 0, 6))
+        tables(pair("QB", "SB", at, at + 128), H, C, "SV", None)
+        tables(pair("QB", "SB", at, at + 128), H, C, None, "SV")
+        cp(A("KG", 16, 112), by(A("KT", 16, 16 + E), A("OK", 0, 6)), "V", scale=512.0)
+        cp(A("KG", 112, 176), by(A("KT", 16, 16 + E), A("OK", 6, 10)), "SV", scale=512.0)
+        tr(A("KX", 0, 160), A("KG", 16, 176))
         for h in range(2):
-            tt(A("T2", h, 40, 2), A("PH", 32 * h, 32 * h + 20), A("KX", 7, 320, 16), Op.add)
+            tt(A("T2", h, 20, 2), A("PH", 16 * h, 16 * h + 10), A("KX", ROW, 160, 16), Op.add)
         ts(A("T3"), A("T2"), 4095, Op.bitwise_and)
         cp(A("OM"), A("T3"))
-        tr(A("KX", 320, 672), A("KG", 16, 368))
-        cp(A("KF"), by(A("KX"), A("LE", 0, 3)), "SV")
-        tt(A("YF", 0, 40), A("PF", 0, 40), A("KF", 0, 40), Op.add)
-        tt(A("YF", 40, 60), A("YF", 20, 40), A("YF", 0, 20), Op.subtract)
-        tt(A("CB"), by(A("YF", 0, 60), A("LC")), A("HT"), Op.add)
+        tr(A("KX", 160, 352), A("KG"))
+        cp(A("KF"), by(A("KX"), A("LE")), "SV")
+        tt(A("YF"), A("PF"), A("KF"), Op.add)
+        tt(A("G1"), by(A("YF"), A("LC", 0, 5)), A("HT"), Op.add)
+        ts(A("G2"), A("G1"), 4095, Op.bitwise_and)
+        tt(A("CB", 0, 80, 2), A("G2", 0, 80, 2), A("G2", 1, 80, 2), Op.subtract)
+        cp(A("CB", 1, 80, 2), A("G2", 1, 80, 2))
         for q in range(2):
-            cp(A("MG", C * q, C * q + C), by(A("MT"), A("OM", 20 * q, 20 * q + 20)), "SV")
-            tr(A("MX", C * q, C * q + C), A("MG", C * q, C * q + C))
-        tt(A("CF", 1, 160, 2), A("MX", 320, 640, 4), A("MX", 0, 320, 4), Op.is_gt)
-        tt(A("CM"), A("MX", 320, 640, 4), A("MX", 0, 320, 4), Op.max)
+            cp(A("MG", 160 * q, 160 * q + 160), by(A("MT"), A("OM", 10 * q, 10 * q + 10)), "SV")
+            tr(A("MX", 160 * q, 160 * q + 160), A("MG", 160 * q, 160 * q + 160))
+        tt(A("CF", 1, 80, 2), A("MX", 160, 320, 4), A("MX", 0, 160, 4), Op.is_gt)
+        tt(A("CM"), A("MX", 160, 320, 4), A("MX", 0, 160, 4), Op.max)
         scan(A("C1"), A("CF"), A("CB"), 0.0, Op.mult, Op.add)
-        tt(A("CTP", 1, 80, 2), A("CM", 40, 80), A("CM", 0, 40), Op.is_gt)
-        tt(A("C1", 0, 80, 2), A("C1", 81, 160, 2), A("C1", 1, 80, 2), Op.subtract)
-        scan(A("C2"), A("CTP"), A("C1", 0, 80), 0.0, Op.mult, Op.add)
+        tt(A("CTP", 1, 72, 2), A("CM", 4, 40), A("CM", 0, 36), Op.is_gt)
+        tt(A("C1", 0, 72, 2), A("C1", 9, 80, 2), A("C1", 1, 72, 2), Op.subtract)
+        scan(A("CZ", 0, 72), A("CTP"), A("C1", 0, 72), 0.0, Op.mult, Op.add)
+        for b in range(4):
+            cp(A("CZ", 72, 144, **blk(b ^ 1)), A("CZ", 0, 72, **blk(b)), "SV")
         for u in range(2):
-            for w in range(2):
-                cp(A("C5", 40 * u, 40 * u + 40, p0=64 * w, p1=64 * w + 64), A("C2", 1, 80, 2, p0=64 * u, p1=64 * u + 64))
-        ts(A("C6"), A("C5"), 4095, Op.bitwise_and)
-        for q in range(4):
-            cp(A("OB", 20 * q, 20 * q + 20), A("C6", q, 80, 4))
+            cp(A("CZ", 144, 288, **blk(1 - u, 64)), A("CZ", 0, 144, **blk(u, 64)), "SV")
+        cp(A("OB"), by(A("CZ"), A("LZ", 0, 5)))
         for q in range(4):
             for j0, j1 in (CUT if q >= 2 else ((0, C),)):
                 tt(A("ZP", C * q + j0, C * q + j1), by(A("VW"), A("OB", 20 * q + j0 // 16, 20 * q + j1 // 16)),
                    A("AP", C * q + j0, C * q + j1), Op.add)
                 for t in range(4):
-                    cp(A("Z", 4 * j0 + t, 4 * j1, 4, p0=32 * q, p1=32 * q + 32),
-                       A("ZP", C * q + j0, C * q + j1, p0=32 * t, p1=32 * t + 32), "SV", scale=0.5)
+                    cp(A("Z", 4 * j0 + t, 4 * j1, 4, **blk(q)), A("ZP", C * q + j0, C * q + j1, **blk(t)),
+                       "SVG" if USE_G else "SV", scale=None if USE_G else 0.5)
         for j0, j1 in CUT:
             QZ = pair("QZ", "SZ", j0, j1)
             quant(QZ, A("Z", 4 * j0, 4 * j1))
@@ -480,21 +532,21 @@ def rank_program(g, core, T, topo):
                 tt(A("X1", 4 * j0 + t, 4 * j1, 4), A("RL", C * t + j0, C * t + j1), A("AS", C * t + j0, C * t + j1), Op.add)
             quant(pair("QX%d" % (r + 1), "SX%d" % (r + 1), j0, j1), A("X1", 4 * j0, 4 * j1))
 
-    cp(A("T6"), A("YF", 0, 40))
+    cp(A("T6"), A("YF"))
     ts(A("T7"), A("T6"), 9, Op.arith_shift_right, 7, Op.bitwise_and)
-    cp(A("SF", 0, 40), A("T7"))
-    cp(A("SH"), by(A("SF"), A("LF")), "S")
-    tr(A("ST"), A("SH"))
-    dma("Y", "do0", [(T.oe[k::2, 160 * u:160 * u + 160], T.ST[64 * u + 10 * k:64 * u + 10 * k + 10, :]) for u in range(2) for k in range(2)],
-        [A("ST")], [], 2000.0)
+    cp(A("SF"), A("T7"))
+    tr(A("ST"), A("SF"))
+    for b in range(4):
+        cp(A("SG", 16 * b, 16 * b + 16, p1=32), A("ST", 0, 16, **blk(b)), "SV")
+    dma("Y", "do0", [(T.oe[:], T.SG[0:20, :])], [A("SG", p1=32)], [], 20, 256)
     for k, (j0, j1) in enumerate(CUT):
         b = turn["v"] % 3
         turn["v"] += 1
         mm(bank("PV", b, 0, j1 - j0), (pair("QV", "SV", 0, 128), pair("QX3", "SX3", j0, j1)))
         cp(A("YO", j0, j1), bank("PV", b, 0, j1 - j0), "SV")
-        dma("Y", "dc%d" % k, [(T.oc[:, 4 * j0:4 * j1], u8(A("QX3", j0, j1)))], [A("QX3", j0, j1)], [], 2200.0 + 2 * (j1 - j0))
-        dma("SY"[k], "dy%d" % k, [(T.y[:, j0:j1], T.YO[:, j0:j1])], [A("YO", j0, j1)], [], 2200.0 + 2 * (j1 - j0))
-    dma("S", "do2", [(T.osc[4 * k:4 * k + 4, :], T.SX3[32 * k:32 * k + 4, :]) for k in range(4)], [A("SX3")], [], 2000.0)
+        dma("Y", "dc%d" % k, [(T.oc[:, 4 * j0:4 * j1], u8(A("QX3", j0, j1)))], [A("QX3", j0, j1)], [], 128, 4 * (j1 - j0))
+        dma("SY"[k], "dy%d" % k, [(T.y[:, j0:j1], T.YO[:, j0:j1])], [A("YO", j0, j1)], [], 128, 4 * (j1 - j0))
+    dma("S", "do2", [(T.osc[4 * k:4 * k + 4, :], T.SX3[32 * k:32 * k + 4, :]) for k in range(4)], [A("SX3")], [], 16, 320)
 
     emit(g, T, Q, ops)
 
@@ -504,63 +556,173 @@ PLAN = {}
 
 def plan(ops, deps, soft):
     n = len(ops)
-    level = [0.0] * n
     users = [[] for _ in range(n)]
+    level = [0.0] * n
     for i in range(n - 1, -1, -1):
-        level[i] += min(a[1] for a in ops[i]["alts"]) + ops[i]["lat"] + SYNC
+        level[i] += min(a[1] for a in ops[i]["alts"]) + ops[i]["lat"] + ops[i]["work"] + SYNC
         for j in deps[i]:
             level[j] = max(level[j], level[i])
             users[j].append(i)
-    best, seed = None, 12345
-    base, tilt = [level[i] + ops[i]["boost"] for i in range(n)], [400.0] * n
-    for trial in range(TRIES):
-        prio, lean = list(base), list(tilt)
-        if trial:
-            run, push = 0, 0.0
-            for i in range(n):
-                seed = (seed * 1103515245 + 12345) % 2147483648
-                k = seed >> 8
-                if k % 80 == 0:
-                    prio[i] += (k >> 6) % 2001 - 1000
-                if k % 80 == 1:
-                    lean[i] = (k >> 6) % 2001 - 600.0
-                if k % 800 == 2:
-                    run, push = (k >> 9) % 24, ((k >> 14) % 41 - 20) * 250.0
-                if run > 0:
-                    run -= 1
-                    prio[i] += push
-        busy = {q: [] for q in "VSPGYR"}
-        start, end, eng = [0.0] * n, [0.0] * n, [0] * n
-        left = [len(d) for d in deps]
-        ready = [i for i in range(n) if not left[i]]
-        while ready:
-            i = max(ready, key=lambda k: prio[k])
-            ready.remove(i)
+    que = [["VSPGYR".index(a[0]) for a in o["alts"]] for o in ops]
+    cost = [[a[1] for a in o["alts"]] for o in ops]
+    lat, work = [o["lat"] for o in ops], [o["work"] for o in ops]
+    hard = [[j for j in deps[i] if j not in soft[i]] for i in range(n)]
+    easy = [sorted(soft[i]) for i in range(n)]
+    eng = [0] * n
+    start, end, why = [0.0] * n, [0.0] * n, [-1] * n
+    seed = [12345]
+
+    def draw(k):
+        seed[0] = (seed[0] * 6364136223846793005 + 1442695040888963407) % 2 ** 64
+        return (seed[0] >> 33) % k
+
+    def run(order, first):
+        free, last, seen = [0.0] * 7, [-1] * 7, 0
+        k = first - 1
+        while k >= 0 and seen < 6:
+            i = order[k]
+            q = que[i][eng[i]]
+            if last[q] < 0 and q < 5:
+                last[q], free[q] = i, start[i] + cost[i][eng[i]]
+                seen += 1
+            if last[6] < 0 and work[i]:
+                last[6], free[6] = i, end[i] - lat[i] / 2
+                seen += 1
+            k -= 1
+        for i in order[first:]:
+            e = eng[i]
+            q = que[i][e]
+            s, w = free[q], last[q]
+            for j in hard[i]:
+                t = end[j] + SYNC
+                if t > s:
+                    s, w = t, j
+            for j in easy[i]:
+                t = end[j] + (0.0 if que[j][eng[j]] == q else SYNC)
+                if t > s:
+                    s, w = t, j
+            start[i], why[i] = s, w
+            s += cost[i][e]
+            free[q], last[q] = s, i
+            if work[i]:
+                s += lat[i] / 2
+                if free[6] > s:
+                    s, why[i] = free[6], last[6]
+                s += work[i]
+                free[6], last[6] = s, i
+                end[i] = s + lat[i] / 2
+            else:
+                end[i] = s + lat[i]
+        return max(end)
+
+    def pack(order):
+        rows, begin, done, lanes = [[] for _ in range(6)], [0.0] * n, [0.0] * n, 0.0
+        for i in order:
             got = None
-            for k, a in enumerate(ops[i]["alts"]):
-                s = 0.0
-                for j in deps[i]:
-                    s = max(s, end[j] + (0.0 if j in soft[i] and ops[j]["alts"][eng[j]][0] == a[0] else SYNC))
-                row = busy[a[0]]
-                at = len(row)
+            for e, q in enumerate(que[i]):
+                s = max([0.0] + [done[j] + SYNC for j in hard[i]] + [done[j] + (0.0 if que[j][eng[j]] == q else SYNC) for j in easy[i]])
+                row, at = rows[q], len(rows[q])
                 while at and row[at - 1][1] > s:
                     at -= 1
-                while at < len(row) and s + a[1] > row[at][0]:
+                while at < len(row) and s + cost[i][e] > row[at][0]:
                     s = max(s, row[at][1])
                     at += 1
-                if got is None or s + a[1] + lean[i] < got[0] + got[2]:
-                    got = (s, k, a[1], a[0], at)
-            start[i], eng[i] = got[0], got[1]
-            end[i] = got[0] + got[2] + ops[i]["lat"]
-            busy[got[3]].insert(got[4], (got[0], got[0] + got[2]))
-            for u in users[i]:
-                left[u] -= 1
-                if not left[u]:
-                    ready.append(u)
-        if best is None or max(end) <= best[0]:
-            best = (max(end), start, end, eng)
-            base, tilt = prio, lean
-    return best
+                key = (s + cost[i][e] > start[i] + cost[i][eng[i]] + 1e-6, q == 0, s + cost[i][e])
+                if got is None or key < got[0]:
+                    got = (key, e, s, at)
+            key, eng[i], begin[i], at = got
+            s = begin[i] + cost[i][eng[i]]
+            rows[que[i][eng[i]]].insert(at, (begin[i], s))
+            if work[i]:
+                lanes = max(s + lat[i] / 2, lanes) + work[i]
+                done[i] = lanes + lat[i] / 2
+            else:
+                done[i] = s + lat[i]
+        order.sort(key=lambda k: begin[k])
+
+    order, left, free = [], [len(d) for d in deps], [0.0] * 6
+    ready = [i for i in range(n) if not left[i]]
+    can = [0.0] * n
+    while ready:
+        best = None
+        for i in ready:
+            for e in range(len(que[i])):
+                s = max(can[i], free[que[i][e]])
+                key = s + cost[i][e] * (e > 0) - WEIGHT * level[i]
+                if best is None or key < best[0]:
+                    best = (key, i, e, s)
+        key, i, e, s = best
+        ready.remove(i)
+        order.append(i)
+        eng[i] = e
+        free[que[i][e]] = s + cost[i][e]
+        for u in users[i]:
+            can[u] = max(can[u], s + cost[i][e] + lat[i] + work[i] + SYNC)
+            left[u] -= 1
+            if not left[u]:
+                ready.append(u)
+    span = run(order, 0)
+    best = (span, list(order), list(eng))
+    for trial in range(TRIES):
+        if trial % 64 == 0:
+            order.sort(key=lambda k: start[k])
+            span = run(order, 0)
+            if trial % 256 == 0:
+                old, was = list(order), list(eng)
+                pack(order)
+                if run(order, 0) > span + 50:
+                    order[:], eng[:] = old, was
+                span = run(order, 0)
+            if span < best[0]:
+                best = (span, list(order), list(eng))
+        path, i = [], end.index(max(end))
+        while i >= 0:
+            if why[i] >= 0 and why[i] not in deps[i]:
+                path.append(i)
+            i = why[i]
+        v = path[draw(len(path))]
+        u, kind = why[v], draw(8)
+        old, keep = list(order), (list(start), list(end), list(why))
+        pu, pv = order.index(u), order.index(v)
+        changed = None
+        if kind < 2:
+            x = (u, v)[kind]
+            if len(que[x]) < 2:
+                continue
+            changed = (x, eng[x])
+            eng[x] = (eng[x] + 1 + draw(len(que[x]) - 1)) % len(que[x])
+            first = pu
+        elif kind < 5:
+            first = max(0, pu - (draw(12) if kind == 4 else 0))
+            need, move = set(deps[v]), [v]
+            for i in order[pv - 1:first - 1 if first else None:-1]:
+                if i in need:
+                    move.append(i)
+                    need.update(deps[i])
+            if u in move:
+                continue
+            ms = set(move)
+            order[first:pv + 1] = move[::-1] + [i for i in order[first:pv + 1] if i not in ms]
+        else:
+            first, stop = pu, min(n, pv + 1 + (draw(30) if kind == 7 else 0))
+            move, ms = [u], {u}
+            for i in order[pu + 1:stop]:
+                if any(j in ms for j in deps[i]):
+                    move.append(i)
+                    ms.add(i)
+            if v in ms:
+                continue
+            order[pu:stop] = [i for i in order[pu:stop] if i not in ms] + move
+        new = run(order, first)
+        if new <= span + HEAT * (1.0 - trial / TRIES) * (draw(1000) / 500.0) ** 2:
+            span = new
+        else:
+            order[:] = old
+            start[:], end[:], why[:] = keep
+            if changed:
+                eng[changed[0]] = changed[1]
+    eng[:] = best[2]
+    return run(best[1], 0), best[1], start, end, eng
 
 
 def emit(g, T, Q, ops):
@@ -585,7 +747,7 @@ def emit(g, T, Q, ops):
                 seen[name] = old + [(i, pm, cm, w)]
     lastsem = {}
     for i, o in enumerate(ops):
-        if o["sem"] is not None:
+        if o["sem"] is not None and not o["free"]:
             if o["sem"] in lastsem:
                 deps[i].add(lastsem[o["sem"]])
                 hard[i].add(lastsem[o["sem"]])
@@ -593,9 +755,9 @@ def emit(g, T, Q, ops):
     soft = [deps[i] - hard[i] for i in range(n)]
     if n not in PLAN:
         PLAN[n] = plan(ops, [sorted(d) for d in deps], soft)
-    span, start, end, eng = PLAN[n]
-    count, known, mark = {}, {q: {} for q in Q}, [None] * n
-    for i in sorted(range(n), key=lambda k: (start[k], k)):
+    span, order, start, end, eng = PLAN[n]
+    count, known, mark, alone = {}, {q: {} for q in Q}, [None] * n, False
+    for i in order:
         o = ops[i]
         q = o["alts"][eng[i]][0]
         sem = o["sem"] or "e" + q
@@ -612,6 +774,11 @@ def emit(g, T, Q, ops):
                 known[q][s] = v
                 for s2, v2 in clock.items():
                     known[q][s2] = max(known[q].get(s2, 0), v2)
+        if sem == "eG":
+            if (o["alone"] or alone) and known[q].get(sem, 0) < count[sem] - 1:
+                g.wait_ge(T.sem[sem], count[sem] - 1)
+                known[q][sem] = count[sem] - 1
+            alone = o["alone"]
         ins = o["alts"][eng[i]][2]()
         if o["sem"] is None:
             ins.then_inc(T.sem[sem], 1)

@@ -52,9 +52,10 @@ SEMAPHORES = ["eV", "eS", "eP", "eG", "dx0", "dx1", "du", "dv", "dw", "dn", "dm"
               "do0", "do2", "dc0", "dc1", "dy0", "dy1", "arr0", "arr1", "arr2", "col0", "col1", "col2", "loc"]
 WIDE = {BF: 2, F32: 4, I32: 4, U16: 2, CD: 4, PL: 1}
 SYNC, OVER, GATHER, PE = 165.0, 66.0, 1.55, 1.1
-USE_DM, USE_DT, USE_G = False, False, False
+USE_DM, USE_DT, USE_G = True, True, False
+LEAD, ROUND, FIRST = 4000.0, 23000.0, 150
 FIXED, PER_ROW, PER_BYTE = 1400.0, 60.0, 0.048
-TRIES, WEIGHT, HEAT = 170000, 0.2, 40.0
+TRIES, WEIGHT, HEAT = 170000, 0.2, 25.0
 CUT = ((0, 192), (192, 320))
 CHUNK = (0, 64, 192)
 ROW = 6
@@ -66,13 +67,11 @@ def rank_program(g, core, T, topo):
     if rank is None:
         return
     N = len(T.cores)
-    ops = []
+    ops, soon = [], []
     Q = {"V": g.vector, "S": g.scalar, "P": g.tensor, "G": g, "Y": g.sync}
 
-    def lanes(k):
-        m = -1
-        for d in STEP:
-            m &= topo.mask(T.cores[k], T.cores[(k - d) % N])
+    def lanes(k, d):
+        m = topo.mask(T.cores[k], T.cores[(k - d) % N])
         return m, bin(m).count("1")
 
     def A(name, c0=0, c1=None, step=1, p0=0, p1=128):
@@ -114,7 +113,8 @@ def rank_program(g, core, T, topo):
 
     def add(alts, reads, writes, **kw):
         o = {"alts": alts, "r": [x for v in reads if isinstance(v, dict) for x in v["regs"]],
-             "w": [x for v in writes for x in v["regs"]], "lat": 0.0, "sem": None, "inc": 1, "after": [], "free": False, "work": 0.0}
+             "w": [x for v in writes for x in v["regs"]], "lat": 0.0, "sem": None, "inc": 1, "after": [], "free": False, "work": 0.0,
+             "due": None if not soon else soon.pop(0) if len(soon) > 1 else soon[0]}
         o.update(kw)
         o["alone"] = any(v["p"][0] for v in list(reads) + list(writes) if isinstance(v, dict) and "p" in v)
         if o["alone"]:
@@ -157,6 +157,7 @@ def rank_program(g, core, T, topo):
                 alts.append(("V", cv(out, in_), lambda: g.vector.tensor_scalar(ap(out), ap(in_), ap(scale), None, Op.mult)))
         if "G" in on:
             alts.append(("G", 260 + 2.2 * out["n"], lambda: g.affine_select(ap(out), ap(in_), [[0, out["n"]]], Op.is_ge, 0.0, 0, 0)))
+        alts.sort(key=lambda x: on.index(x[0]))
         return add(alts, [in_, scale], [out])
 
     def act(out, in_, fn, bias=0.0, scale=1.0):
@@ -375,52 +376,59 @@ def rank_program(g, core, T, topo):
         else:
             cp(A("FT", 32 * t, 32 * t + 32), bank("PL", b, 0, 32), "SV")
 
-    def frames(k):
+    def frames(k, on):
         a, z = 96 * k, 384 * k
         tt(A("FL", a, a + 88), A("PM", a, a + 88), A("PM", a + 8, a + 96), Op.is_lt)
         scan(A("KS", a, a + 96), A("KP"), A("FL", a, a + 96), 0.0, Op.mult, Op.add)
         tr(A("KQ", z, z + 96), A("KS", a, a + 96))
         for b in range(4):
-            cp(A("KQ", z + 96, z + 192, **blk(b ^ 1)), A("KQ", z, z + 96, **blk(b)), "SV")
+            cp(A("KQ", z + 96, z + 192, **blk(b ^ 1)), A("KQ", z, z + 96, **blk(b)), on[b % 2])
         for u in range(2):
-            cp(A("KQ", z + 192, z + 384, **blk(1 - u, 64)), A("KQ", z, z + 192, **blk(u, 64)), "SV")
+            cp(A("KQ", z + 192, z + 384, **blk(1 - u, 64)), A("KQ", z, z + 192, **blk(u, 64)), on[u])
 
-    def tables(src, n, c0, marks, values, slots=8, first=0):
+    def tables(src, n, c0, marks, values, slots=8, first=0, onv=()):
         for h in range(first, slots):
             if values:
                 b = turn["v"] % 3
                 turn["v"] += 1
                 mm(bank("PV", b, 0, max(n, 128)), (EF[h], src))
-                cp(A("VW", 512 * h + c0, 512 * h + c0 + n), bank("PV", b, 0, n), values, scale=0.5 if USE_G else None)
+                cp(A("VW", 512 * h + c0, 512 * h + c0 + n), bank("PV", b, 0, n), "VS" if h in onv else "SV", scale=0.5 if USE_G else None)
             if marks:
-                b = 1 + turn["l"] % 4
+                b = (1 + turn["l"] % 4) if n == H else (1, 4)[turn["l"] % 2]
                 turn["l"] += 1
                 mm(bank("PL", b, 0, max(n, 128)), (UM[h], src))
-                cp(A("MT", 512 * h + c0, 512 * h + c0 + n), bank("PL", b, 0, n), marks)
+                cp(A("MT", 512 * h + c0, 512 * h + c0 + n), bank("PL", b, 0, n), "VS" if h in onv else "SV")
 
     for r, d in enumerate(STEP):
         qx, sx, ql, sl = "QX%d" % r, "SX%d" % r, "QL%d" % r, "SL%d" % r
         X = pair(qx, sx, 0, C)
         dst = T.cores[(rank - d) % N]
 
-        def send(out, in_, sem, view=ap, dst=dst):
+        def due(*times, r=r):
+            soon[:] = [LEAD + ROUND * r + x for x in times]
+
+        def send(out, in_, sem, view=ap, dst=dst, d=d):
             rid, pid = topo.addr(dst)[:2]
-            f = lambda: g.remote_dma(view(out), view(in_), T.sem[sem], T.sem["loc"], pid, rid, lanes(rank)[0])
-            return add([("G", 350.0, f)], [in_], [], sem="loc", inc=lanes(rank)[1], lat=FIXED + 300, free=True,
-                       work=16 * (PER_ROW + 1.3 * PER_BYTE * in_["n"] * in_["w"]))
+            f = lambda: g.remote_dma(view(out), view(in_), T.sem[sem], T.sem["loc"], pid, rid, lanes(rank, d)[0])
+            return add([("G", 350.0, f)], [in_], [], sem="loc", inc=lanes(rank, d)[1], lat=FIXED + 300, free=True,
+                       work=128 / lanes(rank, d)[1] * (PER_ROW + 1.3 * PER_BYTE * in_["n"] * in_["w"]))
 
         def landed(sem, writes, sent):
-            add([("R", 0.0, None)], [], writes, sem=sem, inc=len(sent) * lanes((rank + d) % N)[1], lat=2000.0 if sem == "col0" else 300.0, after=sent)
+            add([("R", 0.0, None)], [], writes, sem=sem, inc=len(sent) * lanes((rank + d) % N, d)[1],
+                lat=2000.0 if sem == "col0" else 300.0, after=sent)
+        due(-1200, 100)
         sent = [send(A(ql, j0, j1), A(qx, j0, j1), "col%d" % r, u8) for j0, j1 in (CUT if r else ((0, C),))]
         landed("col%d" % r, [A(ql), A(sl)], sent + [send(A(sl), A(sx), "col%d" % r)])
         XA, XB = pair(qx, sx, 0, 192), pair(qx, sx, 192, C)
         sc = lambda t: A("FT", 32 * t + 15, 32 * t + 16)
+        due(-1200)
         for t in (0, 1):
             scores(qx, sx, t, 0, 2 + t)
         mm(bank("PL", 1, 0, 192), (U2, XA))
         mm(bank("PL", 0, 0, 192), (U2, XA))
         act(A("DD", 0, 128), bank("PL", 1, 0, 128), Fn.Identity, bias=sc(0), scale=-1.0)
         act(A("DD", 128, 192), bank("PL", 1, 128, 192), Fn.Identity, bias=sc(1), scale=-1.0)
+        due(0)
         ts(A("F1", 512, 768, 4), bank("PL", 0, 128, 192), sc(0), Op.is_le)
         ts(A("F1", 1, 512, 4), bank("PL", 0, 0, 128), sc(1), Op.is_lt)
         tt(A("F1", 3, 768, 4), A("DD", 0, 192), A("MK", 0, 192), Op.is_ge)
@@ -428,6 +436,7 @@ def rank_program(g, core, T, topo):
         mm(bank("PL", 2, 0, 128), (U2, XB))
         mm(bank("PL", 3, 0, 128), (U2, XB))
         act(A("DD", 192, C), bank("PL", 3, 0, 128), Fn.Identity, bias=sc(2), scale=-1.0)
+        due(900, 1100, 780, 1650, 1420, 2140, 1820, 2305, 1980, 2470, 2470, 2870, 3200, 3600, 4215, 4640)
         for t in (0, 1):
             ts(A("F1", 768 + t, 1280, 4), bank("PL", 2, 0, 128), sc(t), Op.is_le)
         ts(A("F1", 2, 768, 4), bank("PL", 0, 0, 192), sc(2), Op.is_lt)
@@ -446,22 +455,26 @@ def rank_program(g, core, T, topo):
         ts(A(ol, 6, 12), A("OT", 1, 192, 32), 192.0, Op.add)
         landed("arr%d" % r, [A(ll)], [send(A(ll), A(ol), "arr%d" % r)])
         if r and USE_DM:
+            due(2700)
             mm(bank("PL", 1, 0, C), (UA, X))
             cp(A("MS"), bank("PL", 1, 0, C), "SV")
-            dma("Y", "dm", [(T.MT[64 * k:64 * k + 64:4, 512 * h:512 * h + C], T.MS[16 * h:16 * h + 16, :]) for h in range(8) for k in range(2)],
-                [A("MS")], [A("MT", 512 * h, 512 * h + C) for h in range(8)], 256, 1280)
         else:
-            tables(X, C, 0, "SV", None)
+            due(*[4400 + 250 * k for k in range(16)])
+            tables(X, C, 0, True, None)
+        due(1975, 2630, 3035, 3430, 3710, 3710, 3830, 3900, 4050, 4050, 4400)
         scan(A("PM", 0, 96), A("RS"), A("FT"), 0.0, Op.add, Op.max)
-        frames(0)
+        frames(0, ("VS", "SV"))
         cp(A("KT", 16, 16 + C), by(A("KQ", 0, 384), A("LQ")), "SV")
-        tables(XA, 192, 0, None, "SV", 4)
-        tables(XB, 128, 192, None, "SV", 4)
+        due(-500, -300, -450, -50, 600, 900, 650, 1150, 1200, 1400, 1250, 1600, 1300, 1800, 1350, 2000, 2300)
+        tables(XA, 192, 0, None, True, 4)
+        tables(XB, 128, 192, None, True, 4)
         if USE_DT:
             dma("Y", "dt", [(T.VW[16 * k:16 * k + 16, 2048:3904], T.VW[16 * (k ^ 1):16 * (k ^ 1) + 16, 0:1856]) for k in range(8)],
                 [A("VW", 0, 1856)], [A("VW", 2048, 3904)], 128, 3712)
         else:
-            tables(X, C, 0, None, "SV", 8, 4)
+            due(2750, 2800, 2760, 3200, 4100, 5100, 4150, 5500)
+            tables(X, C, 0, None, True, 8, 4)
+        due(4950, 5200, 5600, 6350, 6750, 7000)
         tr(A("KXA", 0, C), A("KT", 16, 16 + C))
         tr(A("KXA", C, C + 352), A("KT", 0, 352))
         cp(A("KA"), by(A("KXA"), A("LK", 0, 7)), "SV", scale=512.0)
@@ -469,23 +482,34 @@ def rank_program(g, core, T, topo):
         ts(A("T5"), A("T4"), 4095, Op.bitwise_and)
         cp(A("OA"), A("T5"))
         for q in range(4):
+            due((7200, 7780, 11300, 11900)[q])
             cp(A("AP", C * q, C * q + C), by(A("VW"), A("OA", 20 * q, 20 * q + 20)), "SV")
             a2 = "A2" if USE_G else "AP"
             if USE_G:
                 cp(A("A2", C * q, C * q + C), A("AP", C * q, C * q + C), "SV", scale=2.0)
+            due(11000 + 400 * q)
             dma("Y", "da%d" % q, [(T.AS[32 * q:32 * q + 32, C * t:C * t + C], T[a2][32 * t:32 * t + 32, C * q:C * q + C])
                                   for t in range(4)], [A(a2, C * q, C * q + C)], [A("AS", **blk(q))], 128, 640)
+        due(6100, 6500, 6800)
         tt(A("PF"), A("YF"), A("KA", 80, 112), Op.subtract)
         cp(A("PH", 0, 16), by(A("PF"), A("LF", 0, 1)), "SV")
         plus(A("PH", 16, 32), A("PH", 0, 16), 512.0)
+        due(5565, 5900, 5570, 6050, 5575, 6200, 6460, 6870, 7150, 7430)
         for t in range(3):
-            scores(ql, sl, t, 1, 2 + t)
-        frames(1)
-        cp(A("KT", 16 + C, 16 + E), by(A("KQ", 384, 768), A(ll, 6, 12)), "SV")
+            scores(ql, sl, t, 1, (2, 3, 0)[t])
+        frames(1, ("VS", "VS"))
+        if r and USE_DM:
+            dma("Y", "dm", [(T.MT[64 * k:64 * k + 64:4, 512 * h:512 * h + C], T.MS[16 * h:16 * h + 16, :]) for h in range(8) for k in range(2)],
+                [A("MS"), A("KXA", 0, C)], [A("MT", 512 * h, 512 * h + C) for h in range(8)], 256, 1280)
+        due(8665, 8870, 8665)
+        cp(A("KT", 16 + C, 16 + E), by(A("KQ", 384, 768), A(ll, 6, 12)), "VS")
         at = H * (2 - r)
         pick(pair("QB", "SB", at, at + H), pair(ql, sl, 0, C), A(ll, 0, 6))
-        tables(pair("QB", "SB", at, at + 128), H, C, "SV", None)
-        tables(pair("QB", "SB", at, at + 128), H, C, None, "SV")
+        due(*[9250 + 80 * k + 250 * (k % 2) for k in range(16)])
+        tables(pair("QB", "SB", at, at + 128), H, C, True, None, onv=(2, 4, 6))
+        due(*[11900 + 90 * k + 250 * (k % 2) for k in range(16)])
+        tables(pair("QB", "SB", at, at + 128), H, C, None, True, onv=(5, 7))
+        due(9040, 9040, 9415, 9725, 9810, 10065, 10315, 9560, 9900, 10400, 10500, 11100, 11750, 11800)
         cp(A("KG", 16, 112), by(A("KT", 16, 16 + E), A("OK", 0, 6)), "V", scale=512.0)
         cp(A("KG", 112, 176), by(A("KT", 16, 16 + E), A("OK", 6, 10)), "SV", scale=512.0)
         tr(A("KX", 0, 160), A("KG", 16, 176))
@@ -500,8 +524,9 @@ def rank_program(g, core, T, topo):
         ts(A("G2"), A("G1"), 4095, Op.bitwise_and)
         tt(A("CB", 0, 80, 2), A("G2", 0, 80, 2), A("G2", 1, 80, 2), Op.subtract)
         cp(A("CB", 1, 80, 2), A("G2", 1, 80, 2))
+        due(10765, 11265, 10765, 11490, 11885, 12030, 12200, 12350, 12515, 12820, 13125, 13125, 13260, 13280, 13565, 13565, 13965)
         for q in range(2):
-            cp(A("MG", 160 * q, 160 * q + 160), by(A("MT"), A("OM", 10 * q, 10 * q + 10)), "SV")
+            cp(A("MG", 160 * q, 160 * q + 160), by(A("MT"), A("OM", 10 * q, 10 * q + 10)), ("VS", "SV")[q])
             tr(A("MX", 160 * q, 160 * q + 160), A("MG", 160 * q, 160 * q + 160))
         tt(A("CF", 1, 80, 2), A("MX", 160, 320, 4), A("MX", 0, 160, 4), Op.is_gt)
         tt(A("CM"), A("MX", 160, 320, 4), A("MX", 0, 160, 4), Op.max)
@@ -510,28 +535,34 @@ def rank_program(g, core, T, topo):
         tt(A("C1", 0, 72, 2), A("C1", 9, 80, 2), A("C1", 1, 72, 2), Op.subtract)
         scan(A("CZ", 0, 72), A("CTP"), A("C1", 0, 72), 0.0, Op.mult, Op.add)
         for b in range(4):
-            cp(A("CZ", 72, 144, **blk(b ^ 1)), A("CZ", 0, 72, **blk(b)), "SV")
+            cp(A("CZ", 72, 144, **blk(b ^ 1)), A("CZ", 0, 72, **blk(b)), ("VS", "SV")[b % 2])
         for u in range(2):
-            cp(A("CZ", 144, 288, **blk(1 - u, 64)), A("CZ", 0, 144, **blk(u, 64)), "SV")
+            cp(A("CZ", 144, 288, **blk(1 - u, 64)), A("CZ", 0, 144, **blk(u, 64)), ("VS", "SV")[u])
         cp(A("OB"), by(A("CZ"), A("LZ", 0, 5)))
-        for q in range(4):
-            for j0, j1 in (CUT if q >= 2 else ((0, C),)):
-                tt(A("ZP", C * q + j0, C * q + j1), by(A("VW"), A("OB", 20 * q + j0 // 16, 20 * q + j1 // 16)),
-                   A("AP", C * q + j0, C * q + j1), Op.add)
-                for t in range(4):
-                    cp(A("Z", 4 * j0 + t, 4 * j1, 4, **blk(q)), A("ZP", C * q + j0, C * q + j1, **blk(t)),
-                       "SVG" if USE_G else "SV", scale=None if USE_G else 0.5)
-        for j0, j1 in CUT:
+        for q, (j0, j1), at, mine, then in ((0, (0, C), 14315, 0, 0), (1, (0, C), 14870, 2, 16400), (2, CUT[0], 15430, 2, 16900),
+                                            (3, CUT[0], 15790, 3, 17200), (2, CUT[1], 16150, 0, 0), (3, CUT[1], 17700, 4, 18200)):
+            due(at)
+            tt(A("ZP", C * q + j0, C * q + j1), by(A("VW"), A("OB", 20 * q + j0 // 16, 20 * q + j1 // 16)),
+               A("AP", C * q + j0, C * q + j1), Op.add)
+            for t in range(4):
+                due(then if t < mine else at + 700 + 2000 * (j0 > 0))
+                cp(A("Z", 4 * j0 + t, 4 * j1, 4, **blk(q)), A("ZP", C * q + j0, C * q + j1, **blk(t)),
+                   ("VS" if t < mine else "SV") + "G" * USE_G, scale=None if USE_G else 0.5)
+        for k, (j0, j1) in enumerate(CUT):
             QZ = pair("QZ", "SZ", j0, j1)
+            due(18000 + 900 * k)
             quant(QZ, A("Z", 4 * j0, 4 * j1))
             for t in range(4):
                 b = turn["v"] % 3
                 turn["v"] += 1
+                due(18400 + 1000 * k + 230 * t, 18800 + 1100 * k + 280 * t, 19300 + 2100 * k + 450 * t)
                 mm(bank("PV", b, 0, j1 - j0), (pair("WC", "WS", 128 * t, 128 * t + 128), QZ))
                 act(A("RL", C * t + j0, C * t + j1), bank("PV", b, 0, j1 - j0), Fn.Relu, scale=0.03125)
                 tt(A("X1", 4 * j0 + t, 4 * j1, 4), A("RL", C * t + j0, C * t + j1), A("AS", C * t + j0, C * t + j1), Op.add)
+            due(21600 + 1250 * k)
             quant(pair("QX%d" % (r + 1), "SX%d" % (r + 1), j0, j1), A("X1", 4 * j0, 4 * j1))
 
+    soon[:] = [LEAD + len(STEP) * ROUND]
     cp(A("T6"), A("YF"))
     ts(A("T7"), A("T6"), 9, Op.arith_shift_right, 7, Op.bitwise_and)
     cp(A("SF"), A("T7"))
@@ -640,27 +671,66 @@ def plan(ops, deps, soft):
                 done[i] = s + lat[i]
         order.sort(key=lambda k: begin[k])
 
-    order, left, free = [], [len(d) for d in deps], [0.0] * 6
-    ready = [i for i in range(n) if not left[i]]
-    can = [0.0] * n
-    while ready:
-        best = None
-        for i in ready:
-            for e in range(len(que[i])):
-                s = max(can[i], free[que[i][e]])
-                key = s + cost[i][e] * (e > 0) - WEIGHT * level[i]
-                if best is None or key < best[0]:
-                    best = (key, i, e, s)
-        key, i, e, s = best
-        ready.remove(i)
-        order.append(i)
-        eng[i] = e
-        free[que[i][e]] = s + cost[i][e]
-        for u in users[i]:
-            can[u] = max(can[u], s + cost[i][e] + lat[i] + work[i] + SYNC)
-            left[u] -= 1
-            if not left[u]:
-                ready.append(u)
+    def lay(due, lean):
+        rows, begin, done, lanes = [[] for _ in range(6)], [0.0] * n, [0.0] * n, []
+        left = [len(d) for d in deps]
+        ready = [i for i in range(n) if not left[i]]
+        while ready:
+            i = min(ready, key=lambda k: due[k])
+            ready.remove(i)
+            got = None
+            for e, q in enumerate(que[i]):
+                s = max([0.0] + [done[j] + SYNC for j in hard[i]] + [done[j] + (0.0 if que[j][eng[j]] == q else SYNC) for j in easy[i]])
+                row, at = rows[q], len(rows[q])
+                while at and row[at - 1][1] > s:
+                    at -= 1
+                while at < len(row) and s + cost[i][e] > row[at][0]:
+                    s = max(s, row[at][1])
+                    at += 1
+                key = s + cost[i][e] + ((lean[i] if q == 0 else 0.0) if ops[i]["due"] is None else 1e6 * e)
+                if got is None or key < got[0]:
+                    got = (key, e, s, at)
+            key, eng[i], begin[i], at = got
+            s = begin[i] + cost[i][eng[i]]
+            rows[que[i][eng[i]]].insert(at, (begin[i], s))
+            if work[i]:
+                s += lat[i] / 2
+                for x, y in lanes:
+                    if s < y and s + work[i] > x:
+                        s = y
+                lanes.append((s, s + work[i]))
+                lanes.sort()
+                done[i] = s + work[i] + lat[i] / 2
+            else:
+                done[i] = s + lat[i]
+            for u in users[i]:
+                left[u] -= 1
+                if not left[u]:
+                    ready.append(u)
+        order = sorted(range(n), key=lambda k: (begin[k], k))
+        return run(order, 0), order
+
+    base = [o["due"] for o in ops]
+    for i in range(n - 1, -1, -1):
+        if base[i] is None:
+            base[i] = min([base[u] for u in users[i]] + [1e9]) - min(cost[i]) - lat[i] - work[i] - SYNC
+        else:
+            base[i] += 1e-3 * i
+    tilt, got = [500.0] * n, None
+    for trial in range(FIRST):
+        due, lean = list(base), list(tilt)
+        for k in range(draw(4) + 1 if trial else 0):
+            i, kind = draw(n), draw(3)
+            if kind == 0:
+                lean[i] = draw(1200) - 400.0
+            else:
+                push = (draw(41) - 20) * 150.0
+                for j in range(i, min(n, i + 1 + (draw(16) if kind == 1 else 0))):
+                    due[j] -= push
+        new, order = lay(due, lean)
+        if got is None or new <= got[0]:
+            got, base, tilt = (new, order, list(eng)), due, lean
+    order, eng[:] = got[1], got[2]
     span = run(order, 0)
     best = (span, list(order), list(eng))
     for trial in range(TRIES):

from concourse.mybir import dt, AluOpType, ActivationFunctionType

C, H, E = 320, 96, 416
STEP = [1, 2, 3]
BF, F32, I32, U16, CD, PL = "bfloat16", "float32", "int32", "uint16", "float8_e4m3fn_x4", "uint8"
SB = {
    "X0": (1280, BF), "X1": (1280, BF), "U": (512, BF), "VV": (512, BF),
    "QU": (128, CD), "SU": (128, PL), "QV": (128, CD), "SV": (128, PL),
    "QU2": (160, CD), "SU2": (160, PL), "QUP": (416, CD), "SUP": (416, PL),
    "WC": (512, CD), "WS": (512, PL), "QB": (416, CD), "SB": (416, PL),
    "EB": (512, BF), "ET": (2048, BF), "QE": (512, CD), "SE": (512, PL), "QE2": (512, CD), "SE2": (512, PL),
    "HI": (1, F32), "I32": (32, F32), "CT": (528, BF), "QC": (132, CD), "SC": (132, PL), "ZT": (512, BF),
    "F1": (1280, BF), "QF1": (320, CD), "SF1": (320, PL), "F2": (768, BF), "QF2": (192, CD), "SF2": (192, PL),
    "MK0": (128, BF), "MK": (320, BF), "DD": (320, BF), "INN": (192, BF), "OT": (192, F32),
    "FT": (96, F32), "PM": (192, F32), "FL": (192, BF), "KS": (192, BF), "KQ": (768, BF), "RS": (96, F32), "KP": (96, BF),
    "KT": (432, BF), "KG": (192, BF), "KX": (352, BF), "KXA": (672, BF), "KF": (32, F32),
    "KA": (112, F32), "SQ": (416, BF), "SD": (608, BF), "SW": (608, BF), "HT": (80, F32),
    "NI": (128, I32), "NE": (64, F32), "NF": (64, F32), "ND": (32, F32),
    "YF": (32, F32), "PF": (32, F32), "PH": (32, F32), "T2": (20, I32), "T3": (20, I32),
    "T4": (80, I32), "T5": (80, I32), "T6": (32, I32), "T7": (32, I32), "G1": (80, I32), "G2": (80, I32),
    "CB": (80, F32), "CF": (80, F32), "CM": (40, F32), "CTP": (72, F32), "C1": (80, F32), "CZ": (288, F32),
    "MS": (320, F32), "MT": (4096, F32), "MG": (320, F32), "MX": (320, F32),
    "VW": (4096, BF), "AP": (1280, BF), "AS": (1280, BF), "A2": (1280, BF), "ZP": (1280, BF), "Z": (1280, BF),
    "QZ": (320, CD), "SZ": (320, PL), "RL": (1280, F32), "YO": (320, F32),
    "IT": (256, F32), "PT": (256, F32), "CI": (86, F32), "CX": (12, F32), "PC": (1, F32), "GI": (4, I32), "GJ": (4, I32),
    "GF": (4, F32), "GK": (8, I32), "GL": (8, I32), "AB": (80, F32), "PD": (11, F32),
    "L2": (10, U16), "LU": (26, U16), "LS": (32, U16), "LA": (38, U16), "LK": (8, U16), "LC": (6, U16), "LZ": (6, U16),
    "LE": (2, U16), "LF": (2, U16), "LO": (2, U16), "LN": (2, U16), "LQ": (20, U16),
    "OK": (16, U16), "OM": (20, U16), "OA": (80, U16), "OB": (80, U16),
    "SF": (32, F32), "ST": (32, F32), "SG": (64, F32),
}
for _r in range(4):
    SB["QX%d" % _r] = (320, CD)
    SB["SX%d" % _r] = (320, PL)
for _r in range(3):
    SB["QL%d" % _r] = (320, CD)
    SB["SL%d" % _r] = (320, PL)
    SB["OL%d" % _r] = (12, U16)
    SB["LL%d" % _r] = (12, U16)
PART = {}
for _pool, _names in (("TI", "T2 T3 T4 T5 T6 T7 G1 G2"), ("TF", "CF CM CTP C1 CB KA KF PH YF PF NE NF ND SF ST"),
                      ("TU", "LA LK LC LZ LE LF LO LN LQ"), ("TO", "OK OM OA OB"), ("TG", "GI GJ GK GL")):
    _at = 0
    for _k in _names.split():
        PART[_k] = (_pool, _at, SB[_k][0])
        _at += (SB[_k][0] + 7) // 8 * 8
        SB[_pool] = (_at, SB.pop(_k)[1])
SCRATCH = {k: ("sbuf", [128, n], d) for k, (n, d) in SB.items()}
SCRATCH["PL"] = ("psum", [128, 512 * 5], F32)
SCRATCH["PV"] = ("psum", [128, 512 * 3], F32)
SEMAPHORES = ["eV", "eS", "eP", "eG", "dx0", "dx1", "du", "dv", "dw", "dn", "dm", "dt", "da0", "da1", "da2", "da3",
              "do0", "do2", "dc0", "dc1", "dy0", "dy1", "arr0", "arr1", "arr2", "col0", "col1", "col2", "loc"]
WIDE = {BF: 2, F32: 4, I32: 4, U16: 2, CD: 4, PL: 1}
SYNC, OVER, GATHER, PE = 165.0, 66.0, 1.55, 1.1
USE_DM, USE_DT, USE_G = True, True, False
LEAD, ROUND, FIRST = 4000.0, 23000.0, 150
FIXED, PER_ROW, PER_BYTE = 1400.0, 60.0, 0.048
TRIES, WEIGHT, HEAT = 170000, 0.2, 25.0
CUT = ((0, 192), (192, 320))
CHUNK = (0, 64, 192)
ROW = 6
Op, Fn = AluOpType, ActivationFunctionType


def rank_program(g, core, T, topo):
    rank = T.rank_of(core)
    if rank is None:
        return
    N = len(T.cores)
    ops, soon = [], []
    Q = {"V": g.vector, "S": g.scalar, "P": g.tensor, "G": g, "Y": g.sync}

    def lanes(k, d):
        m = topo.mask(T.cores[k], T.cores[(k - d) % N])
        return m, bin(m).count("1")

    def A(name, c0=0, c1=None, step=1, p0=0, p1=128):
        if name in PART:
            pool, at, width = PART[name]
            return A(pool, at + c0, at + (width if c1 is None else c1), step, p0, p1)
        if name in ("PL", "PV"):
            cm = 0
            for b in range(c0 // 512, (c1 - 1) // 512 + 1):
                cm |= 1 << b
            reg = (name, (1 << 128) - 1, cm)
            kind = F32
        else:
            if c1 is None:
                c1 = SB[name][0]
            if step == 1:
                cm = ((1 << (c1 - c0)) - 1) << c0
            else:
                cm = 0
                for c in range(c0, c1, step):
                    cm |= 1 << c
            reg = (name, ((1 << (p1 - p0)) - 1) << p0, cm)
            kind = SB[name][1]
        view = T[name][p0:p1, c0:c1] if step == 1 else T[name][p0:p1, c0:c1:step]
        return {"ap": view, "regs": [reg], "n": len(range(c0, c1, step)), "w": WIDE[kind], "kind": kind, "ind": False,
                "ps": name in ("PL", "PV"), "p": (p0, p1)}

    def bank(name, b, c0, c1, step=1):
        return A(name, 512 * b + c0, 512 * b + c1, step)

    def by(win, off):
        return {"ap": win["ap"].indirect(off["ap"]), "regs": win["regs"] + off["regs"], "n": 16 * off["n"], "w": 4, "ind": True, "ps": False}

    def blk(b, n=32):
        return {"p0": n * b, "p1": n * b + n}

    def ap(v):
        return v["ap"] if isinstance(v, dict) else v

    def add(alts, reads, writes, **kw):
        o = {"alts": alts, "r": [x for v in reads if isinstance(v, dict) for x in v["regs"]],
             "w": [x for v in writes for x in v["regs"]], "lat": 0.0, "sem": None, "inc": 1, "after": [], "free": False, "work": 0.0,
             "due": None if not soon else soon.pop(0) if len(soon) > 1 else soon[0]}
        o.update(kw)
        o["alone"] = any(v["p"][0] for v in list(reads) + list(writes) if isinstance(v, dict) and "p" in v)
        if o["alone"]:
            o["alts"] = [(a[0], a[1] + SYNC * (a[0] == "G"), a[2]) for a in alts]
        ops.append(o)
        return len(ops) - 1

    def cv(out, *ins):
        vs = [v for v in (out,) + ins if isinstance(v, dict) and (v["n"] > 1 or v is out)]
        n = out["n"]
        if any(v["ind"] for v in vs):
            return 60 + GATHER * n
        return max(64.0, OVER + n * (0.5 if all(v["w"] == 2 for v in vs) else 1.0))

    def cs(out, in_):
        return (80 + GATHER * out["n"]) if in_["ind"] else OVER + 20 + out["n"]

    def ts(out, in0, s1, op0, s2=None, op1=None):
        if op1 is None:
            f = lambda: g.vector.tensor_scalar(ap(out), ap(in0), ap(s1), None, op0)
        else:
            f = lambda: g.vector.tensor_scalar(ap(out), ap(in0), ap(s1), ap(s2), op0, op1)
        return add([("V", cv(out, in0), f)], [in0, s1, s2], [out])

    def tt(out, in0, in1, op):
        c = cv(out, in0) if in0["ind"] else OVER + out["n"] * (1 if in0["ps"] or in1["ps"] else 2)
        return add([("V", c, lambda: g.vector.tensor_tensor(ap(out), ap(in0), ap(in1), op))], [in0, in1], [out])

    def cp(out, in_, on="V", scale=None):
        alts = []
        if "S" in on:
            if scale is None:
                alts.append(("S", cs(out, in_), lambda: g.scalar.activation(ap(out), ap(in_), Fn.Copy)))
            else:
                alts.append(("S", cs(out, in_), lambda: g.scalar.activation(ap(out), ap(in_), Fn.Copy, scale=ap(scale))))
        if "V" in on:
            if scale is None:
                alts.append(("V", cv(out, in_), lambda: g.vector.tensor_copy(ap(out), ap(in_))))
            else:
                alts.append(("V", cv(out, in_), lambda: g.vector.tensor_scalar(ap(out), ap(in_), ap(scale), None, Op.mult)))
        if "G" in on:
            alts.append(("G", 260 + 2.2 * out["n"], lambda: g.affine_select(ap(out), ap(in_), [[0, out["n"]]], Op.is_ge, 0.0, 0, 0)))
        alts.sort(key=lambda x: on.index(x[0]))
        return add(alts, [in_, scale], [out])

    def act(out, in_, fn, bias=0.0, scale=1.0):
        return add([("S", cs(out, in_), lambda: g.scalar.activation(ap(out), ap(in_), fn, bias=ap(bias), scale=ap(scale)))],
                   [in_, bias, scale], [out])

    def plus(out, in_, k):
        return add([("S", cs(out, in_), lambda: g.scalar.activation(ap(out), ap(in_), Fn.Identity, bias=ap(k))),
                    ("V", cv(out, in_), lambda: g.vector.tensor_scalar(ap(out), ap(in_), ap(k), None, Op.add))], [in_, k], [out])

    def count(out, pattern, base=0, cm=0):
        if out["kind"] == I32:
            return ("G", 200 + 2.2 * out["n"], lambda: g.iota(ap(out), pattern, base, cm))
        return ("G", 200 + 2.2 * out["n"], lambda: g.iota(ap(out), pattern, base, cm, allow_small_or_imprecise_dtypes=True))

    def iota(out, pattern, base=0, cm=0):
        return add([count(out, pattern, base, cm)], [], [out])

    def fill(out, k, on="V"):
        alts, zero = [], None
        if "S" in on:
            zero = A("ZT", 0, out["n"], 1, *out["p"])
            alts.append(("S", cs(out, zero), lambda: g.scalar.activation(ap(out), ap(zero), Fn.Identity, bias=k)))
        if "V" in on:
            alts.append(("V", cv(out), lambda: g.vector.memset(ap(out), k)))
        if "G" in on:
            alts.append(count(out, [[0, out["n"]]], int(k)))
        return add(alts, [zero], [out])

    def tr(out, in_):
        return add([("V", cv(out, in_), lambda: g.vector.transpose(ap(out), ap(in_)))], [in_], [out])

    def scan(out, d0, d1, init, op0, op1):
        return add([("V", cv(out, d0, d1), lambda: g.vector.tensor_tensor_scan(ap(out), ap(d0), ap(d1), init, op0, op1))], [d0, d1], [out])

    def pair(q, s, c0, c1):
        return (A(q, c0, c1), A(s, c0, c1))

    def quant(dst, in_):
        return add([("V", 30 + 0.265 * in_["n"], lambda: g.vector.quantize_mx(ap(dst[0]), ap(dst[1]), ap(in_)))], [in_], [dst[0], dst[1]])

    def mm(out, *terms):
        def f():
            last = None
            for k, (w, x) in enumerate(terms):
                last = g.tensor.matmul_mx(ap(out), ap(w[0]), ap(w[1]), ap(x[0]), ap(x[1]), k == 0, k == len(terms) - 1)
            return last
        return add([("P", len(terms) * PE * (out["n"] + 16), f)], [v for w, x in terms for v in w + x], [out])

    def pick(dst, src, off):
        f = lambda: g.vector.tensor_copy(ap(dst[0]).bitcast(dt.uint32), ap(src[0]).bitcast(dt.uint32).indirect(ap(off)))
        add([("V", 60 + GATHER * dst[0]["n"], f)], [src[0], off], [dst[0]])
        cp(dst[1], by(src[1], off), "S")

    def dma(q, sem, moves, reads, writes, rows, width):
        def f():
            for o, i in moves:
                Q[q].dma_start(o, i).then_inc(T.sem[sem], 16)
        return add([(q, 100.0 * len(moves), f)], reads, writes, sem=sem, inc=16 * len(moves), lat=FIXED,
                   work=rows / 16 * (PER_ROW + PER_BYTE * width))

    u8 = lambda v: ap(v).bitcast(dt.uint8)

    dma("Y", "dx0", [(T.X0[:, 0:768], T.x[:, 0:768])], [], [A("X0", 0, 768)], 128, 1536)
    dma("S", "du", [(T.U[:], T.u[:])], [], [A("U")], 128, 1024)
    dma("S", "dx1", [(T.X0[:, 768:1280], T.x[:, 768:1280])], [], [A("X0", 768, 1280)], 128, 1024)
    fill(A("ZT"), 0.0)
    fill(A("NI", p1=32), 0)
    dma("Y", "dn", [(T.NI[0:20, 0:64], T.nb[:]), (T.NI[0:20, 64:128], T.e[:])], [], [A("NI", p1=32)], 40, 256)
    dma("Y", "dw", [(u8(A("WC")), T.wc[:]), (T.WS[:], T.ws[:])], [], [A("WC"), A("WS")], 256, 1280)
    dma("Y", "dv", [(T.VV[:], T.v[:])], [], [A("VV")], 128, 1024)

    FAR = C // 16 + 1
    tabs = [([[0, 2], [1, 16]], 0),
            ([[0, 4], [16, 8]], 1),
            ([[0, 2], [32, 4], [0, 4]], 0),
            ([[0, 8], [2, 4]], 0),
            ([[16, 2], [0, 16]], 0),
            ([[10, 2], [1, 16]], 0),
            ([[1, 2], [2, 8], [10, 2]], 0)]
    col = lambda k: A("PT", 32 * k, 32 * k + 1)
    pd = lambda k: A("PD", k, k + 1)
    fill(A("MK0"), 2.0 ** -120)
    add([("G", 200 + 256, lambda: g.affine_select(T.MK[:, 0:128], T.MK0[:], [[-1, 128]], Op.is_ge, 0.0, 0, 1))],
        [A("MK0")], [A("MK", 0, 128)])
    add([("G", 200 + 128, lambda: g.affine_select(T.MK[:, 128:192], T.MK0[:, 0:64], [[-1, 64]], Op.is_ge, 0.0, -64, 1))],
        [A("MK0")], [A("MK", 128, 192)])
    fill(A("MK", 128, 192, p1=64), 1e29, "SV")
    cp(A("MK", 192, 320), A("MK", 0, 128), "SV")
    for k, (pat, base) in enumerate(tabs):
        if k != 3 or USE_DM:
            iota(A("IT", 32 * k, 32 * k + 32), pat, base)
    fill(A("IT", 47, 64, 16), 2.0, "SVG")
    for b in range(4):
        iota(A("IT", 224, 256, **blk(b)), [[0, 8], [2 - 4 * (b // 2), 2], [1 - 2 * (b % 2), 2]], b)
    for t in range(3):
        act(A("CX", 4 * t, 4 * t + 4), A("IT", 224, 228), Fn.Identity, bias=32.0 * t, scale=96.0)
    iota(A("PC"), [[0, 1]], 0, 1)
    iota(A("INN"), [[16, 6], [0, 2], [1, 16]])
    if USE_DM:
        iota(A("CI", 0, 8), [[1, 8]])
    iota(A("CI", 8, 12), [[192, 2], [64, 2]], -160)
    iota(A("CI", 16, 30), [[16, 7], [112, 2]])
    iota(A("CI", 30, 54), [[16, 12], [0, 2]], 224)
    for a in range(2):
        iota(A("SQ", 112 * a, 112 * a + 80), [[0, 4], [2, 10], [1 + FAR * (1 - 2 * a), 2]], FAR * a)
        iota(A("SQ", 112 * a + 80, 112 * a + 100), [[12 - 22 * a, 2], [1, 10]], 10 * a)
        fill(A("SQ", 112 * a + 100, 112 * a + 112), 0.0, "SVG")
    iota(A("SQ", 224, 244), [[0, 4], [4, 5]])
    fill(A("SQ", 244, 256), 0.0, "SVG")
    for k in range(2):
        iota(A("SQ", 256 + k, 336, 2), [[1, 5], [10, 2], [0, 4]], 5 - 5 * k)
    iota(A("SQ", 336, 416), [[2, 4], [16, 5], [0, 4]], 1)
    iota(A("HT"), [[0, 10], [1024, 4], [0, 2]])
    iota(A("AB"), [[1024, 4], [16, 20]])
    for k0, k1 in ((0, 2), (2, 3 + USE_DM), (4, 8)):
        tr(A("PT", 32 * k0, 32 * k1), A("IT", 32 * k0, 32 * k1))
    fill(A("L2", 2, 10), 2)
    ts(A("LA"), A("CI", 16, 54), col(0), Op.add)
    for k0, k1 in ((0, 9), (9, 19)):
        cp(A("SD", 32 * k0, 32 * k1), by(A("SQ"), A("LA", 2 * k0, 2 * k1)), "S")
        tr(A("SW", 32 * k0, 32 * k1), A("SD", 32 * k0, 32 * k1))
    turned = lambda k0, k1: A("SW", 32 * k0, 32 * k1, 32)
    tt(pd(0), A("IT", 225, 226), A("IT", 224, 225), Op.subtract)
    act(pd(1), col(4), Fn.Identity, bias=-8.0 * FAR, scale=float(FAR))
    act(pd(2), A("IT", 224, 225), Fn.Identity, bias=8.0 * FAR + ROW, scale=16.0)
    act(pd(3), pd(0), Fn.Identity, bias=pd(2), scale=pd(1))
    act(pd(4), col(7), Fn.Copy, scale=72.0)
    act(pd(6), col(4), Fn.Copy, scale=160.0)
    ts(A("LK", 0, 5), turned(0, 5), 16.0, Op.mult, float(ROW), Op.add)
    ts(A("LE"), turned(5, 7), 16.0, Op.mult, float(ROW), Op.add)
    ts(A("LK", 5, 7), turned(7, 9), 16.0, Op.mult, pd(3), Op.add)
    cp(A("LC", 0, 5), turned(9, 14))
    ts(A("LZ", 0, 5), turned(14, 19), pd(4), Op.add)
    for a in range(2):
        ts(A("LQ", a, 8, 2), A("CX", 0, 4), col(0), Op.add, 16.0 * a, Op.add)
        ts(A("LQ", 8 + a, 20, 2), A("CX", 6, 12), col(0), Op.add, 16.0 * a, Op.add)
    plus(A("HT"), A("HT"), pd(6))
    ts(A("AB"), A("AB"), col(0), Op.add, pd(6), Op.add)
    cp(A("LF"), A("PT", 160, 162))
    cp(A("LO"), A("PT", 192, 194))
    ts(A("LN"), A("IT", 224, 229, 4), 16.0, Op.mult, col(0), Op.add)
    fill(A("CT"), 0.0)
    plus(pd(5), col(4), -192.0)
    ts(A("PD", 8, 11), A("CI", 8, 11), A("PC"), Op.add, col(0), Op.subtract)
    for t in range(3):
        plus(A("CT", t, 512, 128), A("ZT", 0, 4), pd(8 + t))
        plus(A("CT", 4 + t, 512, 128), A("CX", 4 * t, 4 * t + 4), pd(5))
        for k in (8, 12):
            plus(A("CT", k + t, 512, 128), A("ZT", 0, 4), col(0))
    fill(A("CT", 16, 20), 1.0, "SV")
    fill(A("CT", 1, 512, 4, p1=64), 0.0, "SV")
    quant(pair("QC", "SC", 0, 132), A("CT"))
    for u in range(2):
        iota(A("GI", **blk(u, 64)), [[-16, 4]], 0, 1)
        fill(A("HI", **blk(u, 64)), 16.0 * u)
    iota(A("I32"), [[1, 32]])
    iota(A("CI", 54, 86), [[32, 16], [-16, 2]], 16)
    plus(A("HI"), A("HI"), col(0))
    fill(A("EB"), 0.0, "SV")
    for t in range(4):
        ts(A("EB", 129 * t, 128 * t + 128, 4), A("I32"), A("HI"), Op.is_equal)
    ts(A("GJ"), A("GI"), 4, Op.arith_shift_right)
    ts(A("GF"), A("GJ"), 0.0, Op.is_equal)
    for f in range(4):
        cp(A("ET", 512 * f, 512 * f + 512), A("EB"), "SV", scale=A("GF", f, f + 1))
    for k in range(2):
        quant(pair("QE", "SE", 256 * k, 256 * k + 256), A("ET", 1024 * k, 1024 * k + 1024))
    ts(A("LS"), A("CI", 54, 86), col(0), Op.add)
    pick(pair("QE2", "SE2", 0, 512), pair("QE", "SE", 0, 512), A("LS"))
    cp(A("L2", 0, 2), A("PT", 32, 34))
    cp(A("LU", 0, 9), A("PT", 64, 73))
    ts(A("LU", 9, 18), A("PT", 64, 73), 16.0, Op.add)
    if USE_DM:
        ts(A("GK"), A("CI", 0, 8), col(3), Op.add)
        ts(A("GL"), A("GK"), 7, Op.bitwise_and)
        ts(A("LU", 18, 26), A("GL"), 16.0, Op.mult)
    quant(pair("QB", "SB", 288, 416), A("ZT"))
    fill(A("RS"), 0.0, "SVG")
    fill(A("RS", 0, 96, 16), -1e29, "SV")
    fill(A("KP"), 1.0, "SVG")
    fill(A("KP", 0, 96, 16), 0.0, "SVG")
    for name, c0, c1, step in (("FL", 88, 96, 1), ("FL", 184, 192, 1), ("KT", 0, 16, 1), ("KT", 336, 352, 1), ("KG", 0, 16, 1),
                               ("KG", 176, 192, 1), ("F1", 0, 512, 4), ("F1", 513, 768, 4), ("F1", 770, 1280, 4), ("F2", 3, 768, 4),
                               ("CF", 0, 80, 2), ("CTP", 0, 72, 2)):
        fill(A(name, c0, c1, step), 0.0, "SVG")
    for h in range(3 * USE_DT):
        fill(A("VW", 512 * h + C, 512 * h + 512), 0.0, "SVG")
    quant(pair("QU", "SU", 0, 128), A("U"))
    pick(pair("QU2", "SU2", 0, 160), pair("QU", "SU", 0, 128), A("L2"))
    pick(pair("QUP", "SUP", 0, 288), pair("QU", "SU", 0, 128), A("LU", 0, 18))
    if USE_DM:
        pick(pair("QUP", "SUP", 288, 416), pair("QU", "SU", 0, 128), A("LU", 18, 26))
    quant(pair("QV", "SV", 0, 128), A("VV"))
    U2, UF, UA = pair("QU2", "SU2", 32, 160), pair("QU2", "SU2", 0, 128), pair("QUP", "SUP", 288, 416)
    UM = [pair("QUP", "SUP", 144 * (h % 2) + 4 * (h // 2), 128 + 144 * (h % 2) + 4 * (h // 2)) for h in range(8)]
    EF = [pair("QE" + k, "SE" + k, 128 * f, 128 * f + 128) for k in ("", "2") for f in range(4)]
    ts(A("NE", p1=32), A("NI", 64, 128, p1=32), 512.0, Op.mult)
    tt(A("NF", p1=32), A("NE", p1=32), A("NI", 0, 64, p1=32), Op.add)
    cp(A("NF", p0=32, p1=64), A("NF", p1=32), "SV")
    cp(A("NF", p0=64), A("NF", p1=64), "SV")
    cp(A("ND"), by(A("NF"), A("LN")), "SV")
    tr(A("YF"), A("ND"))
    cp(A("T6", 0, 16), by(A("YF"), A("LO", 0, 1)))
    ts(A("T7", 0, 16), A("T6", 0, 16), 511, Op.bitwise_and)
    cp(A("OK"), A("T7", 0, 16))

    for j0, j1 in CUT:
        quant(pair("QX0", "SX0", j0, j1), A("X0", 4 * j0, 4 * j1))
    turn = {"l": 0, "v": 0}

    def scores(q, s, t, k, b):
        mm(bank("PL", b, 0, 128), (pair(q, s, CHUNK[t], CHUNK[t] + 128), UF))
        if k:
            scan(A("PM", 96 + 32 * t, 128 + 32 * t), A("RS", 0, 32), bank("PL", b, 0, 32), 0.0, Op.add, Op.max)
        else:
            cp(A("FT", 32 * t, 32 * t + 32), bank("PL", b, 0, 32), "SV")

    def frames(k, on):
        a, z = 96 * k, 384 * k
        tt(A("FL", a, a + 88), A("PM", a, a + 88), A("PM", a + 8, a + 96), Op.is_lt)
        scan(A("KS", a, a + 96), A("KP"), A("FL", a, a + 96), 0.0, Op.mult, Op.add)
        tr(A("KQ", z, z + 96), A("KS", a, a + 96))
        for b in range(4):
            cp(A("KQ", z + 96, z + 192, **blk(b ^ 1)), A("KQ", z, z + 96, **blk(b)), on[b % 2])
        for u in range(2):
            cp(A("KQ", z + 192, z + 384, **blk(1 - u, 64)), A("KQ", z, z + 192, **blk(u, 64)), on[u])

    def tables(src, n, c0, marks, values, slots=8, first=0, onv=()):
        for h in range(first, slots):
            if values:
                b = turn["v"] % 3
                turn["v"] += 1
                mm(bank("PV", b, 0, max(n, 128)), (EF[h], src))
                cp(A("VW", 512 * h + c0, 512 * h + c0 + n), bank("PV", b, 0, n), "VS" if h in onv else "SV", scale=0.5 if USE_G else None)
            if marks:
                b = (1 + turn["l"] % 4) if n == H else (1, 4)[turn["l"] % 2]
                turn["l"] += 1
                mm(bank("PL", b, 0, max(n, 128)), (UM[h], src))
                cp(A("MT", 512 * h + c0, 512 * h + c0 + n), bank("PL", b, 0, n), "VS" if h in onv else "SV")

    for r, d in enumerate(STEP):
        qx, sx, ql, sl = "QX%d" % r, "SX%d" % r, "QL%d" % r, "SL%d" % r
        X = pair(qx, sx, 0, C)
        dst = T.cores[(rank - d) % N]

        def due(*times, r=r):
            soon[:] = [LEAD + ROUND * r + x for x in times]

        def send(out, in_, sem, view=ap, dst=dst, d=d):
            rid, pid = topo.addr(dst)[:2]
            f = lambda: g.remote_dma(view(out), view(in_), T.sem[sem], T.sem["loc"], pid, rid, lanes(rank, d)[0])
            return add([("G", 350.0, f)], [in_], [], sem="loc", inc=lanes(rank, d)[1], lat=FIXED + 300, free=True,
                       work=128 / lanes(rank, d)[1] * (PER_ROW + 1.3 * PER_BYTE * in_["n"] * in_["w"]))

        def landed(sem, writes, sent):
            add([("R", 0.0, None)], [], writes, sem=sem, inc=len(sent) * lanes((rank + d) % N, d)[1],
                lat=2000.0 if sem == "col0" else 300.0, after=sent)
        due(-1200, 100)
        sent = [send(A(ql, j0, j1), A(qx, j0, j1), "col%d" % r, u8) for j0, j1 in (CUT if r else ((0, C),))]
        landed("col%d" % r, [A(ql), A(sl)], sent + [send(A(sl), A(sx), "col%d" % r)])
        XA, XB = pair(qx, sx, 0, 192), pair(qx, sx, 192, C)
        sc = lambda t: A("FT", 32 * t + 15, 32 * t + 16)
        due(-1200)
        for t in (0, 1):
            scores(qx, sx, t, 0, 2 + t)
        mm(bank("PL", 1, 0, 192), (U2, XA))
        mm(bank("PL", 0, 0, 192), (U2, XA))
        act(A("DD", 0, 128), bank("PL", 1, 0, 128), Fn.Identity, bias=sc(0), scale=-1.0)
        act(A("DD", 128, 192), bank("PL", 1, 128, 192), Fn.Identity, bias=sc(1), scale=-1.0)
        due(0)
        ts(A("F1", 512, 768, 4), bank("PL", 0, 128, 192), sc(0), Op.is_le)
        ts(A("F1", 1, 512, 4), bank("PL", 0, 0, 128), sc(1), Op.is_lt)
        tt(A("F1", 3, 768, 4), A("DD", 0, 192), A("MK", 0, 192), Op.is_ge)
        scores(qx, sx, 2, 0, 4)
        mm(bank("PL", 2, 0, 128), (U2, XB))
        mm(bank("PL", 3, 0, 128), (U2, XB))
        act(A("DD", 192, C), bank("PL", 3, 0, 128), Fn.Identity, bias=sc(2), scale=-1.0)
        due(900, 1100, 780, 1650, 1420, 2140, 1820, 2305, 1980, 2470, 2470, 2870, 3200, 3600, 4215, 4640)
        for t in (0, 1):
            ts(A("F1", 768 + t, 1280, 4), bank("PL", 2, 0, 128), sc(t), Op.is_le)
        ts(A("F1", 2, 768, 4), bank("PL", 0, 0, 192), sc(2), Op.is_lt)
        tt(A("F1", 771, 1280, 4), A("DD", 192, C), A("MK", 192, C), Op.is_ge)
        for j0, j1 in CUT:
            quant(pair("QF1", "SF1", j0, j1), A("F1", 4 * j0, 4 * j1))
        for t in range(3):
            mm(bank("PL", 2 + t, 0, 128), (pair("QF1", "SF1", CHUNK[t], CHUNK[t] + 128), pair("QC", "SC", 4, 132)))
            ts(A("F2", t, 768, 4), A("INN"), bank("PL", 2 + t, 0, 1), Op.is_equal)
        quant(pair("QF2", "SF2", 0, 192), A("F2"))
        f2 = pair("QF2", "SF2", 0, 192)
        mm(bank("PL", 0, 0, 192), (pair("QC", "SC", 0, 128), f2), (pair("QC", "SC", 2, 130), f2))
        tr(A("OT"), bank("PL", 0, 0, 192))
        ol, ll = "OL%d" % r, "LL%d" % r
        ts(A(ol, 0, 6), A("OT", 0, 192, 32), 160.0, Op.add)
        ts(A(ol, 6, 12), A("OT", 1, 192, 32), 192.0, Op.add)
        landed("arr%d" % r, [A(ll)], [send(A(ll), A(ol), "arr%d" % r)])
        if r and USE_DM:
            due(2700)
            mm(bank("PL", 1, 0, C), (UA, X))
            cp(A("MS"), bank("PL", 1, 0, C), "SV")
        else:
            due(*[4400 + 250 * k for k in range(16)])
            tables(X, C, 0, True, None)
        due(1975, 2630, 3035, 3430, 3710, 3710, 3830, 3900, 4050, 4050, 4400)
        scan(A("PM", 0, 96), A("RS"), A("FT"), 0.0, Op.add, Op.max)
        frames(0, ("VS", "SV"))
        cp(A("KT", 16, 16 + C), by(A("KQ", 0, 384), A("LQ")), "SV")
        due(-500, -300, -450, -50, 600, 900, 650, 1150, 1200, 1400, 1250, 1600, 1300, 1800, 1350, 2000, 2300)
        tables(XA, 192, 0, None, True, 4)
        tables(XB, 128, 192, None, True, 4)
        if USE_DT:
            dma("Y", "dt", [(T.VW[16 * k:16 * k + 16, 2048:3904], T.VW[16 * (k ^ 1):16 * (k ^ 1) + 16, 0:1856]) for k in range(8)],
                [A("VW", 0, 1856)], [A("VW", 2048, 3904)], 128, 3712)
        else:
            due(2750, 2800, 2760, 3200, 4100, 5100, 4150, 5500)
            tables(X, C, 0, None, True, 8, 4)
        due(4950, 5200, 5600, 6350, 6750, 7000)
        tr(A("KXA", 0, C), A("KT", 16, 16 + C))
        tr(A("KXA", C, C + 352), A("KT", 0, 352))
        cp(A("KA"), by(A("KXA"), A("LK", 0, 7)), "SV", scale=512.0)
        tt(A("T4"), A("AB"), A("KA", 0, 80), Op.add)
        ts(A("T5"), A("T4"), 4095, Op.bitwise_and)
        cp(A("OA"), A("T5"))
        for q in range(4):
            due((7200, 7780, 11300, 11900)[q])
            cp(A("AP", C * q, C * q + C), by(A("VW"), A("OA", 20 * q, 20 * q + 20)), "SV")
            a2 = "A2" if USE_G else "AP"
            if USE_G:
                cp(A("A2", C * q, C * q + C), A("AP", C * q, C * q + C), "SV", scale=2.0)
            due(11000 + 400 * q)
            dma("Y", "da%d" % q, [(T.AS[32 * q:32 * q + 32, C * t:C * t + C], T[a2][32 * t:32 * t + 32, C * q:C * q + C])
                                  for t in range(4)], [A(a2, C * q, C * q + C)], [A("AS", **blk(q))], 128, 640)
        due(6100, 6500, 6800)
        tt(A("PF"), A("YF"), A("KA", 80, 112), Op.subtract)
        cp(A("PH", 0, 16), by(A("PF"), A("LF", 0, 1)), "SV")
        plus(A("PH", 16, 32), A("PH", 0, 16), 512.0)
        due(5565, 5900, 5570, 6050, 5575, 6200, 6460, 6870, 7150, 7430)
        for t in range(3):
            scores(ql, sl, t, 1, (2, 3, 0)[t])
        frames(1, ("VS", "VS"))
        if r and USE_DM:
            dma("Y", "dm", [(T.MT[64 * k:64 * k + 64:4, 512 * h:512 * h + C], T.MS[16 * h:16 * h + 16, :]) for h in range(8) for k in range(2)],
                [A("MS"), A("KXA", 0, C)], [A("MT", 512 * h, 512 * h + C) for h in range(8)], 256, 1280)
        due(8665, 8870, 8665)
        cp(A("KT", 16 + C, 16 + E), by(A("KQ", 384, 768), A(ll, 6, 12)), "VS")
        at = H * (2 - r)
        pick(pair("QB", "SB", at, at + H), pair(ql, sl, 0, C), A(ll, 0, 6))
        due(*[9250 + 80 * k + 250 * (k % 2) for k in range(16)])
        tables(pair("QB", "SB", at, at + 128), H, C, True, None, onv=(2, 4, 6))
        due(*[11900 + 90 * k + 250 * (k % 2) for k in range(16)])
        tables(pair("QB", "SB", at, at + 128), H, C, None, True, onv=(5, 7))
        due(9040, 9040, 9415, 9725, 9810, 10065, 10315, 9560, 9900, 10400, 10500, 11100, 11750, 11800)
        cp(A("KG", 16, 112), by(A("KT", 16, 16 + E), A("OK", 0, 6)), "V", scale=512.0)
        cp(A("KG", 112, 176), by(A("KT", 16, 16 + E), A("OK", 6, 10)), "SV", scale=512.0)
        tr(A("KX", 0, 160), A("KG", 16, 176))
        for h in range(2):
            tt(A("T2", h, 20, 2), A("PH", 16 * h, 16 * h + 10), A("KX", ROW, 160, 16), Op.add)
        ts(A("T3"), A("T2"), 4095, Op.bitwise_and)
        cp(A("OM"), A("T3"))
        tr(A("KX", 160, 352), A("KG"))
        cp(A("KF"), by(A("KX"), A("LE")), "SV")
        tt(A("YF"), A("PF"), A("KF"), Op.add)
        tt(A("G1"), by(A("YF"), A("LC", 0, 5)), A("HT"), Op.add)
        ts(A("G2"), A("G1"), 4095, Op.bitwise_and)
        tt(A("CB", 0, 80, 2), A("G2", 0, 80, 2), A("G2", 1, 80, 2), Op.subtract)
        cp(A("CB", 1, 80, 2), A("G2", 1, 80, 2))
        due(10765, 11265, 10765, 11490, 11885, 12030, 12200, 12350, 12515, 12820, 13125, 13125, 13260, 13280, 13565, 13565, 13965)
        for q in range(2):
            cp(A("MG", 160 * q, 160 * q + 160), by(A("MT"), A("OM", 10 * q, 10 * q + 10)), ("VS", "SV")[q])
            tr(A("MX", 160 * q, 160 * q + 160), A("MG", 160 * q, 160 * q + 160))
        tt(A("CF", 1, 80, 2), A("MX", 160, 320, 4), A("MX", 0, 160, 4), Op.is_gt)
        tt(A("CM"), A("MX", 160, 320, 4), A("MX", 0, 160, 4), Op.max)
        scan(A("C1"), A("CF"), A("CB"), 0.0, Op.mult, Op.add)
        tt(A("CTP", 1, 72, 2), A("CM", 4, 40), A("CM", 0, 36), Op.is_gt)
        tt(A("C1", 0, 72, 2), A("C1", 9, 80, 2), A("C1", 1, 72, 2), Op.subtract)
        scan(A("CZ", 0, 72), A("CTP"), A("C1", 0, 72), 0.0, Op.mult, Op.add)
        for b in range(4):
            cp(A("CZ", 72, 144, **blk(b ^ 1)), A("CZ", 0, 72, **blk(b)), ("VS", "SV")[b % 2])
        for u in range(2):
            cp(A("CZ", 144, 288, **blk(1 - u, 64)), A("CZ", 0, 144, **blk(u, 64)), ("VS", "SV")[u])
        cp(A("OB"), by(A("CZ"), A("LZ", 0, 5)))
        for q, (j0, j1), at, mine, then in ((0, (0, C), 14315, 0, 0), (1, (0, C), 14870, 2, 16400), (2, CUT[0], 15430, 2, 16900),
                                            (3, CUT[0], 15790, 3, 17200), (2, CUT[1], 16150, 0, 0), (3, CUT[1], 17700, 4, 18200)):
            due(at)
            tt(A("ZP", C * q + j0, C * q + j1), by(A("VW"), A("OB", 20 * q + j0 // 16, 20 * q + j1 // 16)),
               A("AP", C * q + j0, C * q + j1), Op.add)
            for t in range(4):
                due(then if t < mine else at + 700 + 2000 * (j0 > 0))
                cp(A("Z", 4 * j0 + t, 4 * j1, 4, **blk(q)), A("ZP", C * q + j0, C * q + j1, **blk(t)),
                   ("VS" if t < mine else "SV") + "G" * USE_G, scale=None if USE_G else 0.5)
        for k, (j0, j1) in enumerate(CUT):
            QZ = pair("QZ", "SZ", j0, j1)
            due(18000 + 900 * k)
            quant(QZ, A("Z", 4 * j0, 4 * j1))
            for t in range(4):
                b = turn["v"] % 3
                turn["v"] += 1
                due(18400 + 1000 * k + 230 * t, 18800 + 1100 * k + 280 * t, 19300 + 2100 * k + 450 * t)
                mm(bank("PV", b, 0, j1 - j0), (pair("WC", "WS", 128 * t, 128 * t + 128), QZ))
                act(A("RL", C * t + j0, C * t + j1), bank("PV", b, 0, j1 - j0), Fn.Relu, scale=0.03125)
                tt(A("X1", 4 * j0 + t, 4 * j1, 4), A("RL", C * t + j0, C * t + j1), A("AS", C * t + j0, C * t + j1), Op.add)
            due(21600 + 1250 * k)
            quant(pair("QX%d" % (r + 1), "SX%d" % (r + 1), j0, j1), A("X1", 4 * j0, 4 * j1))

    soon[:] = [LEAD + len(STEP) * ROUND]
    cp(A("T6"), A("YF"))
    ts(A("T7"), A("T6"), 9, Op.arith_shift_right, 7, Op.bitwise_and)
    cp(A("SF"), A("T7"))
    tr(A("ST"), A("SF"))
    for b in range(4):
        cp(A("SG", 16 * b, 16 * b + 16, p1=32), A("ST", 0, 16, **blk(b)), "SV")
    dma("Y", "do0", [(T.oe[:], T.SG[0:20, :])], [A("SG", p1=32)], [], 20, 256)
    for k, (j0, j1) in enumerate(CUT):
        b = turn["v"] % 3
        turn["v"] += 1
        mm(bank("PV", b, 0, j1 - j0), (pair("QV", "SV", 0, 128), pair("QX3", "SX3", j0, j1)))
        cp(A("YO", j0, j1), bank("PV", b, 0, j1 - j0), "SV")
        dma("Y", "dc%d" % k, [(T.oc[:, 4 * j0:4 * j1], u8(A("QX3", j0, j1)))], [A("QX3", j0, j1)], [], 128, 4 * (j1 - j0))
        dma("SY"[k], "dy%d" % k, [(T.y[:, j0:j1], T.YO[:, j0:j1])], [A("YO", j0, j1)], [], 128, 4 * (j1 - j0))
    dma("S", "do2", [(T.osc[4 * k:4 * k + 4, :], T.SX3[32 * k:32 * k + 4, :]) for k in range(4)], [A("SX3")], [], 16, 320)

    emit(g, T, Q, ops)


PLAN = {}


def plan(ops, deps, soft):
    n = len(ops)
    users = [[] for _ in range(n)]
    level = [0.0] * n
    for i in range(n - 1, -1, -1):
        level[i] += min(a[1] for a in ops[i]["alts"]) + ops[i]["lat"] + ops[i]["work"] + SYNC
        for j in deps[i]:
            level[j] = max(level[j], level[i])
            users[j].append(i)
    que = [["VSPGYR".index(a[0]) for a in o["alts"]] for o in ops]
    cost = [[a[1] for a in o["alts"]] for o in ops]
    lat, work = [o["lat"] for o in ops], [o["work"] for o in ops]
    hard = [[j for j in deps[i] if j not in soft[i]] for i in range(n)]
    easy = [sorted(soft[i]) for i in range(n)]
    eng = [0] * n
    start, end, why = [0.0] * n, [0.0] * n, [-1] * n
    seed = [12345]

    def draw(k):
        seed[0] = (seed[0] * 6364136223846793005 + 1442695040888963407) % 2 ** 64
        return (seed[0] >> 33) % k

    def run(order, first):
        free, last, seen = [0.0] * 7, [-1] * 7, 0
        k = first - 1
        while k >= 0 and seen < 6:
            i = order[k]
            q = que[i][eng[i]]
            if last[q] < 0 and q < 5:
                last[q], free[q] = i, start[i] + cost[i][eng[i]]
                seen += 1
            if last[6] < 0 and work[i]:
                last[6], free[6] = i, end[i] - lat[i] / 2
                seen += 1
            k -= 1
        for i in order[first:]:
            e = eng[i]
            q = que[i][e]
            s, w = free[q], last[q]
            for j in hard[i]:
                t = end[j] + SYNC
                if t > s:
                    s, w = t, j
            for j in easy[i]:
                t = end[j] + (0.0 if que[j][eng[j]] == q else SYNC)
                if t > s:
                    s, w = t, j
            start[i], why[i] = s, w
            s += cost[i][e]
            free[q], last[q] = s, i
            if work[i]:
                s += lat[i] / 2
                if free[6] > s:
                    s, why[i] = free[6], last[6]
                s += work[i]
                free[6], last[6] = s, i
                end[i] = s + lat[i] / 2
            else:
                end[i] = s + lat[i]
        return max(end)

    def pack(order):
        rows, begin, done, lanes = [[] for _ in range(6)], [0.0] * n, [0.0] * n, 0.0
        for i in order:
            got = None
            for e, q in enumerate(que[i]):
                s = max([0.0] + [done[j] + SYNC for j in hard[i]] + [done[j] + (0.0 if que[j][eng[j]] == q else SYNC) for j in easy[i]])
                row, at = rows[q], len(rows[q])
                while at and row[at - 1][1] > s:
                    at -= 1
                while at < len(row) and s + cost[i][e] > row[at][0]:
                    s = max(s, row[at][1])
                    at += 1
                key = (s + cost[i][e] > start[i] + cost[i][eng[i]] + 1e-6, q == 0, s + cost[i][e])
                if got is None or key < got[0]:
                    got = (key, e, s, at)
            key, eng[i], begin[i], at = got
            s = begin[i] + cost[i][eng[i]]
            rows[que[i][eng[i]]].insert(at, (begin[i], s))
            if work[i]:
                lanes = max(s + lat[i] / 2, lanes) + work[i]
                done[i] = lanes + lat[i] / 2
            else:
                done[i] = s + lat[i]
        order.sort(key=lambda k: begin[k])

    def lay(due, lean):
        rows, begin, done, lanes = [[] for _ in range(6)], [0.0] * n, [0.0] * n, []
        left = [len(d) for d in deps]
        ready = [i for i in range(n) if not left[i]]
        while ready:
            i = min(ready, key=lambda k: due[k])
            ready.remove(i)
            got = None
            for e, q in enumerate(que[i]):
                s = max([0.0] + [done[j] + SYNC for j in hard[i]] + [done[j] + (0.0 if que[j][eng[j]] == q else SYNC) for j in easy[i]])
                row, at = rows[q], len(rows[q])
                while at and row[at - 1][1] > s:
                    at -= 1
                while at < len(row) and s + cost[i][e] > row[at][0]:
                    s = max(s, row[at][1])
                    at += 1
                key = s + cost[i][e] + ((lean[i] if q == 0 else 0.0) if ops[i]["due"] is None else 1e6 * e)
                if got is None or key < got[0]:
                    got = (key, e, s, at)
            key, eng[i], begin[i], at = got
            s = begin[i] + cost[i][eng[i]]
            rows[que[i][eng[i]]].insert(at, (begin[i], s))
            if work[i]:
                s += lat[i] / 2
                for x, y in lanes:
                    if s < y and s + work[i] > x:
                        s = y
                lanes.append((s, s + work[i]))
                lanes.sort()
                done[i] = s + work[i] + lat[i] / 2
            else:
                done[i] = s + lat[i]
            for u in users[i]:
                left[u] -= 1
                if not left[u]:
                    ready.append(u)
        order = sorted(range(n), key=lambda k: (begin[k], k))
        return run(order, 0), order

    base = [o["due"] for o in ops]
    for i in range(n - 1, -1, -1):
        if base[i] is None:
            base[i] = min([base[u] for u in users[i]] + [1e9]) - min(cost[i]) - lat[i] - work[i] - SYNC
        else:
            base[i] += 1e-3 * i
    tilt, got = [500.0] * n, None
    for trial in range(FIRST):
        due, lean = list(base), list(tilt)
        for k in range(draw(4) + 1 if trial else 0):
            i, kind = draw(n), draw(3)
            if kind == 0:
                lean[i] = draw(1200) - 400.0
            else:
                push = (draw(41) - 20) * 150.0
                for j in range(i, min(n, i + 1 + (draw(16) if kind == 1 else 0))):
                    due[j] -= push
        new, order = lay(due, lean)
        if got is None or new <= got[0]:
            got, base, tilt = (new, order, list(eng)), due, lean
    order, eng[:] = got[1], got[2]
    span = run(order, 0)
    best = (span, list(order), list(eng))
    for trial in range(TRIES):
        if trial % 64 == 0:
            order.sort(key=lambda k: start[k])
            span = run(order, 0)
            if trial % 256 == 0:
                old, was = list(order), list(eng)
                pack(order)
                if run(order, 0) > span + 50:
                    order[:], eng[:] = old, was
                span = run(order, 0)
            if span < best[0]:
                best = (span, list(order), list(eng))
        path, i = [], end.index(max(end))
        while i >= 0:
            if why[i] >= 0 and why[i] not in deps[i]:
                path.append(i)
            i = why[i]
        v = path[draw(len(path))]
        u, kind = why[v], draw(8)
        old, keep = list(order), (list(start), list(end), list(why))
        pu, pv = order.index(u), order.index(v)
        changed = None
        if kind < 2:
            x = (u, v)[kind]
            if len(que[x]) < 2:
                continue
            changed = (x, eng[x])
            eng[x] = (eng[x] + 1 + draw(len(que[x]) - 1)) % len(que[x])
            first = pu
        elif kind < 5:
            first = max(0, pu - (draw(12) if kind == 4 else 0))
            need, move = set(deps[v]), [v]
            for i in order[pv - 1:first - 1 if first else None:-1]:
                if i in need:
                    move.append(i)
                    need.update(deps[i])
            if u in move:
                continue
            ms = set(move)
            order[first:pv + 1] = move[::-1] + [i for i in order[first:pv + 1] if i not in ms]
        else:
            first, stop = pu, min(n, pv + 1 + (draw(30) if kind == 7 else 0))
            move, ms = [u], {u}
            for i in order[pu + 1:stop]:
                if any(j in ms for j in deps[i]):
                    move.append(i)
                    ms.add(i)
            if v in ms:
                continue
            order[pu:stop] = [i for i in order[pu:stop] if i not in ms] + move
        new = run(order, first)
        if new <= span + HEAT * (1.0 - trial / TRIES) * (draw(1000) / 500.0) ** 2:
            span = new
        else:
            order[:] = old
            start[:], end[:], why[:] = keep
            if changed:
                eng[changed[0]] = changed[1]
    eng[:] = best[2]
    return run(best[1], 0), best[1], start, end, eng


def emit(g, T, Q, ops):
    n = len(ops)
    deps = [set(o["after"]) for o in ops]
    hard = [set(o["after"]) for o in ops]
    seen = {}
    for i, o in enumerate(ops):
        for regs, w in ((o["r"], False), (o["w"], True)):
            for name, pm, cm in regs:
                ps = name in ("PL", "PV")
                for j, pj, cj, wj in seen.get(name, ()):
                    if j != i and (w or wj or ps) and pm & pj and cm & cj:
                        deps[i].add(j)
                        if w or wj:
                            hard[i].add(j)
        for regs, w in ((o["r"], False), (o["w"], True)):
            for name, pm, cm in regs:
                old = seen.get(name, [])
                if w:
                    old = [e for e in old if (e[1] & ~pm) or (e[2] & ~cm)]
                seen[name] = old + [(i, pm, cm, w)]
    lastsem = {}
    for i, o in enumerate(ops):
        if o["sem"] is not None and not o["free"]:
            if o["sem"] in lastsem:
                deps[i].add(lastsem[o["sem"]])
                hard[i].add(lastsem[o["sem"]])
            lastsem[o["sem"]] = i
    soft = [deps[i] - hard[i] for i in range(n)]
    if n not in PLAN:
        PLAN[n] = plan(ops, [sorted(d) for d in deps], soft)
    span, order, start, end, eng = PLAN[n]
    count, known, mark, alone = {}, {q: {} for q in Q}, [None] * n, False
    for i in order:
        o = ops[i]
        q = o["alts"][eng[i]][0]
        sem = o["sem"] or "e" + q
        count[sem] = count.get(sem, 0) + o["inc"]
        if q == "R":
            mark[i] = (sem, count[sem], {})
            continue
        for j in sorted(deps[i], key=lambda k: (-end[k], k)):
            if j in soft[i] and ops[j]["alts"][eng[j]][0] == q:
                continue
            s, v, clock = mark[j]
            if known[q].get(s, 0) < v:
                Q[q].wait_ge(T.sem[s], v)
                known[q][s] = v
                for s2, v2 in clock.items():
                    known[q][s2] = max(known[q].get(s2, 0), v2)
        if sem == "eG":
            if (o["alone"] or alone) and known[q].get(sem, 0) < count[sem] - 1:
                g.wait_ge(T.sem[sem], count[sem] - 1)
                known[q][sem] = count[sem] - 1
            alone = o["alone"]
        ins = o["alts"][eng[i]][2]()
        if o["sem"] is None:
            ins.then_inc(T.sem[sem], 1)
        mark[i] = (sem, count[sem], dict(known[q]))
    for s, v in count.items():
        g.wait_ge(T.sem[s], v)
